import numpy as np, ml_dtypes
CORES = [5,29,101,125,133,157,229,253]
N = 8
BF = ml_dtypes.bfloat16
def f(rng, *shape):
    return (rng.standard_normal(shape, dtype=np.float32) * np.exp2(rng.integers(-2, 3, shape[:-1] + (1,)))).astype(BF)
def wide(rng, *shape):
    v = f(rng, *shape).astype(np.float32); k = shape[:-2] + (1, shape[-1])
    return (v * np.exp2(rng.integers(-6, 7, k)) * (rng.random(k) > 0.0625)).astype(BF)
W, L, T, C, TH, SH = 4096, 128, 4, 6, 11, 12
def at(tab, a):
    return np.take_along_axis(tab, a.reshape(tab.shape[:-1] + (-1,)), -1).reshape(a.shape)
def tax(rng, key):
    term = np.argsort(key, axis=-1); gap = W - 1 - np.argsort(term, axis=-1)
    def up(lo, hi):
        v = np.where(rng.random((N, 8, W)) < 0.75, rng.random((1, 8, W)), rng.random((N, 8, W)))
        return np.take_along_axis(np.broadcast_to(term, (N, 8, W)), W - 1 - (gap * (lo + (hi - lo) * v)).astype(np.int64), 2)
    return term, gap, up(0.3, 0.7), up(0.05, 0.4)
def heights(rng, gap):
    h = (1.5 * (SH - np.log2(gap + 1.0))).astype(np.float32)[None, :, None, :]
    e = (h + rng.standard_normal((N, 8, 16, W), dtype=np.float32)) * np.exp2(rng.integers(-2, 3, (N, 8, 16, 1))).astype(np.float32)
    return e.reshape(N, 128, W).astype(BF)
def low(rng, term, n, top):
    return np.take_along_axis(np.broadcast_to(term, (N, 8, W)), rng.integers(0, top, (N, 8, n)), 2)
def lanes(rng, term, p0, p1):
    s = low(rng, term, 16 * L, W // 2).reshape(N, 8, 16, L)
    z = np.where(rng.random((N, 8, 16 * T * L)) < 0.1, low(rng, term, 16 * T * L, W), low(rng, term, 16 * T * L, W // 2)).reshape(N, 8, 16, T, L)
    kind = rng.integers(0, 8, (N, 8, 1, L))
    d = np.where(kind < 4, rng.integers(2, C + 1, s.shape), rng.integers(1, C + 1, s.shape)); d = np.where((kind < 3) & (rng.random(s.shape) < 0.1), 1, d)
    a = s
    for i in range(C):
        nx = at(p0, a)
        if i == 0: nx = np.where(rng.random(s.shape) < 0.4, at(p1, a), nx)
        a = np.where(d > i, nx, a)
    g = np.where(kind == 7, low(rng, term, 16 * L, W).reshape(s.shape), a)
    return s, g, z, (rng.random((N, 8, T, L)) < 0.4).astype(np.int64)
def pack(e, pa, s, g, z, sg):
    i4 = lambda v, *sh: np.ascontiguousarray(np.reshape(v, (N,) + sh)).astype(np.int32)
    return {"ev": np.reshape(e, (N, 128, W)).astype(BF), "par": i4(pa, 8, W), "s0": i4(s, 128, L), "g0": i4(g, 128, L), "z": i4(z, 128, T * L), "sg": i4(sg, 8, T * L)}
def setup_inputs(rng):
    term, gap, p0, p1 = tax(rng, rng.random((8, W)))
    return pack(heights(rng, gap), p0 + W * p1, *lanes(rng, term, p0, p1))
def setup_inputs_corners(rng):
    term, gap, p0, p1 = tax(rng, rng.random((8, W))); own = np.arange(W); c = rng.integers(0, 7, (1, 8, W))
    p0 = np.where(c == 0, own, np.where((c == 1) | (c == 4), W - 1, np.where((c == 2) | (c == 3), 0, p0)))
    p1 = np.where((c == 0) | (c == 3), own, np.where(c == 1, W - 1, np.where((c == 2) | (c == 4), 0, p1)))
    b = np.where(np.arange(N)[:, None, None] == 0, own, W - 1); p0 = np.where(c == 6, b, p0); p1 = np.where(c == 6, b, p1)
    for p in (p0, p1): p[:, ::2, W - 1] = W - 1; p[:, 1::2, W - 1] = 0
    e = heights(rng, gap).astype(np.float32); e[:, :, 0] = -256.0; e[:, :, W - 1] = 256.0
    s, g, z, sg = lanes(rng, term, p0, p1); one = (N, 8, 1, L)
    n = rng.choice(np.array([0, 0, 1, 4, 5, 16]), one); k = np.argsort(rng.random(s.shape), axis=2)
    g = np.where(rng.random(one) < 0.8, np.where(k < n, 0, W - 1), g)
    same = rng.random(one) < 0.2; s = np.where(same, s[:, :, :1], s); z = np.where(same[:, :, :, None], z[:, :, :1], z)
    g = np.where(rng.random(one) < 0.08, s, g); m = rng.integers(0, 8, (N, 8, 1, T, L))
    z = np.where(m == 0, s[:, :, :, None], np.where((m == 1) & (rng.random(z.shape) < 0.5), W - 1, np.where((m == 2) & (rng.random(z.shape) < 0.3), 0, z)))
    sg[0, :, 0] = 0; sg[1, :, 0] = 1; sg[2, :, 0] = 1; g[0] = W - 1
    for h in range(8):
        o = np.nonzero(c[0, h, 1:W - 1] == 0)[0] + 1; v = np.nonzero(c[0, h, 1:W - 1] == 6)[0] + 1
        s[0, h] = np.where(rng.random((1, L)) < 0.4, rng.choice(o, (16, L)), rng.choice(v, (16, L)))
        a, u = rng.permutation(v)[:2]; w = e[:, 16 * h:16 * h + 16]
        w[1:, :, a] = w[1:, :, u]; w[1, rng.permutation(16)[TH:], a] = -256.0
        j = np.append(rng.permutation(L - 1)[:L // 8], L - 1); i = rng.integers(0, 16, j.size)
        s[0, h, :, j] = rng.choice(o, (j.size, 16)); s[0, h, i, j] = a; z[0, h, i, 0, j] = u
    s[2, 7, :, L - 1] = rng.choice(o, 16); g[2, 7, :, L - 1] = W - 1; sg[2, 7, 0, L - 1] = 0
    for h in range(8):
        o = np.nonzero(c[0, h, 1:W - 1] == 0)[0] + 1; j = L if h < 7 else 1
        s[N - 1, h, :, :j] = rng.choice(o, (16, j)); g[N - 1, h, :, :j] = W - 1; sg[N - 1, h, 0] = 1; sg[N - 1, h, 0, :j] = 0
    return pack(e, p0 + W * p1, s, g, z, sg)
def setup_inputs_ends(rng):
    term, gap, p0, p1 = tax(rng, rng.random((8, W))); e = heights(rng, gap).astype(np.float32).reshape(N, 8, 16, W)
    cnt = rng.choice(np.array([0, 16, 8, 7, TH, TH - 1]), (N, 8, 1)); cnt[:, 0] = 16; cnt[:, 7] = 0
    v = np.where(np.argsort(rng.random((N, 8, 16)), axis=2) < cnt, 32.0, -32.0); v[:, 3] = 0.0
    e[..., 0] = v; e[..., W - 1] = -v
    pa = np.where(rng.random((N, 8, W)) < 0.85, (W * W - 1) * rng.integers(0, 2, (N, 8, W)), p0 + W * p1)
    kind = rng.integers(0, 5, (N, 8)); kind[:, 0] = 0; kind[:, 7] = 0; kind[N - 1] = 2
    pa[:, :, 0] = np.array([W * W - 1, 0, W * W - 1, 0, W - 1])[kind]; pa[:, :, W - 1] = np.array([0, W * W - 1, W * W - 1, 0, W * (W - 1)])[kind]
    def ends(*t):
        sh = (N, 8, 16) + t + (L,); one = (N, 8, 1) + t + (L,)
        x = np.where(rng.random(one) < 0.5, (W - 1) * rng.integers(0, 2, one), (W - 1) * rng.integers(0, 2, sh))
        return np.where((rng.random(one) < 0.25) & (rng.random(sh) < 0.5), rng.integers(0, W, sh), x)
    s = ends(); g = ends(); z = ends(T); sg = rng.integers(0, 2, (N, 8, T, L))
    x = (W - 1) * rng.integers(0, 2, (8, 16, L)); s[N - 1] = x; g[N - 1] = x; z[N - 1, :, :, 0] = x; sg[N - 1, :, 0] = 0; sg[1, :, 0] = 1
    s[:N - 1, 7, :, L - 3:] = 0; g[:N - 1, 7, :, L - 2:] = W - 1; g[:N - 1, 7, :, L - 3] = 0
    z[:N - 1, 7, :, 0, L - 3:] = W - 1; z[:N - 1, 7, :15, 0, L - 1] = 0; sg[:N - 1, 7, 0, L - 3:] = np.array([1, 0, 0])
    return pack(e, pa, s, g, z, sg)
def setup_inputs_spread(rng):
    c = rng.integers(-6, 7, (8, W)); term, gap, p0, p1 = tax(rng, c + rng.random((8, W)))
    w = np.abs(wide(rng, N, 128, W).astype(np.float32)).reshape(N, 8, 16, W) * np.exp2(2.0 * c).astype(np.float32)[None, :, None, :]
    w = np.where(rng.random((N, 8, 16, 1)) < 0.06, -w, w)
    return pack(w, p0 + W * p1, *lanes(rng, term, p0, p1))
def setup_inputs_ties(rng):
    term, gap, p0, p1 = tax(rng, rng.random((8, W))); q = W // 8; top = gap < q
    x = rng.integers(0, 4, (N, 8, 16, W)); x = np.where(top[None, :, None, :] & (rng.random(x.shape) < 0.75), 3, x)
    x[:, 5] = x[:, 5] // 2; x[:, 2] = 1
    u = np.take_along_axis(term[:, W - q:], rng.integers(0, q, (8, W)), 1)[None]
    p0 = np.where(rng.random((N, 8, W)) < 0.9, u, p0); p1 = np.where(rng.random((1, 8, W)) < 0.6, p0, p1)
    s, g, z, sg = lanes(rng, term, p0, p1); g = np.where(rng.random((N, 8, 1, L)) < 0.7, at(p0, s), g)
    return pack(x.astype(np.float32), p0 + W * p1, s, g, z, sg)
def check_inputs(d):
    bad = []
    for k, hi in (("par", W * W - 1), ("s0", W - 1), ("g0", W - 1), ("z", W - 1), ("sg", 1)):
        if np.min(d[k]) < 0 or np.max(d[k]) > hi: bad.append("range of " + k)
    e = d["ev"].astype(np.float32)
    if not np.all(np.isfinite(e)): bad.append("ev is not finite")
    if np.any((e != 0) & (np.abs(e) < np.float32(2.0 ** -126))): bad.append("ev holds subnormal numbers")
    return bad
def wits(tab, a):
    return np.take_along_axis(tab, a.reshape(8, 1, -1), 2).reshape(8, 16, 16, L)
def reference(ev, par, s0, g0, z, sg):
    e = ev.astype(np.float32).reshape(N, 8, 16, W); pa = par.astype(np.int64); p0 = pa & (W - 1); p1 = pa >> SH
    zs = z.astype(np.int64).reshape(N, 8, 16, T, L); plus = sg.reshape(N, 8, T, L) == 1
    S = s0.astype(np.int64).reshape(N, 8, 16, L); G = g0.astype(np.int64).reshape(N, 8, 16, L)
    ride = np.zeros((N, 8, L), bool); rz = np.zeros((N, 8, 16, L), np.int64)
    for t in range(T):
        for r in range(N):
            q = (r + t) % N; th = TH + (int(np.sum(ride[r])) & 1)
            x = np.where(ride[r][:, None], rz[r], zs[q, :, :, t]); pos = (plus[q, :, t] & ~ride[r])[:, None]
            ex = wits(e[q], x); g = G[r]; a = S[r]
            miss = np.sum(np.sum(wits(e[q], g) >= ex, axis=1) < th, axis=1)[:, None]
            for i in range(C):
                cov = np.sum(wits(e[q], a) >= ex, axis=1)
                nx = np.where(cov >= 8, at(p0[q], a), at(p1[q], a))
                stop = np.where(pos, cov >= th, nx == g)
                a = np.where(stop, a, nx)
            full = ~pos & (miss == 0); can = full & stop & (cov < th)
            win = np.argmin(np.where(can, cov, 99), axis=1)
            hit = can & (np.arange(16)[None, :, None] == win[:, None])
            S[r] = np.where(pos, a, S[r]); G[r] = np.where((pos & (miss > 4)) | hit, a, g)
            ride[r] = full[:, 0] & ~np.any(can, axis=1); rz[r] = x
    return {"ys": S.reshape(N, 128, L).astype(np.float32), "yg": G.reshape(N, 128, L).astype(np.float32)}

@@ -1,0 +1,546 @@
+import math
+from concourse.mybir import dt, AluOpType, AxisListType, ActivationFunctionType
+
+A_ = AluOpType
+F_ = ActivationFunctionType
+NV, NC, L2, STEPS = 4, 2, 64, 6
+CUT_A, CUT_B, CUT_G, CUT_P0, CUT_P = (32, 32), (32, 32), (32, 32), (32, 32), (64,)
+XV = (0,)
+ALPHA = 0.8318
+TOP = 86.0
+E11, E12 = [math.exp(TOP - 16 * ALPHA * _th) for _th in (11, 12)]
+
+SCRATCH = {
+    "tev": ("sbuf", [128, 4096], "bfloat16"), "ptab": ("sbuf", [128, 4096], "bfloat16"),
+    "pc": ("sbuf", [128, 256], "int32"), "ti": ("sbuf", [128, 256], "int32"),
+    "dgi": ("sbuf", [128, 6 * 256], "int32"), "dg": ("sbuf", [128, 6 * 256], "bfloat16"),
+    "zi": ("sbuf", [128, 512], "int32"), "zf": ("sbuf", [128, 512], "float32"),
+    "sgi": ("sbuf", [128, 512], "int32"), "sgb": ("sbuf", [128, 512], "bfloat16"), "sgl": ("sbuf", [128, 512], "bfloat16"),
+    "si": ("sbuf", [128, 128], "int32"), "gi": ("sbuf", [128, 128], "int32"),
+    "inm": ("sbuf", [128, 10 * 192], "uint16"), "som": ("sbuf", [128, 8 * 192], "uint16"),
+    "rxm": ("sbuf", [128, 8 * 64], "uint16"), "oxm": ("sbuf", [128, 8 * 64], "uint16"),
+    "thb": ("sbuf", [128, 16], "float32"), "cnt": ("sbuf", [128, 8], "float32"), "cni": ("sbuf", [128, 16], "int32"),
+    "yo": ("sbuf", [128, 256], "float32"),
+    "pcol": ("sbuf", [128, 16], "int32"), "fcol": ("sbuf", [128, 32], "float32"),
+    "itf": ("sbuf", [128, 144], "float32"), "itg": ("sbuf", [128, 128], "float32"), "it8": ("sbuf", [128, 8], "float32"),
+    "itk": ("sbuf", [128, 8, 8], "float32"),
+    "bo": ("sbuf", [128, 2, 8], "bfloat16"), "wp": ("sbuf", [128, 3, 8], "bfloat16"),
+    "cna": ("sbuf", [128, 2, 8, 8], "bfloat16"), "cnb": ("sbuf", [128, 8, 8], "bfloat16"),
+    "c128": ("sbuf", [128, 8, 8], "bfloat16"), "cg": ("sbuf", [128, 64], "float32"),
+    "ch0": ("sbuf", [128, 64], "float32"), "ch1": ("sbuf", [128, 64], "float32"),
+    "cb0": ("sbuf", [128, 64], "bfloat16"), "cb1": ("sbuf", [128, 64], "bfloat16"),
+    "blk": ("sbuf", [128, 128], "bfloat16"), "idb": ("sbuf", [128, 128], "bfloat16"),
+    "one": ("sbuf", [128, 128], "bfloat16"), "w0": ("sbuf", [128, 144], "bfloat16"), "r8": ("sbuf", [128, 128], "bfloat16"),
+    "vsl": ("psum", [128, 512], "float32"), "gl": ("psum", [128, 512], "float32"),
+}
+for _c in "AB":
+    SCRATCH.update({
+        "sgf" + _c: ("sbuf", [128, 128], "float32"), "rxf" + _c: ("sbuf", [128, 64], "float32"),
+        "drz" + _c: ("sbuf", [128, 64], "float32"), "om" + _c: ("sbuf", [128, 64], "bfloat16"),
+        "xf" + _c: ("sbuf", [128, 64], "float32"),
+        "ex" + _c: ("sbuf", [128, 1024], "bfloat16"), "ge" + _c: ("sbuf", [128, 1024], "bfloat16"),
+        "gg" + _c: ("sbuf", [128, 1024], "bfloat16"), "gp" + _c: ("sbuf", [128, 1024], "bfloat16"),
+        "off" + _c: ("sbuf", [128, 64], "uint16"),
+        "cz" + _c: ("sbuf", [128, 2, 8, 8], "float32"), "tu" + _c: ("sbuf", [128, 8, 8], "float32"),
+        "zm" + _c: ("sbuf", [128, 17, 8], "float32"),
+        "zz" + _c: ("sbuf", [128, 17, 8], "float32"), "zk" + _c: ("sbuf", [128, 17, 8], "bfloat16"),
+        "pos" + _c: ("sbuf", [128, 64], "float32"), "p2" + _c: ("sbuf", [128, 64], "bfloat16"),
+        "nq" + _c: ("sbuf", [128, 64, 2], "bfloat16"), "pg" + _c: ("sbuf", [128, 64, 2], "float32"),
+        "mi" + _c: ("sbuf", [128, 64], "bfloat16"), "fu" + _c: ("sbuf", [128, 64], "float32"),
+        "pu" + _c: ("sbuf", [128, 64], "float32"), "nf" + _c: ("sbuf", [128, 64], "bfloat16"),
+        "mx" + _c: ("sbuf", [128, 8, 8], "float32"), "ww" + _c: ("sbuf", [128, 64], "bfloat16"),
+        "hit" + _c: ("sbuf", [128, 64], "float32"), "upd" + _c: ("sbuf", [128, 64], "float32"),
+        "nc" + _c: ("sbuf", [128, 64], "float32"), "st" + _c: ("sbuf", [128, 192], "float32"),
+        "cv" + _c: ("psum", [128, 8, 8, 8], "float32"), "pa" + _c: ("psum", [128, 8, 8, 8], "float32"),
+        "tr" + _c: ("psum", [128, 512], "float32"),
+    })
+NDMA = 24
+SEMAPHORES = ["v", "s", "p", "q", "loc"] + ["d%d" % i for i in range(NDMA)] \
+    + ["arr%d%s" % (t, c) for t in range(1, 5) for c in "AB"] + ["xar%d%s" % (t, c) for t in range(1, 4) for c in "AB"]
+
+SHIFT = {'3Bs': 13.5, 'pBs': -0.6, '5AG': -20.6, '1As': 24.9, 'u6s': 18.4, 'u7s': -3.6, 'u9s': 29.1, 'u1s': 22.7, '5AP': 32.9,
+         'gAs': 6.3, 'fAs': -14.2, '0As': -0.8, '2AP': -40.1, 'u3s': 4.5, 'ubs': 5.8, 'u4s': 13.2, 'ues': 29.5, 'pts': 18.3,
+         'u5s': 11.1, 'uas': 9.1, '2AG': -7.5, 'uks': -5.4, 'uAs': 0.2, '1AP': 8.0, 'ups': -11.3, 'u0s': -2.0, 'u2s': -0.6,
+         'u8s': 1.2, '0BP': 14.9, 'pAs': 5.9, 'gBG': 0.4, 'gAG': -3.3, '4AP': -30.8, '0AG': -10.3, '3AG': -22.4, 'uBs': -2.3,
+         '0AS': -3.7, '3AP': 27.3}
+CYC, PEC, LAT = 1.04e-3, 0.75e-3, 0.12
+
+
+def gath(n):
+    return 0.06 + 1.55 * CYC * n
+
+
+def cuts(ws):
+    out = []
+    for w in ws:
+        a = out[-1][1] if out else 0
+        out.append((a, a + w))
+    return out
+
+
+def small(n):
+    return max(64, n) * CYC
+
+
+def routes(core, dst, topo):
+    if topo.may_write(core, dst):
+        return [core, core]
+    own = [c for c in topo.cores_of(core) if c != core and topo.may_write(c, dst)]
+    own.sort(key=lambda c: topo.die(c) != topo.die(core))
+    return [own[0], own[1]]
+
+
+def build(T):
+    ops = []
+    nd = [0]
+    cur = ["u"]
+
+    def op(eng, cost, R, W, fn, bank=None, lat=0.0):
+        kind = "P" if eng == "p" else "s"
+        if eng in "vs" and cost > 0.45 and cur[0] != "u":
+            kind = "G" if eng == "v" else "S"
+        ops.append({"e": eng, "c": cost, "R": R, "W": W, "f": fn, "b": bank, "lat": lat, "key": cur[0] + W[0][-1] + kind})
+        return len(ops) - 1
+
+    def v(cost, R, W, fn, bank=None):
+        return op("v", cost, R, W, fn, bank)
+
+    def dma(queue, R, W, o, i, dur):
+        k = nd[0]
+        nd[0] += 1
+        ops.append({"e": queue, "c": 0.1, "R": R, "W": W, "b": None, "lat": dur, "dsem": "d%d" % k, "key": "us",
+                    "f": (lambda q, o=o, i=i: q.dma_start(o, i))})
+
+    def ts(out, in0, s1, o0, s2=None, o1=None):
+        if o1 is None:
+            return lambda q: q.tensor_scalar(out, in0, s1, None, o0)
+        return lambda q: q.tensor_scalar(out, in0, s1, s2, o0, o1)
+
+    def tt(out, a, b, o):
+        return lambda q: q.tensor_tensor(out, a, b, o)
+
+    def cp(out, a):
+        return lambda q: q.tensor_copy(out, a)
+
+    def act(out, a, f, bias=0.0, scale=1.0):
+        return lambda q: q.activation(out, a, f, bias=bias, scale=scale)
+
+    def mms(lst, first=True, last=True):
+        def f(q):
+            r = None
+            n = len(lst)
+            for i, (o, a, b) in enumerate(lst):
+                r = q.matmul(o, a, b, first and i == 0, last and i == n - 1)
+            return r
+        return f
+
+    def mmk(lst):
+        def f(q):
+            r = None
+            for o, a, b in lst:
+                r = q.matmul(o, a, b, True, True)
+            return r
+        return f
+
+    dma("y", [], ["zi"], T.zi[:], T.z[:], 3.0)
+    dma("y", [], ["pc"], T.pc[:], T.par[:], 2.5)
+    dma("s", [], ["sgi"], T.sgi[0:8, :], T.sg[:], 2.0)
+    dma("s", [], ["si"], T.si[:], T.s0[:], 2.0)
+    dma("s", [], ["gi"], T.gi[:], T.g0[:], 2.0)
+    dma("y", [], ["tev0"], T.tev[0:64, :], T.ev[0:64, :], 6.0)
+    dma("y", [], ["tev1"], T.tev[64:128, :], T.ev[64:128, :], 6.0)
+
+    fl = True
+    op("g", 0.2, [], ["pcol0"], lambda q: q.iota(T.pcol[:, 0:1], [[0, 1]], 0, 1))
+    op("g", 0.6, [], ["ti"], lambda q: q.iota(T.ti[:], [[1, 256]], 0, 256))
+    op("g", 0.4, [], ["itf"], lambda q: q.iota(T.itf[:], [[1, 144]], 0, 0, allow_small_or_imprecise_dtypes=fl))
+    op("g", 0.4, [], ["itg"], lambda q: q.iota(T.itg[:], [[1, 8], [0, 16]], 0, 0, allow_small_or_imprecise_dtypes=fl))
+    op("g", 0.2, [], ["it8"], lambda q: q.iota(T.it8[:], [[1, 8]], 0, 0, allow_small_or_imprecise_dtypes=fl))
+    op("g", 0.3, [], ["itk"], lambda q: q.iota(T.itk[:], [[1, 8], [0, 8]], 0, 0, allow_small_or_imprecise_dtypes=fl))
+    v(small(2048), [], ["ptab%d" % d for d in range(6)], lambda q: q.memset(T.ptab[:], 0.0))
+
+    def icol(j, src, *a):
+        v(small(1), ["pcol%d" % src], ["pcol%d" % j], ts(T.pcol[:, j:j + 1], T.pcol[:, src:src + 1], *a))
+    icol(1, 0, 4, A_.arith_shift_right)
+    icol(2, 0, 7, A_.bitwise_and)
+    icol(3, 0, 3, A_.arith_shift_right, 1, A_.bitwise_and)
+    icol(4, 0, 1, A_.arith_shift_right)
+    icol(5, 0, 1, A_.bitwise_and)
+    icol(6, 0, 1, A_.arith_shift_right, 7, A_.bitwise_and)
+    icol(7, 0, 15, A_.bitwise_and)
+    v(small(8), ["pcol%d" % j for j in range(8)], ["fc"], cp(T.fcol[:, 0:8], T.pcol[:, 0:8]))
+    FC = lambda j: T.fcol[:, j:j + 1]
+
+    def fcol(j, in0, s1, o0, s2=None, o1=None, dep=()):
+        v(small(1), ["fc"] + list(dep), ["fc%d" % j], ts(FC(j), in0, s1, o0, s2, o1))
+    fcol(8, FC(1), 8.0, A_.mult, FC(2), A_.add)
+    fcol(9, FC(5), -1000.0, A_.mult, FC(4), A_.add)
+    fcol(10, FC(5), 1000.0, A_.mult, FC(4), A_.add)
+    fcol(11, FC(10), -1000.0, A_.add, dep=["fc10"])
+    fcol(12, FC(1), 16.0, A_.mult, 16.0, A_.add)
+    fcol(13, FC(3), -1.0, A_.mult, 1.0, A_.add)
+    fcol(14, FC(7), -ALPHA, A_.mult, TOP - 64 * 16 * ALPHA, A_.add)
+    fcol(15, FC(6), 0.0, A_.is_equal)
+    fcol(16, FC(6), 1.0, A_.is_equal)
+    fcol(20, FC(6), 2.0, A_.is_equal, 2.0, A_.mult)
+    v(small(1), ["fc15", "fc16"], ["fc18"], tt(FC(18), FC(15), FC(16), A_.subtract))
+    v(small(1), ["fc15", "fc16"], ["fc19"], tt(FC(19), FC(15), FC(16), A_.add))
+    for o in range(2):
+        v(small(8), ["it8", "fc"], ["bo"], ts(T.bo[:, o], T.it8[:], FC(1), A_.is_equal, 1.0 - 2.0 * o, A_.mult))
+    for o in range(3):
+        v(small(8), ["it8", "fc", "fc%d" % (18 + o)], ["wp"], ts(T.wp[:, o], T.it8[:], FC(1), A_.is_equal, FC(18 + o), A_.mult))
+    v(small(64), [], ["cna"], lambda q: q.memset(T.cna[:, 0], 0.0))
+    v(small(64), ["itk", "fc"], ["cna"], ts(T.cna[:, 1], T.itk[:], FC(1), A_.is_equal, 2.0, A_.mult))
+    v(small(64), ["itk", "fc"], ["cnb"], ts(T.cnb[:], T.itk[:], FC(1), A_.is_equal, -512.0, A_.mult))
+    v(small(64), [], ["c128"], lambda q: q.memset(T.c128[:], 128.0))
+    v(small(64), ["itf", "fc8"], ["cg"], ts(T.cg[:], T.itf[:, 0:64], FC(8), A_.is_equal))
+    v(small(64), ["itf", "fc9"], ["ch0"], ts(T.ch0[:], T.itf[:, 0:64], FC(9), A_.is_equal))
+    v(small(64), ["itf", "fc11"], ["ch1"], ts(T.ch1[:], T.itf[:, 0:64], FC(11), A_.is_equal))
+    v(small(64), ["itf", "fc9"], ["cb0"], ts(T.cb0[:], T.itf[:, 0:64], FC(9), A_.is_equal))
+    v(small(64), ["itf", "fc11"], ["cb1"], ts(T.cb1[:], T.itf[:, 0:64], FC(11), A_.is_equal))
+    v(small(128), ["itg", "fc"], ["blk"], ts(T.blk[:], T.itg[:], FC(1), A_.is_equal))
+    v(small(128), ["itf", "fc", "pcol0"], ["idb"], ts(T.idb[:], T.itf[:, 0:128], FC(0), A_.is_equal))
+    v(small(128), ["itg", "fc"], ["r8"], ts(T.r8[:], T.itg[:], FC(0), A_.is_equal))
+    v(small(144), ["itf", "fc12"], ["w0"], ts(T.w0[:], T.itf[:], FC(12), A_.is_equal))
+    v(small(64), [], ["one"], lambda q: q.memset(T.one[:], 1.0))
+    for j, x in enumerate((11.0, 21.5, 1.5 * E11, 2.0 * E11)):
+        v(small(1), [], ["th0%d" % j], (lambda x, j: lambda q: q.memset(T.thb[:, j:j + 1], x))(x, j))
+    op("s", 0.1, ["th00"], ["warm"], act(T.fcol[:, 24:25], T.thb[:, 0:1], F_.Exp))
+    for c in "AB":
+        v(small(136), [], ["zz" + c], (lambda c: lambda q: q.memset(T["zz" + c][:], 0.0))(c))
+        v(small(136), [], ["zm" + c], (lambda c: lambda q: q.memset(T["zm" + c][:], 0.0))(c))
+        v(small(68), [], ["zk" + c], (lambda c: lambda q: q.memset(T["zk" + c][:], 0.0))(c))
+
+    DI = lambda d: T.dgi[:, 256 * d:256 * d + 256]
+    DG = lambda d: T.dg[:, 256 * d:256 * d + 256]
+    for d in (4, 5, 0, 1, 2, 3):
+        src, nm = (T.ti, "ti") if d > 3 else (T.pc, "pc")
+        sh = 6 * (d % 4) if d < 4 else 6 * (d - 4)
+        if sh:
+            v(small(256), [nm], ["dgi%d" % d], ts(DI(d), src[:], sh, A_.arith_shift_right, 63, A_.bitwise_and))
+        else:
+            v(small(256), [nm], ["dgi%d" % d], ts(DI(d), src[:], 63, A_.bitwise_and))
+        v(small(256), ["dgi%d" % d], ["dg%d" % d], ts(DG(d), DI(d), 0.5 if d % 2 == 0 else 32.0, A_.mult))
+        dma("y", ["dg%d" % d], ["ptab%d" % d], T.ptab[d::16, :], DG(d), 2.5)
+    PT = ["ptab%d" % d for d in range(6)]
+    EV = ["tev0", "tev1"]
+
+    v(small(512), ["sgi"], ["sgb"], cp(T.sgb[0:8, :], T.sgi[0:8, :]))
+    op("p", 0.3, ["r8", "sgb"], ["vsl"], lambda q: q.matmul(T.vsl[:], T.r8[0:8, :], T.sgb[0:8, :], True, True), "vsl")
+    v(small(512), ["vsl"], ["sgl"], cp(T.sgl[:], T.vsl[:]), "vsl")
+    v(small(512), ["zi"], ["zf"], cp(T.zf[:], T.zi[:]))
+
+    def slot(t, ci):
+        return 192 * (2 * t + ci)
+
+    for t in range(NV):
+        cur[0] = "p"
+        for ci, c in enumerate("AB"):
+            B = lambda n, c=c: T[n + c]
+            lanes = slice(L2 * ci, L2 * ci + L2)
+            tl = slice(128 * t + L2 * ci, 128 * t + L2 * ci + L2)
+            q0 = slot(t, ci)
+            IS, IG, IR = T.inm[:, q0:q0 + 64], T.inm[:, q0 + 64:q0 + 128], T.inm[:, q0 + 128:q0 + 192]
+            OX = T.oxm[:, 64 * (2 * t + ci):64 * (2 * t + ci) + 64]
+            RX = T.rxm[:, 64 * (2 * t + ci):64 * (2 * t + ci) + 64]
+            kS, kG, kR, kO = ["%s%d%s" % (n, t, c) for n in ("iS", "iG", "iR", "ox")]
+            if t == 0:
+                v(small(64), ["zi"], [kO], cp(OX, T.zi[:, tl]))
+                v(small(64), ["si"], [kS], cp(IS, T.si[:, lanes]))
+                v(small(64), ["gi"], [kG], cp(IG, T.gi[:, lanes]))
+                v(small(64), ["sgl"], ["pos" + c], cp(B("pos")[:], T.sgl[:, tl]))
+            else:
+                kX = "rx%d%s" % (t, c)
+                v(small(64), [kX], ["rxf" + c], cp(B("rxf")[:], RX))
+                v(small(128), ["rxf" + c, "zf"], ["drz" + c], tt(B("drz")[:], B("rxf")[:], T.zf[:, tl], A_.subtract))
+                v(small(64), [kR], ["om" + c], ts(B("om")[:], IR, -1.0, A_.mult, 1.0, A_.add))
+                vx = T.vsl[:, 256 * ci + 128:256 * ci + 192]
+                v(small(128), ["om" + c, "drz" + c], ["va" + c], tt(vx, B("om")[:], B("drz")[:], A_.mult), "vsl")
+                v(small(64), ["va" + c, "rxf" + c], ["xf" + c], tt(B("xf")[:], B("rxf")[:], vx, A_.subtract), "vsl")
+                v(small(64), ["xf" + c], [kO], cp(OX, B("xf")[:]))
+                v(small(128), ["om" + c, "sgl"], ["pos" + c], tt(B("pos")[:], B("om")[:], T.sgl[:, tl], A_.mult))
+            if t < NV - 1:
+                op("net", 1.2, [kO], ["rx%d%s" % (t + 1, c)], ("x", t + 1, ci, OX), None, 6.0)
+            op("s", gath(512), EV + [kO], ["exs" + c], act(B("ex")[:, 512:1024], T.tev[:].indirect(OX[:, 32:64]), F_.Copy))
+            if ci in XV:
+                v(gath(512), EV + [kO], ["exv" + c], cp(B("ex")[:, 0:512], T.tev[:].indirect(OX[:, 0:32])))
+            else:
+                op("s", gath(512), EV + [kO], ["exv" + c], act(B("ex")[:, 0:512], T.tev[:].indirect(OX[:, 0:32]), F_.Copy))
+            v(small(64), [kS], ["Sf" + c], cp(B("sgf")[:, 0:64], IS))
+            v(small(64), [kG], ["Gf" + c], cp(B("sgf")[:, 64:128], IG))
+            for h in range(2):
+                op("s", 0.07, ["pos" + c], ["nq" + c], act(B("nq")[:, :, h], B("pos")[:], F_.Copy, 2.0, -1.0))
+                v(small(64), [kG, "fc13"], ["pg" + c], ts(B("pg")[:, :, h], IG, FC(13) if h == 0 else FC(3), A_.mult))
+            op("s", 0.07, ["pos" + c], ["p2" + c], act(B("p2")[:], B("pos")[:], F_.Copy, 0.0, 2.0))
+            op("p", 384 * PEC, ["pg" + c, "cg", "nq" + c, "cnb", "one", "c128"], ["gE" + c],
+               mms([(B("pa")[:, 3], B("pg")[:], T.cg[:]), (B("pa")[:, 3], B("nq")[:], T.cnb[:]), (B("pa")[:, 3], T.one[:], T.c128[:])]), "pa" + c)
+        if t > 0:
+            op("p", 0.1, ["omA", "omB", "one"], ["par"],
+               mms([(T.trA[:, 320:384], T.one[:], T.omA[:]), (T.trA[:, 320:384], T.one[:], T.omB[:])]), "trA")
+            v(small(64), ["par"], ["cnt"], lambda q, t=t: q.tensor_reduce(T.cnt[:, t:t + 1], T.trA[:, 320:384], AxisListType.X, A_.add), "trA")
+            v(small(1), ["cnt"], ["cni"], cp(T.cni[:, t:t + 1], T.cnt[:, t:t + 1]))
+            v(small(1), ["cni"], ["cnj"], ts(T.cni[:, 8 + t:9 + t], T.cni[:, t:t + 1], 16, A_.bitwise_and))
+            TB = lambda j, t=t: T.thb[:, 4 * t + j:4 * t + j + 1]
+            for j, (m, b) in ((1, (-0.0625, 21.5)), (0, (0.0625, 11.0))):
+                v(small(1), ["cnj"], ["th%d%d" % (t, j)], ts(TB(j), T.cni[:, 8 + t:9 + t], m, A_.mult, b, A_.add))
+            for j, m in ((2, 1.5), (3, 2.0)):
+                k = "th%d%d" % (t, j)
+                v(small(1), ["cnj"], [k], ts(TB(j), T.cni[:, 8 + t:9 + t], -m * E11 / 16, A_.mult, m * E11, A_.add))
+                v(small(1), [k], [k], ts(TB(j), TB(j), m * E12, A_.max))
+        TH = lambda j, t=t: T.thb[:, 4 * t + j:4 * t + j + 1]
+        for i in range(STEPS):
+            cur[0] = str(i)
+            for ci, c in enumerate("AB"):
+                B = lambda n, c=c: T[n + c]
+                q0 = slot(t, ci)
+                off, kF = (T.inm[:, q0:q0 + 64], "iS%d%s" % (t, c)) if i == 0 else (B("off"), "off" + c)
+                for a, b in cuts(CUT_P0 if i == 0 else CUT_P):
+                    op("s", gath(16 * (b - a)), PT + [kF], ["gp" + c],
+                       act(B("gp")[:, 16 * a:16 * b], T.ptab[:].indirect(off[:, a:b]), F_.Copy))
+                for a, b in cuts((CUT_A, CUT_B)[ci]):
+                    v(gath(16 * (b - a)), EV + [kF, "exs" + c, "exv" + c], ["ge" + c],
+                      tt(B("ge")[:, 16 * a:16 * b], T.tev[:].indirect(off[:, a:b]), B("ex")[:, 16 * a:16 * b], A_.is_ge))
+                op("p", 512 * PEC, ["gp" + c, "wp"], ["pa" + c],
+                   mmk([(B("pa")[:, 0:3, :, k], B("gp")[:, k::8], T.wp[:]) for k in range(8)]), "pa" + c)
+                op("p", 128 * PEC, ["nq" + c, "cna"], ["cw" + c], mms([(B("cv")[:, 0:2], B("nq")[:], T.cna[:])], True, False), "cv" + c)
+                op("p", 512 * PEC, ["cw" + c, "ge" + c, "bo"], ["cv" + c],
+                   mms([(B("cv")[:, 0:2, :, k], B("ge")[:, k::8], T.bo[:]) for k in range(8)], False, True), "cv" + c)
+                op("s", 0.08, ["cv" + c], ["cz0" + c], act(B("cz")[:, 0], B("cv")[:, 0], F_.Sign, -7.5), "cv" + c)
+                op("s", 0.08, ["cv" + c, "th%d1" % t], ["cz1" + c], act(B("cz")[:, 1], B("cv")[:, 1], F_.Sign, TH(1), -1.0), "cv" + c)
+                VE, VD = T.vsl[:, 256 * ci:256 * ci + 64], T.vsl[:, 256 * ci + 64:256 * ci + 128]
+                v(small(64), ["cz0" + c, "pa" + c], ["tu" + c], tt(B("tu")[:], B("cz")[:, 0], B("pa")[:, 0], A_.mult), "pa" + c)
+                NX, MV = B("zz")[:, 1::2, :], B("zm")[:, 1::2, :]
+                v(small(64), ["tu" + c, "pa" + c], ["zz" + c], tt(NX, B("tu")[:], B("pa")[:, 1], A_.add), "pa" + c)
+                op("p", 512 * PEC, ["zz" + c, "ch0", "ch1"], ["aN" + c],
+                   mms([(B("tr")[:, 0:64], B("zz")[:, 1:17, :], T.ch0[:]), (B("tr")[:, 0:64], B("zz")[:, 0:16, :], T.ch1[:])], True, False), "tr" + c)
+                v(small(64), ["zz" + c, "gE" + c], ["ve" + c], tt(VE, NX, B("pa")[:, 3], A_.is_equal), "pa" + c)
+                v(small(64), ["zz" + c, "pa" + c], ["vd" + c], tt(VD, B("pa")[:, 2], NX, A_.subtract), "pa" + c)
+                v(small(64), ["ve" + c, "cz1" + c], ["mx" + c], tt(B("mx")[:], B("cz")[:, 1], VE, A_.max))
+                v(small(64), ["mx" + c, "vd" + c], ["zm" + c], tt(MV, B("mx")[:], VD, A_.mult))
+                if i == STEPS - 1:
+                    v(small(64), ["mx" + c, "cv" + c], ["zk" + c], tt(B("zk")[:, 1::2, :], B("mx")[:], B("cv")[:, 1], A_.mult), "cv" + c)
+                op("p", 512 * PEC, ["zm" + c, "aN" + c, "ch0", "ch1"], ["aL" + c],
+                   mms([(B("tr")[:, 0:64], B("zm")[:, 1:17, :], T.ch0[:]), (B("tr")[:, 0:64], B("zm")[:, 0:16, :], T.ch1[:])], False, True), "tr" + c)
+                if i < STEPS - 1:
+                    v(small(64), ["aL" + c], ["off" + c], cp(B("off")[:], B("tr")[:, 0:64]), "tr" + c)
+            if i == 0:
+                cur[0] = "g"
+                for ci, c in enumerate("AB"):
+                    B = lambda n, c=c: T[n + c]
+                    q0 = slot(t, ci) + 64
+                    for a, b in cuts(CUT_G):
+                        v(gath(16 * (b - a)), EV + ["iG%d%s" % (t, c), "exs" + c, "exv" + c], ["gg" + c],
+                          tt(B("gg")[:, 16 * a:16 * b], T.tev[:].indirect(T.inm[:, q0 + a:q0 + b]), B("ex")[:, 16 * a:16 * b], A_.is_ge))
+                    CG, FM = T.gl[:, 128 * ci:128 * ci + 64], T.gl[:, 128 * ci + 64:128 * ci + 128]
+                    op("p", 1024 * PEC, ["gg" + c, "w0"], ["cG" + c],
+                       mms([(CG, T.w0[:, 16 - k:144 - k], B("gg")[:, k::16]) for k in range(16)]), "gl")
+                    v(small(64), ["cG" + c, "th%d0" % t], ["mi" + c], ts(B("mi")[:], CG, TH(0), A_.is_lt), "gl")
+                    op("p", 0.1, ["mi" + c, "p2" + c, "blk"], ["fm" + c],
+                       mms([(FM, T.blk[:], B("mi")[:]), (FM, T.blk[:], B("p2")[:])]), "gl")
+                    v(small(64), ["fm" + c], ["fu" + c], ts(B("fu")[:], FM, 0.0, A_.is_equal), "gl")
+                    v(small(64), ["fm" + c], ["pu" + c], ts(B("pu")[:], FM, 36.0, A_.is_gt), "gl")
+                    v(small(64), ["fm" + c], ["nf" + c], ts(B("nf")[:], FM, 0.0, A_.is_gt, -64.0, A_.mult), "gl")
+        cur[0] = "f"
+        for ci, c in enumerate("AB"):
+            B = lambda n, c=c: T[n + c]
+            bk, bg = "tr" + c, "gl"
+            KL, MM, AL = T.gl[:, 256 + 128 * ci:320 + 128 * ci], T.gl[:, 320 + 128 * ci:384 + 128 * ci], B("tr")[:, 0:64]
+            va, vb, vm = [T.vsl[:, 256 * ci + 64 * j:256 * ci + 64 * j + 64] for j in (2, 3, 0)]
+            Sf, Gf = B("sgf")[:, 0:64], B("sgf")[:, 64:128]
+            so = T.som[:, slot(t, ci):slot(t, ci) + 192]
+            kM = "so%d%s" % (t, c)
+            op("p", 0.15, ["zk" + c, "nf" + c, "cb0", "cb1", "idb"], ["kL" + c],
+               mms([(KL, B("zk")[:, 1:17, :], T.cb0[:]), (KL, B("zk")[:, 0:16, :], T.cb1[:]), (KL, T.idb[:], B("nf")[:])]), bg)
+            op("s", 0.08, ["kL" + c, "fc14"], ["ww" + c], act(B("ww")[:], KL, F_.Exp, FC(14), 16 * ALPHA), bg)
+            op("p", 0.1, ["ww" + c, "blk"], ["MM" + c], mms([(MM, T.blk[:], B("ww")[:])]), bg)
+            v(small(64), ["MM" + c, "th%d2" % t], ["ve" + c], ts(vm, MM, 0.5, A_.mult, TH(2), A_.max), bg)
+            if t < NV - 1:
+                v(small(64), ["MM" + c, "th%d3" % t], ["nc" + c], ts(B("nc")[:], MM, TH(3), A_.is_lt), bg)
+            v(small(64), ["aL" + c, "Sf" + c], ["va" + c], tt(va, AL, Sf, A_.subtract), bk)
+            v(small(64), ["va" + c, "pos" + c], ["va" + c], tt(va, B("pos")[:], va, A_.mult))
+            v(small(64), ["va" + c, "Sf" + c], ["stS" + c], tt(B("st")[:, 0:64], Sf, va, A_.add))
+            v(small(64), ["stS" + c], [kM + "S"], cp(so[:, 0:64], B("st")[:, 0:64]))
+            v(small(64), ["aL" + c, "Gf" + c], ["vb" + c], tt(vb, AL, Gf, A_.subtract), bk)
+            vp = T.vsl[:, 256 * ci + 64:256 * ci + 128]
+            v(small(64), ["vb" + c, "pu" + c], ["vd" + c], tt(vp, B("pu")[:], vb, A_.mult))
+            v(small(64), ["vd" + c, "Gf" + c], ["upd" + c], tt(B("upd")[:], Gf, vp, A_.add))
+            v(small(64), ["ve" + c, "ww" + c], ["hit" + c], tt(B("hit")[:], B("ww")[:], vm, A_.is_gt))
+            if t < NV - 1:
+                v(small(128), ["nc" + c, "fu" + c], ["stR" + c], tt(B("st")[:, 128:192], B("nc")[:], B("fu")[:], A_.mult))
+            v(small(64), ["hit" + c, "vb" + c], ["vb" + c], tt(vb, B("hit")[:], vb, A_.mult))
+            v(small(64), ["vb" + c, "upd" + c], ["stG" + c], tt(B("st")[:, 64:128], B("upd")[:], vb, A_.add))
+            nw = 192 if t < NV - 1 else 128
+            v(small(nw - 64), ["stG" + c] + (["stR" + c] if t < NV - 1 else []), [kM], cp(so[:, 64:nw], B("st")[:, 64:nw]))
+            op("net", 1.2, [kM, kM + "S"], ["%s%d%s" % (n, t + 1, c) for n in ("iS", "iG", "iR")],
+               ("m", t + 1, ci, so[:, 0:nw]), None, 6.0)
+    for ci, c in enumerate("AB"):
+        q0 = slot(NV, ci)
+        for j in range(2):
+            v(small(64), ["iS4" + c], ["yo%d%s" % (j, c)], cp(T.yo[:, 128 * j + 64 * ci:128 * j + 64 * ci + 64], T.inm[:, q0 + 64 * j:q0 + 64 * j + 64]))
+            dma("ys"[j], ["yo%d%s" % (j, c)], [], (T.ys, T.yg)[j][:, 64 * ci:64 * ci + 64], T.yo[:, 128 * j + 64 * ci:128 * j + 64 * ci + 64], 2.0)
+    return ops
+
+
+def link(ops):
+    wr, rd, base, bank = {}, {}, {}, {}
+    for n, o in enumerate(ops):
+        d = set()
+        for k in o["R"]:
+            d.update(wr.get(k, ()))
+        for k in o["W"]:
+            old = wr.get(k, [])
+            piece = old and k not in o["R"] and not rd.get(k) and all(ops[m]["e"] == o["e"] and ops[m]["W"] == o["W"] for m in old)
+            if piece:
+                wr[k] = old + [n]
+            else:
+                base[k] = set(old) | set(rd.get(k, ()))
+                wr[k] = [n]
+                rd[k] = []
+            d.update(base[k])
+        if o["b"]:
+            sg = bank.get(o["b"])
+            if not sg or sg["e"] != o["e"]:
+                sg = bank[o["b"]] = {"e": o["e"], "n": [], "pre": set(sg["n"]) if sg else set()}
+            d.update(sg["pre"])
+            sg["n"].append(n)
+        d.discard(n)
+        o["D"] = sorted(d)
+        for k in o["R"]:
+            if k not in o["W"]:
+                rd.setdefault(k, []).append(n)
+    return ops
+
+
+def order(ops):
+    n = len(ops)
+    suc = [[] for _ in ops]
+    pri = [0.0] * n
+    need = [len(o["D"]) for o in ops]
+    for i, o in enumerate(ops):
+        for d in o["D"]:
+            suc[d].append(i)
+    for i in range(n - 1, -1, -1):
+        o = ops[i]
+        pri[i] = o["c"] + o["lat"] + LAT + max([pri[j] for j in suc[i]] or [0.0])
+    for i in range(n):
+        pri[i] += SHIFT.get(ops[i]["key"], 0.0)
+    free, ready, est, done, seq = {}, [], [0.0] * n, [0.0] * n, []
+    ready = [i for i in range(n) if not need[i]]
+    q = lambda e: "g" if e == "net" else e
+    while ready:
+        tm = min(max(est[i], free.get(q(ops[i]["e"]), 0.0)) for i in ready)
+        first = min((max(est[i], free.get(q(ops[i]["e"]), 0.0)), -pri[i], i) for i in ready)
+        eng = q(ops[first[2]]["e"])
+        cand = [i for i in ready if q(ops[i]["e"]) == eng and max(est[i], free.get(eng, 0.0)) <= tm + 0.02]
+        b = max(cand, key=lambda i: (pri[i], -i))
+        s = max(est[b], free.get(eng, 0.0))
+        free[eng] = s + ops[b]["c"]
+        done[b] = s + ops[b]["c"] + ops[b]["lat"]
+        ready.remove(b)
+        seq.append(b)
+        for j in suc[b]:
+            need[j] -= 1
+            est[j] = max(est[j], done[b] + LAT)
+            if not need[j]:
+                ready.append(j)
+    return seq
+
+
+def emit(g, core, T, topo, ops, seq, nxt, home):
+    qs = {"v": g.vector, "s": g.scalar, "p": g.tensor, "g": g, "net": g, "y": g.sync}
+    cs = {"v": "v", "s": "s", "p": "p", "g": "q"}
+    known = {e: {} for e in "vspgy"}
+    count = {}
+    loc = 0
+    for n in seq:
+        o = ops[n]
+        e = "g" if o["e"] == "net" else o["e"]
+        q, kn = qs[e], known[e]
+        for d in o["D"]:
+            for sem, val, clk in ops[d]["sig"]:
+                if kn.get(sem, 0) < val:
+                    q.wait_ge(T.sem[sem], val)
+                    kn[sem] = val
+                    for k2, v2 in clk.items():
+                        if kn.get(k2, 0) < v2:
+                            kn[k2] = v2
+        if o["e"] == "net":
+            kind, t, ci, src = o["f"]
+            dst = home if t == NV else nxt
+            via = routes(core, dst, topo)[ci]
+            to = dst if via == core else via
+            sem = ("arr%d%s" if kind == "m" else "xar%d%s") % (t, "AB"[ci])
+            wide = 192 if kind == "m" else 64
+            w = 128 if kind == "m" and t == NV else wide
+            at = wide * (2 * t + ci)
+            land = (T.inm if kind == "m" else T.rxm)[:, at:at + w]
+            rid, pid = topo.addr(to, core)
+            g.remote_dma(land, src, T.sem[sem], T.sem.loc, pid, rid, topo.mask(core, to))
+            loc += len(topo.engines(core, to))
+            o["sig"] = [(sem, last_hop(T, core, t, kind, ci, topo), {})]
+        elif "dsem" in o:
+            o["f"](q).then_inc(T.sem[o["dsem"]], 16)
+            o["sig"] = [(o["dsem"], 16, dict(kn))]
+        else:
+            sem = cs[e]
+            count[sem] = count.get(sem, 0) + 1
+            o["f"](q).then_inc(T.sem[sem], 1)
+            clk = dict(kn)
+            clk[sem] = count[sem]
+            o["sig"] = [(sem, count[sem], clk)]
+    for o in ops:
+        if "dsem" in o:
+            g.wait_ge(T.sem[o["dsem"]], 16)
+    for sem, val in count.items():
+        g.wait_ge(T.sem[sem], val)
+    g.wait_ge(T.sem.loc, loc)
+
+
+def ends(rank, T, kind, t):
+    n = len(T.cores)
+    return (rank - (NV - 1)) % n if t == NV else (rank + 1) % n
+
+
+def last_hop(T, core, t, kind, ci, topo):
+    rank, n = T.rank_of(core), len(T.cores)
+    src = T.cores[(rank + (NV - 1)) % n] if t == NV else T.cores[(rank - 1) % n]
+    via = routes(src, core, topo)[ci]
+    return len(topo.engines(via, core))
+
+
+def relay(g, core, T, topo):
+    jobs = []
+    for rank, src in enumerate(T.cores):
+        if core not in topo.cores_of(src):
+            continue
+        for t in range(1, NV + 1):
+            dst = T.cores[ends(rank, T, "m", t)]
+            for ci in range(NC):
+                if routes(src, dst, topo)[ci] == core:
+                    if t < NV:
+                        jobs.append((src, dst, t, 0, ci))
+                    jobs.append((src, dst, t, 1, ci))
+    jobs.sort(key=lambda j: (j[2], j[3], j[4]))
+    loc = 0
+    for src, dst, t, m, ci in jobs:
+        wide = 192 if m else 64
+        w = 128 if m and t == NV else wide
+        at = wide * (2 * t + ci)
+        sem = T.sem[("arr%d%s" if m else "xar%d%s") % (t, "AB"[ci])]
+        buf = (T.inm if m else T.rxm)[:, at:at + w]
+        g.wait_ge(sem, len(topo.engines(src, core)))
+        rid, pid = topo.addr(dst, core)
+        g.remote_dma(buf, buf, sem, T.sem.loc, pid, rid, topo.mask(core, dst))
+        loc += len(topo.engines(core, dst))
+    if loc:
+        g.wait_ge(T.sem.loc, loc)
+
+
+def rank_program(g, core, T, topo):
+    rank = T.rank_of(core)
+    if rank is None:
+        relay(g, core, T, topo)
+        return
+    ops = link(build(T))
+    seq = order(ops)
+    emit(g, core, T, topo, ops, seq, T.cores[ends(rank, T, "m", 1)], T.cores[ends(rank, T, "m", NV)])

@@ -4,70 +4,69 @@ from concourse.mybir import dt, AluOpType, AxisListType, ActivationFunctionType
 A_ = AluOpType
 F_ = ActivationFunctionType
 NV, NC, L2, STEPS = 4, 2, 64, 6
-CUT_A, CUT_B, CUT_G, CUT_P0, CUT_P = (32, 32), (32, 32), (32, 32), (32, 32), (64,)
+CUT = {"v": (34, 16, 14), "v0": (32, 32), "g": (32, 32), "s": (24, 20, 20), "s0": (32, 32), "x": (32, 32)}
 XV = (0,)
-ALPHA = 0.8318
-TOP = 86.0
-E11, E12 = [math.exp(TOP - 16 * ALPHA * _th) for _th in (11, 12)]
+OPT = {"late": 5, "nev": True}
+PF = False
+ALPHA, GAP, TOP = 0.8, 18, 86.0
+TAU = 5.0 * math.exp(TOP - ALPHA * GAP * 12)
+MID = 2048.0
+BIG = 16384.0
+MX, MS, MG, MR, MW = 0, 64, 128, 192, 256
 
 SCRATCH = {
     "tev": ("sbuf", [128, 4096], "bfloat16"), "ptab": ("sbuf", [128, 4096], "bfloat16"),
     "pc": ("sbuf", [128, 256], "int32"), "ti": ("sbuf", [128, 256], "int32"),
     "dgi": ("sbuf", [128, 6 * 256], "int32"), "dg": ("sbuf", [128, 6 * 256], "bfloat16"),
-    "zi": ("sbuf", [128, 512], "int32"), "zf": ("sbuf", [128, 512], "float32"),
-    "sgi": ("sbuf", [128, 512], "int32"), "sgb": ("sbuf", [128, 512], "bfloat16"), "sgl": ("sbuf", [128, 512], "bfloat16"),
-    "si": ("sbuf", [128, 128], "int32"), "gi": ("sbuf", [128, 128], "int32"),
-    "inm": ("sbuf", [128, 10 * 192], "uint16"), "som": ("sbuf", [128, 8 * 192], "uint16"),
-    "rxm": ("sbuf", [128, 8 * 64], "uint16"), "oxm": ("sbuf", [128, 8 * 64], "uint16"),
-    "thb": ("sbuf", [128, 16], "float32"), "cnt": ("sbuf", [128, 8], "float32"), "cni": ("sbuf", [128, 16], "int32"),
+    "zi": ("sbuf", [128, 4, 2, 64], "int32"), "li": ("sbuf", [128, 2, 2, 64], "int32"),
+    "zo": ("sbuf", [128, 2, 192], "float16"), "zn": ("sbuf", [128, 2, 192], "float16"),
+    "sgi": ("sbuf", [128, 512], "int32"), "sgb": ("sbuf", [128, 512], "float16"),
+    "inm": ("sbuf", [128, 10 * MW], "uint16"), "som": ("sbuf", [128, 8 * MW], "uint16"),
+    "cnt": ("sbuf", [128, 8], "float32"), "cni": ("sbuf", [128, 16], "int32"), "junk": ("sbuf", [128, 64], "float32"),
     "yo": ("sbuf", [128, 256], "float32"),
     "pcol": ("sbuf", [128, 16], "int32"), "fcol": ("sbuf", [128, 32], "float32"),
-    "itf": ("sbuf", [128, 144], "float32"), "itg": ("sbuf", [128, 128], "float32"), "it8": ("sbuf", [128, 8], "float32"),
-    "itk": ("sbuf", [128, 8, 8], "float32"),
-    "bo": ("sbuf", [128, 2, 8], "bfloat16"), "wp": ("sbuf", [128, 3, 8], "bfloat16"),
-    "cna": ("sbuf", [128, 2, 8, 8], "bfloat16"), "cnb": ("sbuf", [128, 8, 8], "bfloat16"),
-    "c128": ("sbuf", [128, 8, 8], "bfloat16"), "cg": ("sbuf", [128, 64], "float32"),
-    "ch0": ("sbuf", [128, 64], "float32"), "ch1": ("sbuf", [128, 64], "float32"),
-    "cb0": ("sbuf", [128, 64], "bfloat16"), "cb1": ("sbuf", [128, 64], "bfloat16"),
-    "blk": ("sbuf", [128, 128], "bfloat16"), "idb": ("sbuf", [128, 128], "bfloat16"),
-    "one": ("sbuf", [128, 128], "bfloat16"), "w0": ("sbuf", [128, 144], "bfloat16"), "r8": ("sbuf", [128, 128], "bfloat16"),
-    "vsl": ("psum", [128, 512], "float32"), "gl": ("psum", [128, 512], "float32"),
+    "itf": ("sbuf", [128, 144], "bfloat16"), "itg": ("sbuf", [128, 128], "bfloat16"), "it8": ("sbuf", [128, 8], "bfloat16"),
+    "itk": ("sbuf", [128, 8, 8], "bfloat16"),
+    "bo": ("sbuf", [128, 2, 8], "bfloat16"), "wp0": ("sbuf", [128, 8, 4], "bfloat16"), "wp1": ("sbuf", [128, 8, 3], "bfloat16"),
+    "cna": ("sbuf", [128, 2, 8, 8], "bfloat16"), "cne": ("sbuf", [128, 8, 8], "bfloat16"), "cg": ("sbuf", [128, 64], "float16"),
+    "w0": ("sbuf", [128, 144], "bfloat16"),
 }
+for _n in ("ch0", "ch1", "nh0", "nh1"):
+    SCRATCH[_n] = ("sbuf", [128, 64], "float16")
+for _n in ("cb0", "cb1"):
+    SCRATCH[_n] = ("sbuf", [128, 64], "bfloat16")
+for _n in ("idh", "ndh", "hw0", "r8"):
+    SCRATCH[_n] = ("sbuf", [128, 128], "float16")
+for _n in ("idb", "blk", "nbk", "tbk", "wr0", "wr1"):
+    SCRATCH[_n] = ("sbuf", [128, 128], "bfloat16")
 for _c in "AB":
+    SCRATCH["mh" + _c] = ("sbuf", [128, MW], "float16")
+    SCRATCH["off" + _c] = ("sbuf", [128, 64], "uint16")
+    for _n in ("ex", "ge", "gg", "gp"):
+        SCRATCH[_n + _c] = ("sbuf", [128, 1024], "bfloat16")
+    for _n, _w in (("d1", 192), ("dG", 192), ("dX", 128), ("dS", 128), ("mi", 64), ("nf", 64), ("pu", 64), ("w4", 64), ("w5", 64)):
+        SCRATCH[_n + _c] = ("sbuf", [128, _w], "bfloat16")
+    for _n, _w in (("va", 192), ("nx", 192), ("oG", 192), ("oX", 128), ("oS", 128), ("ab", 64)):
+        SCRATCH[_n + _c] = ("sbuf", [128, _w], "float32")
     SCRATCH.update({
-        "sgf" + _c: ("sbuf", [128, 128], "float32"), "rxf" + _c: ("sbuf", [128, 64], "float32"),
-        "drz" + _c: ("sbuf", [128, 64], "float32"), "om" + _c: ("sbuf", [128, 64], "bfloat16"),
-        "xf" + _c: ("sbuf", [128, 64], "float32"),
-        "ex" + _c: ("sbuf", [128, 1024], "bfloat16"), "ge" + _c: ("sbuf", [128, 1024], "bfloat16"),
-        "gg" + _c: ("sbuf", [128, 1024], "bfloat16"), "gp" + _c: ("sbuf", [128, 1024], "bfloat16"),
-        "off" + _c: ("sbuf", [128, 64], "uint16"),
-        "cz" + _c: ("sbuf", [128, 2, 8, 8], "float32"), "tu" + _c: ("sbuf", [128, 8, 8], "float32"),
-        "zm" + _c: ("sbuf", [128, 17, 8], "float32"),
-        "zz" + _c: ("sbuf", [128, 17, 8], "float32"), "zk" + _c: ("sbuf", [128, 17, 8], "bfloat16"),
-        "pos" + _c: ("sbuf", [128, 64], "float32"), "p2" + _c: ("sbuf", [128, 64], "bfloat16"),
-        "nq" + _c: ("sbuf", [128, 64, 2], "bfloat16"), "pg" + _c: ("sbuf", [128, 64, 2], "float32"),
-        "mi" + _c: ("sbuf", [128, 64], "bfloat16"), "fu" + _c: ("sbuf", [128, 64], "float32"),
-        "pu" + _c: ("sbuf", [128, 64], "float32"), "nf" + _c: ("sbuf", [128, 64], "bfloat16"),
-        "mx" + _c: ("sbuf", [128, 8, 8], "float32"), "ww" + _c: ("sbuf", [128, 64], "bfloat16"),
-        "hit" + _c: ("sbuf", [128, 64], "float32"), "upd" + _c: ("sbuf", [128, 64], "float32"),
-        "nc" + _c: ("sbuf", [128, 64], "float32"), "st" + _c: ("sbuf", [128, 192], "float32"),
-        "cv" + _c: ("psum", [128, 8, 8, 8], "float32"), "pa" + _c: ("psum", [128, 8, 8, 8], "float32"),
-        "tr" + _c: ("psum", [128, 512], "float32"),
+        "ne" + _c: ("sbuf", [128, 192], "float16"), "a0" + _c: ("sbuf", [128, 64], "float16"),
+        "zc4" + _c: ("sbuf", [128, 17, 8], "bfloat16"), "zc5" + _c: ("sbuf", [128, 17, 8], "bfloat16"),
+        "pq" + _c: ("sbuf", [128, 64, 2], "bfloat16"), "pg" + _c: ("sbuf", [128, 64, 2], "float16"),
+        "cv" + _c: ("psum", [128, 8, 8, 8], "float32"), "pa" + _c: ("psum", [128, 512] if PF else [128, 2, 8, 8, 4], "float32"),
+        "tr" + _c: ("psum", [128, 512], "float32"), "fz" + _c: ("psum", [128, 8, 64], "float32"),
     })
+    for _j in range(3):
+        SCRATCH["zz%d%s" % (_j, _c)] = ("sbuf", [128, 17, 8], "float16")
 NDMA = 24
-SEMAPHORES = ["v", "s", "p", "q", "loc"] + ["d%d" % i for i in range(NDMA)] \
-    + ["arr%d%s" % (t, c) for t in range(1, 5) for c in "AB"] + ["xar%d%s" % (t, c) for t in range(1, 4) for c in "AB"]
+SEMAPHORES = ["v", "s", "p", "q", "loc", "zarA", "zarB"] + ["d%d" % i for i in range(NDMA)] \
+    + ["arr%d%s" % (t, c) for t in range(1, 5) for c in "AB"]
 
-SHIFT = {'3Bs': 13.5, 'pBs': -0.6, '5AG': -20.6, '1As': 24.9, 'u6s': 18.4, 'u7s': -3.6, 'u9s': 29.1, 'u1s': 22.7, '5AP': 32.9,
-         'gAs': 6.3, 'fAs': -14.2, '0As': -0.8, '2AP': -40.1, 'u3s': 4.5, 'ubs': 5.8, 'u4s': 13.2, 'ues': 29.5, 'pts': 18.3,
-         'u5s': 11.1, 'uas': 9.1, '2AG': -7.5, 'uks': -5.4, 'uAs': 0.2, '1AP': 8.0, 'ups': -11.3, 'u0s': -2.0, 'u2s': -0.6,
-         'u8s': 1.2, '0BP': 14.9, 'pAs': 5.9, 'gBG': 0.4, 'gAG': -3.3, '4AP': -30.8, '0AG': -10.3, '3AG': -22.4, 'uBs': -2.3,
-         '0AS': -3.7, '3AP': 27.3}
-CYC, PEC, LAT = 1.04e-3, 0.75e-3, 0.12
+SHIFT = {}
+PAR = {"cyc": 0.95e-3, "pec": 0.55e-3, "lat": 0.16, "gat": 1.4, "net": 5.0, "ev": 8.5}
 
 
 def gath(n):
-    return 0.06 + 1.55 * CYC * n
+    return 0.06 + PAR["gat"] * PAR["cyc"] * n
 
 
 def cuts(ws):
@@ -79,7 +78,7 @@ def cuts(ws):
 
 
 def small(n):
-    return max(64, n) * CYC
+    return max(64, n) * PAR["cyc"]
 
 
 def routes(core, dst, topo):
@@ -90,26 +89,32 @@ def routes(core, dst, topo):
     return [own[0], own[1]]
 
 
+def span(t, ci):
+    return (MW * (2 * t + ci), MW) if t < NV else (MW * (2 * t + ci) + MS, 128)
+
+
 def build(T):
     ops = []
     nd = [0]
     cur = ["u"]
 
-    def op(eng, cost, R, W, fn, bank=None, lat=0.0):
-        kind = "P" if eng == "p" else "s"
-        if eng in "vs" and cost > 0.45 and cur[0] != "u":
-            kind = "G" if eng == "v" else "S"
-        ops.append({"e": eng, "c": cost, "R": R, "W": W, "f": fn, "b": bank, "lat": lat, "key": cur[0] + W[0][-1] + kind})
-        return len(ops) - 1
+    def op(eng, cost, R, W, fn, bank=None, lat=0.0, line=None):
+        ops.append({"e": eng, "c": cost, "R": R, "W": W, "f": fn, "b": bank, "lat": lat, "key": cur[0] + W[0], "line": line})
 
     def v(cost, R, W, fn, bank=None):
-        return op("v", cost, R, W, fn, bank)
+        op("v", cost, R, W, fn, bank)
+
+    def s(cost, R, W, fn, bank=None):
+        op("s", cost, R, W, fn, bank)
+
+    def gather(eng, lanes, R, W, fn):
+        op(eng, gath(16 * lanes), R, W, fn, line=eng)
 
     def dma(queue, R, W, o, i, dur):
         k = nd[0]
         nd[0] += 1
-        ops.append({"e": queue, "c": 0.1, "R": R, "W": W, "b": None, "lat": dur, "dsem": "d%d" % k, "key": "us",
-                    "f": (lambda q, o=o, i=i: q.dma_start(o, i))})
+        ops.append({"e": queue, "c": 0.1, "R": R, "W": W, "b": None, "lat": dur, "dsem": "d%d" % k, "key": "u" + (W or ["out"])[0],
+                    "f": (lambda q, o=o, i=i: q.dma_start(o, i)), "line": "d" + queue})
 
     def ts(out, in0, s1, o0, s2=None, o1=None):
         if o1 is None:
@@ -122,33 +127,30 @@ def build(T):
     def cp(out, a):
         return lambda q: q.tensor_copy(out, a)
 
+    def ms(out, x):
+        return lambda q: q.memset(out, x)
+
     def act(out, a, f, bias=0.0, scale=1.0):
         return lambda q: q.activation(out, a, f, bias=bias, scale=scale)
 
-    def mms(lst, first=True, last=True):
+    def scan(out, d0, d1):
+        return lambda q: q.tensor_tensor_scan(out, d0, d1, 0.0, A_.mult, A_.add)
+
+    def mm(n, R, W, lst, bank, first=True, last=True):
         def f(q):
             r = None
-            n = len(lst)
             for i, (o, a, b) in enumerate(lst):
-                r = q.matmul(o, a, b, first and i == 0, last and i == n - 1)
+                r = q.matmul(o, a, b, first and i == 0, last and i == len(lst) - 1)
             return r
-        return f
+        op("p", n * PAR["pec"], R, W, f, bank)
 
-    def mmk(lst):
-        def f(q):
-            r = None
-            for o, a, b in lst:
-                r = q.matmul(o, a, b, True, True)
-            return r
-        return f
-
-    dma("y", [], ["zi"], T.zi[:], T.z[:], 3.0)
-    dma("y", [], ["pc"], T.pc[:], T.par[:], 2.5)
-    dma("s", [], ["sgi"], T.sgi[0:8, :], T.sg[:], 2.0)
-    dma("s", [], ["si"], T.si[:], T.s0[:], 2.0)
-    dma("s", [], ["gi"], T.gi[:], T.g0[:], 2.0)
-    dma("y", [], ["tev0"], T.tev[0:64, :], T.ev[0:64, :], 6.0)
-    dma("y", [], ["tev1"], T.tev[64:128, :], T.ev[64:128, :], 6.0)
+    dma("y", [], ["pc"], T.pc[:], T.par[:], 2.3)
+    dma("s", [], ["zi"], T.zi[:], T.z[:], 2.8)
+    dma("s", [], ["liS"], T.li[:, :, 0], T.s0[:], 3.0)
+    dma("s", [], ["liG"], T.li[:, :, 1], T.g0[:], 3.0)
+    dma("s", [], ["sgi"], T.sgi[0:8, :], T.sg[:], 3.0)
+    dma("y", [], ["tev0"], T.tev[0:64, :], T.ev[0:64, :], PAR["ev"])
+    dma("s", [], ["tev1"], T.tev[64:128, :], T.ev[64:128, :], PAR["ev"])
 
     fl = True
     op("g", 0.2, [], ["pcol0"], lambda q: q.iota(T.pcol[:, 0:1], [[0, 1]], 0, 1))
@@ -157,232 +159,312 @@ def build(T):
     op("g", 0.4, [], ["itg"], lambda q: q.iota(T.itg[:], [[1, 8], [0, 16]], 0, 0, allow_small_or_imprecise_dtypes=fl))
     op("g", 0.2, [], ["it8"], lambda q: q.iota(T.it8[:], [[1, 8]], 0, 0, allow_small_or_imprecise_dtypes=fl))
     op("g", 0.3, [], ["itk"], lambda q: q.iota(T.itk[:], [[1, 8], [0, 8]], 0, 0, allow_small_or_imprecise_dtypes=fl))
-    v(small(2048), [], ["ptab%d" % d for d in range(6)], lambda q: q.memset(T.ptab[:], 0.0))
+    v(small(2048), [], ["ptab%d" % d for d in range(6)], ms(T.ptab[:], 1.0))
 
-    def icol(j, src, *a):
-        v(small(1), ["pcol%d" % src], ["pcol%d" % j], ts(T.pcol[:, j:j + 1], T.pcol[:, src:src + 1], *a))
-    icol(1, 0, 4, A_.arith_shift_right)
-    icol(2, 0, 7, A_.bitwise_and)
-    icol(3, 0, 3, A_.arith_shift_right, 1, A_.bitwise_and)
-    icol(4, 0, 1, A_.arith_shift_right)
-    icol(5, 0, 1, A_.bitwise_and)
-    icol(6, 0, 1, A_.arith_shift_right, 7, A_.bitwise_and)
-    icol(7, 0, 15, A_.bitwise_and)
-    v(small(8), ["pcol%d" % j for j in range(8)], ["fc"], cp(T.fcol[:, 0:8], T.pcol[:, 0:8]))
+    def icol(j, *a):
+        v(small(1), ["pcol0"], ["pcol%d" % j], ts(T.pcol[:, j:j + 1], T.pcol[:, 0:1], *a))
+    icol(1, 4, A_.arith_shift_right)
+    icol(2, 1, A_.arith_shift_right, 7, A_.bitwise_and)
+    icol(3, 15, A_.bitwise_and)
+    icol(4, 7, A_.bitwise_and)
+    icol(5, 3, A_.arith_shift_right, 1, A_.bitwise_and)
+    v(small(8), ["pcol%d" % j for j in range(6)], ["fc"], cp(T.fcol[:, 0:6], T.pcol[:, 0:6]))
     FC = lambda j: T.fcol[:, j:j + 1]
 
     def fcol(j, in0, s1, o0, s2=None, o1=None, dep=()):
-        v(small(1), ["fc"] + list(dep), ["fc%d" % j], ts(FC(j), in0, s1, o0, s2, o1))
-    fcol(8, FC(1), 8.0, A_.mult, FC(2), A_.add)
-    fcol(9, FC(5), -1000.0, A_.mult, FC(4), A_.add)
-    fcol(10, FC(5), 1000.0, A_.mult, FC(4), A_.add)
-    fcol(11, FC(10), -1000.0, A_.add, dep=["fc10"])
+        v(small(1), ["fc"] + ["fc%d" % x for x in dep], ["fc%d" % j], ts(FC(j), in0, s1, o0, s2, o1))
+    fcol(8, FC(1), 8.0, A_.mult, FC(4), A_.add)
+    fcol(9, FC(0), 0.5, A_.mult)
+    fcol(11, FC(0), -1.0, A_.add, 0.5, A_.mult)
     fcol(12, FC(1), 16.0, A_.mult, 16.0, A_.add)
-    fcol(13, FC(3), -1.0, A_.mult, 1.0, A_.add)
-    fcol(14, FC(7), -ALPHA, A_.mult, TOP - 64 * 16 * ALPHA, A_.add)
-    fcol(15, FC(6), 0.0, A_.is_equal)
-    fcol(16, FC(6), 1.0, A_.is_equal)
-    fcol(20, FC(6), 2.0, A_.is_equal, 2.0, A_.mult)
-    v(small(1), ["fc15", "fc16"], ["fc18"], tt(FC(18), FC(15), FC(16), A_.subtract))
-    v(small(1), ["fc15", "fc16"], ["fc19"], tt(FC(19), FC(15), FC(16), A_.add))
-    for o in range(2):
-        v(small(8), ["it8", "fc"], ["bo"], ts(T.bo[:, o], T.it8[:], FC(1), A_.is_equal, 1.0 - 2.0 * o, A_.mult))
-    for o in range(3):
-        v(small(8), ["it8", "fc", "fc%d" % (18 + o)], ["wp"], ts(T.wp[:, o], T.it8[:], FC(1), A_.is_equal, FC(18 + o), A_.mult))
-    v(small(64), [], ["cna"], lambda q: q.memset(T.cna[:, 0], 0.0))
-    v(small(64), ["itk", "fc"], ["cna"], ts(T.cna[:, 1], T.itk[:], FC(1), A_.is_equal, 2.0, A_.mult))
-    v(small(64), ["itk", "fc"], ["cnb"], ts(T.cnb[:], T.itk[:], FC(1), A_.is_equal, -512.0, A_.mult))
-    v(small(64), [], ["c128"], lambda q: q.memset(T.c128[:], 128.0))
-    v(small(64), ["itf", "fc8"], ["cg"], ts(T.cg[:], T.itf[:, 0:64], FC(8), A_.is_equal))
-    v(small(64), ["itf", "fc9"], ["ch0"], ts(T.ch0[:], T.itf[:, 0:64], FC(9), A_.is_equal))
-    v(small(64), ["itf", "fc11"], ["ch1"], ts(T.ch1[:], T.itf[:, 0:64], FC(11), A_.is_equal))
-    v(small(64), ["itf", "fc9"], ["cb0"], ts(T.cb0[:], T.itf[:, 0:64], FC(9), A_.is_equal))
-    v(small(64), ["itf", "fc11"], ["cb1"], ts(T.cb1[:], T.itf[:, 0:64], FC(11), A_.is_equal))
-    v(small(128), ["itg", "fc"], ["blk"], ts(T.blk[:], T.itg[:], FC(1), A_.is_equal))
-    v(small(128), ["itf", "fc", "pcol0"], ["idb"], ts(T.idb[:], T.itf[:, 0:128], FC(0), A_.is_equal))
-    v(small(128), ["itg", "fc"], ["r8"], ts(T.r8[:], T.itg[:], FC(0), A_.is_equal))
-    v(small(144), ["itf", "fc12"], ["w0"], ts(T.w0[:], T.itf[:], FC(12), A_.is_equal))
-    v(small(64), [], ["one"], lambda q: q.memset(T.one[:], 1.0))
-    for j, x in enumerate((11.0, 21.5, 1.5 * E11, 2.0 * E11)):
-        v(small(1), [], ["th0%d" % j], (lambda x, j: lambda q: q.memset(T.thb[:, j:j + 1], x))(x, j))
-    op("s", 0.1, ["th00"], ["warm"], act(T.fcol[:, 24:25], T.thb[:, 0:1], F_.Exp))
-    for c in "AB":
-        v(small(136), [], ["zz" + c], (lambda c: lambda q: q.memset(T["zz" + c][:], 0.0))(c))
-        v(small(136), [], ["zm" + c], (lambda c: lambda q: q.memset(T["zm" + c][:], 0.0))(c))
-        v(small(68), [], ["zk" + c], (lambda c: lambda q: q.memset(T["zk" + c][:], 0.0))(c))
+    fcol(13, FC(5), -1.0, A_.mult, 1.0, A_.add)
+    fcol(14, FC(3), -ALPHA, A_.mult, TOP, A_.add)
+    fcol(15, FC(2), 0.0, A_.is_equal, 0.5, A_.mult)
+    fcol(16, FC(2), 1.0, A_.is_equal, 2.0 ** -13, A_.mult)
+    fcol(17, FC(2), 2.0, A_.is_equal, 0.5, A_.mult)
+    fcol(18, FC(3), 6.0, A_.is_equal, -MID, A_.mult)
+    fcol(19, FC(3), 6.0, A_.is_equal, -BIG, A_.mult)
+    fcol(20, FC(17), FC(15), A_.subtract, dep=(17, 15))
+    fcol(21, FC(17), FC(16), A_.subtract, dep=(17, 16))
+    fcol(22, FC(15), FC(16), A_.add, FC(18), A_.add, dep=(15, 16, 18))
+    fcol(23, FC(17), 2.0, A_.mult, FC(18), A_.add, dep=(17, 18))
+    fcol(10, FC(22), FC(19), A_.add, dep=(22, 19))
+    fcol(24, FC(3), 0.0, A_.is_equal)
+    fcol(25, FC(3), 1.0, A_.is_equal)
+    fcol(26, FC(3), 1.0, A_.is_equal, 67.0, A_.mult)
+    fcol(27, FC(3), 0.0, A_.is_equal, 64.0, A_.mult)
+    fcol(28, FC(24), FC(25), A_.subtract, dep=(24, 25))
+    fcol(29, FC(3), 0.0, A_.is_equal, 128.0, A_.mult)
+    fcol(30, FC(3), 1.0, A_.is_equal, -1.0, A_.mult)
 
-    DI = lambda d: T.dgi[:, 256 * d:256 * d + 256]
-    DG = lambda d: T.dg[:, 256 * d:256 * d + 256]
+    def sel(name, out, src, col, w=None, dep=()):
+        R = [src.split(":")[0], "fc"] + ["fc%d" % x for x in (col,) + tuple(dep) if x > 7]
+        it = T.itf[:, 0:int(src.split(":")[1])] if ":" in src else T[src][:]
+        v(small(1), R, [name], ts(out, it, FC(col), A_.is_equal) if w is None else ts(out, it, FC(col), A_.is_equal, w, A_.mult))
+    for o in range(2):
+        sel("bo", T.bo[:, o], "it8", 1)
+    for n, cols in (("wp0", (20, 21, 22, 23)), ("wp1", (20, 21, 10))):
+        for o, col in enumerate(cols):
+            sel(n, T[n][:, :, o], "it8", 1, FC(col), (col,))
+    v(small(64), [], ["cna1"], ms(T.cna[:, 1], 0.0))
+    sel("cna", T.cna[:, 0], "itk", 1, FC(28), (28,))
+    sel("cne", T.cne[:], "itk", 1, FC(29), (29,))
+    sel("cg", T.cg[:], "itf:64", 8, -1.0)
+    for h, col in ((0, 9), (1, 11)):
+        sel("ch%d" % h, T["ch%d" % h][:], "itf:64", col)
+        sel("nh%d" % h, T["nh%d" % h][:], "itf:64", col, -1.0)
+        sel("cb%d" % h, T["cb%d" % h][:], "itf:64", col, 2.0 ** -12)
+    sel("idh", T.idh[:], "itf:128", 0)
+    sel("ndh", T.ndh[:], "itf:128", 0, -1.0)
+    sel("idb", T.idb[:], "itf:128", 0)
+    sel("blk", T.blk[:], "itg", 1)
+    sel("nbk", T.nbk[:], "itg", 1, -1.0)
+    sel("wr0", T.wr0[:], "itg", 1, FC(24), (24,))
+    sel("wr1", T.wr1[:], "itg", 1, FC(30), (30,))
+    sel("r8", T.r8[:], "itg", 0)
+    sel("w0", T.w0[:], "itf:144", 12)
+    sel("tb0", T.tbk[:], "itf:128", 0, 2.0)
+    v(small(256), ["tb0", "nbk"], ["tbk"], tt(T.tbk[:], T.tbk[:], T.nbk[:], A_.add))
+    v(small(64), ["itg", "fc24"], ["hw0"], ts(T.hw0[:], T.itg[:], 0.0, A_.mult, FC(24), A_.add))
+    s(1.4, ["fc"], ["warm"], act(T.junk[:, 0:1], FC(0), F_.Exp, 0.0, -1.0))
+    for c in "AB":
+        for n in ("zz0", "zz1", "zz2", "zc4", "zc5"):
+            v(small(68), [], [n + c], ms(T[n + c][:], 0.0))
+        v(small(96), [], ["nez" + c], ms(T["ne" + c][:], 0.0))
+        for n, k in (("d1", 3), ("dG", 3), ("dX", 2), ("dS", 2)):
+            v(small(64), [], [n + "z" + c], ms(T[n + c][:, 0::k], 0.0))
+
     for d in (4, 5, 0, 1, 2, 3):
         src, nm = (T.ti, "ti") if d > 3 else (T.pc, "pc")
-        sh = 6 * (d % 4) if d < 4 else 6 * (d - 4)
-        if sh:
-            v(small(256), [nm], ["dgi%d" % d], ts(DI(d), src[:], sh, A_.arith_shift_right, 63, A_.bitwise_and))
-        else:
-            v(small(256), [nm], ["dgi%d" % d], ts(DI(d), src[:], 63, A_.bitwise_and))
-        v(small(256), ["dgi%d" % d], ["dg%d" % d], ts(DG(d), DI(d), 0.5 if d % 2 == 0 else 32.0, A_.mult))
-        dma("y", ["dg%d" % d], ["ptab%d" % d], T.ptab[d::16, :], DG(d), 2.5)
+        DI, DG = T.dgi[:, 256 * d:256 * d + 256], T.dg[:, 256 * d:256 * d + 256]
+        v(small(256), [nm], ["dgi%d" % d], ts(DI, src[:], 63 << (6 * (d % 4)), A_.bitwise_and))
+        v(small(256), ["dgi%d" % d], ["dg%d" % d], cp(DG, DI))
+        dma("y", ["dg%d" % d], ["ptab%d" % d], T.ptab[d::16, :], DG, 2.5)
     PT = ["ptab%d" % d for d in range(6)]
     EV = ["tev0", "tev1"]
 
-    v(small(512), ["sgi"], ["sgb"], cp(T.sgb[0:8, :], T.sgi[0:8, :]))
-    op("p", 0.3, ["r8", "sgb"], ["vsl"], lambda q: q.matmul(T.vsl[:], T.r8[0:8, :], T.sgb[0:8, :], True, True), "vsl")
-    v(small(512), ["vsl"], ["sgl"], cp(T.sgl[:], T.vsl[:]), "vsl")
-    v(small(512), ["zi"], ["zf"], cp(T.zf[:], T.zi[:]))
+    v(small(512), ["sgi"], ["sgb"], ts(T.sgb[0:8, :], T.sgi[0:8, :], -MID, A_.add))
+    for ci, c in enumerate("AB"):
+        v(small(192), ["zi"], ["zo" + c], ts(T.zo[:, ci], T.zi[:, 1:4, ci], -MID, A_.add))
+        op("net", 0.4, ["zo" + c], ["zn" + c], ("z", 0, ci, T.zo[:, ci], T.zn[:, ci]), None, 8.0)
 
     def slot(t, ci):
-        return 192 * (2 * t + ci)
+        return MW * (2 * t + ci)
 
-    for t in range(NV):
+    def arrive(t, ci):
+        c = "AB"[ci]
+        B = lambda n: T[n + c]
         cur[0] = "p"
-        for ci, c in enumerate("AB"):
-            B = lambda n, c=c: T[n + c]
-            lanes = slice(L2 * ci, L2 * ci + L2)
-            tl = slice(128 * t + L2 * ci, 128 * t + L2 * ci + L2)
-            q0 = slot(t, ci)
-            IS, IG, IR = T.inm[:, q0:q0 + 64], T.inm[:, q0 + 64:q0 + 128], T.inm[:, q0 + 128:q0 + 192]
-            OX = T.oxm[:, 64 * (2 * t + ci):64 * (2 * t + ci) + 64]
-            RX = T.rxm[:, 64 * (2 * t + ci):64 * (2 * t + ci) + 64]
-            kS, kG, kR, kO = ["%s%d%s" % (n, t, c) for n in ("iS", "iG", "iR", "ox")]
-            if t == 0:
-                v(small(64), ["zi"], [kO], cp(OX, T.zi[:, tl]))
-                v(small(64), ["si"], [kS], cp(IS, T.si[:, lanes]))
-                v(small(64), ["gi"], [kG], cp(IG, T.gi[:, lanes]))
-                v(small(64), ["sgl"], ["pos" + c], cp(B("pos")[:], T.sgl[:, tl]))
+        q0 = slot(t, ci)
+        M = lambda a, w=64: T.inm[:, q0 + a:q0 + a + w]
+        kX, kM = "iX%d%s" % (t, c), "iM%d%s" % (t, c)
+        if t == 0:
+            v(small(64), ["zi"], [kX], cp(M(MX), T.zi[:, 0, ci]))
+            v(small(128), ["liS", "liG"], [kM], cp(M(MS, 128), T.li[:, ci]))
+            v(small(64), [], ["iR" + c], ms(M(MR), 0))
+        for j, (a, b) in enumerate(cuts(CUT["x"])):
+            EX, IN = B("ex")[:, 16 * a:16 * b], T.tev[:].indirect(T.inm[:, q0 + a:q0 + b])
+            if ci in XV and j == 0:
+                gather("v", b - a, EV + [kX], ["exv" + c], cp(EX, IN))
             else:
-                kX = "rx%d%s" % (t, c)
-                v(small(64), [kX], ["rxf" + c], cp(B("rxf")[:], RX))
-                v(small(128), ["rxf" + c, "zf"], ["drz" + c], tt(B("drz")[:], B("rxf")[:], T.zf[:, tl], A_.subtract))
-                v(small(64), [kR], ["om" + c], ts(B("om")[:], IR, -1.0, A_.mult, 1.0, A_.add))
-                vx = T.vsl[:, 256 * ci + 128:256 * ci + 192]
-                v(small(128), ["om" + c, "drz" + c], ["va" + c], tt(vx, B("om")[:], B("drz")[:], A_.mult), "vsl")
-                v(small(64), ["va" + c, "rxf" + c], ["xf" + c], tt(B("xf")[:], B("rxf")[:], vx, A_.subtract), "vsl")
-                v(small(64), ["xf" + c], [kO], cp(OX, B("xf")[:]))
-                v(small(128), ["om" + c, "sgl"], ["pos" + c], tt(B("pos")[:], B("om")[:], T.sgl[:, tl], A_.mult))
-            if t < NV - 1:
-                op("net", 1.2, [kO], ["rx%d%s" % (t + 1, c)], ("x", t + 1, ci, OX), None, 6.0)
-            op("s", gath(512), EV + [kO], ["exs" + c], act(B("ex")[:, 512:1024], T.tev[:].indirect(OX[:, 32:64]), F_.Copy))
-            if ci in XV:
-                v(gath(512), EV + [kO], ["exv" + c], cp(B("ex")[:, 0:512], T.tev[:].indirect(OX[:, 0:32])))
-            else:
-                op("s", gath(512), EV + [kO], ["exv" + c], act(B("ex")[:, 0:512], T.tev[:].indirect(OX[:, 0:32]), F_.Copy))
-            v(small(64), [kS], ["Sf" + c], cp(B("sgf")[:, 0:64], IS))
-            v(small(64), [kG], ["Gf" + c], cp(B("sgf")[:, 64:128], IG))
-            for h in range(2):
-                op("s", 0.07, ["pos" + c], ["nq" + c], act(B("nq")[:, :, h], B("pos")[:], F_.Copy, 2.0, -1.0))
-                v(small(64), [kG, "fc13"], ["pg" + c], ts(B("pg")[:, :, h], IG, FC(13) if h == 0 else FC(3), A_.mult))
-            op("s", 0.07, ["pos" + c], ["p2" + c], act(B("p2")[:], B("pos")[:], F_.Copy, 0.0, 2.0))
-            op("p", 384 * PEC, ["pg" + c, "cg", "nq" + c, "cnb", "one", "c128"], ["gE" + c],
-               mms([(B("pa")[:, 3], B("pg")[:], T.cg[:]), (B("pa")[:, 3], B("nq")[:], T.cnb[:]), (B("pa")[:, 3], T.one[:], T.c128[:])]), "pa" + c)
+                gather("s", b - a, EV + [kX], ["ex" + "vs"[j > 0] + c], act(EX, IN, F_.Copy))
+        v(small(128), [kX, kM, "iR" + c], ["mh" + c], ts(B("mh")[:], M(0, MW), -MID, A_.add))
+        for h in range(2):
+            v(small(64), [kM, "fc", "fc13"], ["pg" + c], ts(B("pg")[:, :, h], M(MG), -MID, A_.add, FC(13) if h == 0 else FC(5), A_.mult))
+        lo = 128 * t + L2 * ci
+        mm(128, ["sgb", "r8", "ndh", "mh" + c], ["y" + c],
+           [(B("fz")[:, 0], T.r8[0:8, :], T.sgb[0:8, lo:lo + L2]), (B("fz")[:, 0], T.ndh[:], B("mh")[:, MR:MR + 64])], "fz" + c)
+
+    def threshold(t):
+        cur[0] = "p"
+        bias, kb = FC(26), "fc26"
         if t > 0:
-            op("p", 0.1, ["omA", "omB", "one"], ["par"],
-               mms([(T.trA[:, 320:384], T.one[:], T.omA[:]), (T.trA[:, 320:384], T.one[:], T.omB[:])]), "trA")
-            v(small(64), ["par"], ["cnt"], lambda q, t=t: q.tensor_reduce(T.cnt[:, t:t + 1], T.trA[:, 320:384], AxisListType.X, A_.add), "trA")
+            bias, kb = T.cnt[:, 4 + t:5 + t], "th"
+            mm(128, ["hw0", "mhA", "mhB"], ["par"],
+               [(T.fzB[:, 2], T.hw0[:], T.mhA[:, MR:MR + 64]), (T.fzB[:, 2], T.hw0[:], T.mhB[:, MR:MR + 64])], "fzB")
+            s(small(64) + 0.02, ["par"], ["cnt"],
+              lambda q: q.activation(T.junk[:], T.fzB[:, 2], F_.Copy, bias=16 * MID, accum_out=T.cnt[:, t:t + 1]), "fzB")
             v(small(1), ["cnt"], ["cni"], cp(T.cni[:, t:t + 1], T.cnt[:, t:t + 1]))
-            v(small(1), ["cni"], ["cnj"], ts(T.cni[:, 8 + t:9 + t], T.cni[:, t:t + 1], 16, A_.bitwise_and))
-            TB = lambda j, t=t: T.thb[:, 4 * t + j:4 * t + j + 1]
-            for j, (m, b) in ((1, (-0.0625, 21.5)), (0, (0.0625, 11.0))):
-                v(small(1), ["cnj"], ["th%d%d" % (t, j)], ts(TB(j), T.cni[:, 8 + t:9 + t], m, A_.mult, b, A_.add))
-            for j, m in ((2, 1.5), (3, 2.0)):
-                k = "th%d%d" % (t, j)
-                v(small(1), ["cnj"], [k], ts(TB(j), T.cni[:, 8 + t:9 + t], -m * E11 / 16, A_.mult, m * E11, A_.add))
-                v(small(1), [k], [k], ts(TB(j), TB(j), m * E12, A_.max))
-        TH = lambda j, t=t: T.thb[:, 4 * t + j:4 * t + j + 1]
-        for i in range(STEPS):
-            cur[0] = str(i)
-            for ci, c in enumerate("AB"):
-                B = lambda n, c=c: T[n + c]
-                q0 = slot(t, ci)
-                off, kF = (T.inm[:, q0:q0 + 64], "iS%d%s" % (t, c)) if i == 0 else (B("off"), "off" + c)
-                for a, b in cuts(CUT_P0 if i == 0 else CUT_P):
-                    op("s", gath(16 * (b - a)), PT + [kF], ["gp" + c],
-                       act(B("gp")[:, 16 * a:16 * b], T.ptab[:].indirect(off[:, a:b]), F_.Copy))
-                for a, b in cuts((CUT_A, CUT_B)[ci]):
-                    v(gath(16 * (b - a)), EV + [kF, "exs" + c, "exv" + c], ["ge" + c],
-                      tt(B("ge")[:, 16 * a:16 * b], T.tev[:].indirect(off[:, a:b]), B("ex")[:, 16 * a:16 * b], A_.is_ge))
-                op("p", 512 * PEC, ["gp" + c, "wp"], ["pa" + c],
-                   mmk([(B("pa")[:, 0:3, :, k], B("gp")[:, k::8], T.wp[:]) for k in range(8)]), "pa" + c)
-                op("p", 128 * PEC, ["nq" + c, "cna"], ["cw" + c], mms([(B("cv")[:, 0:2], B("nq")[:], T.cna[:])], True, False), "cv" + c)
-                op("p", 512 * PEC, ["cw" + c, "ge" + c, "bo"], ["cv" + c],
-                   mms([(B("cv")[:, 0:2, :, k], B("ge")[:, k::8], T.bo[:]) for k in range(8)], False, True), "cv" + c)
-                op("s", 0.08, ["cv" + c], ["cz0" + c], act(B("cz")[:, 0], B("cv")[:, 0], F_.Sign, -7.5), "cv" + c)
-                op("s", 0.08, ["cv" + c, "th%d1" % t], ["cz1" + c], act(B("cz")[:, 1], B("cv")[:, 1], F_.Sign, TH(1), -1.0), "cv" + c)
-                VE, VD = T.vsl[:, 256 * ci:256 * ci + 64], T.vsl[:, 256 * ci + 64:256 * ci + 128]
-                v(small(64), ["cz0" + c, "pa" + c], ["tu" + c], tt(B("tu")[:], B("cz")[:, 0], B("pa")[:, 0], A_.mult), "pa" + c)
-                NX, MV = B("zz")[:, 1::2, :], B("zm")[:, 1::2, :]
-                v(small(64), ["tu" + c, "pa" + c], ["zz" + c], tt(NX, B("tu")[:], B("pa")[:, 1], A_.add), "pa" + c)
-                op("p", 512 * PEC, ["zz" + c, "ch0", "ch1"], ["aN" + c],
-                   mms([(B("tr")[:, 0:64], B("zz")[:, 1:17, :], T.ch0[:]), (B("tr")[:, 0:64], B("zz")[:, 0:16, :], T.ch1[:])], True, False), "tr" + c)
-                v(small(64), ["zz" + c, "gE" + c], ["ve" + c], tt(VE, NX, B("pa")[:, 3], A_.is_equal), "pa" + c)
-                v(small(64), ["zz" + c, "pa" + c], ["vd" + c], tt(VD, B("pa")[:, 2], NX, A_.subtract), "pa" + c)
-                v(small(64), ["ve" + c, "cz1" + c], ["mx" + c], tt(B("mx")[:], B("cz")[:, 1], VE, A_.max))
-                v(small(64), ["mx" + c, "vd" + c], ["zm" + c], tt(MV, B("mx")[:], VD, A_.mult))
-                if i == STEPS - 1:
-                    v(small(64), ["mx" + c, "cv" + c], ["zk" + c], tt(B("zk")[:, 1::2, :], B("mx")[:], B("cv")[:, 1], A_.mult), "cv" + c)
-                op("p", 512 * PEC, ["zm" + c, "aN" + c, "ch0", "ch1"], ["aL" + c],
-                   mms([(B("tr")[:, 0:64], B("zm")[:, 1:17, :], T.ch0[:]), (B("tr")[:, 0:64], B("zm")[:, 0:16, :], T.ch1[:])], False, True), "tr" + c)
-                if i < STEPS - 1:
-                    v(small(64), ["aL" + c], ["off" + c], cp(B("off")[:], B("tr")[:, 0:64]), "tr" + c)
-            if i == 0:
-                cur[0] = "g"
-                for ci, c in enumerate("AB"):
-                    B = lambda n, c=c: T[n + c]
-                    q0 = slot(t, ci) + 64
-                    for a, b in cuts(CUT_G):
-                        v(gath(16 * (b - a)), EV + ["iG%d%s" % (t, c), "exs" + c, "exv" + c], ["gg" + c],
-                          tt(B("gg")[:, 16 * a:16 * b], T.tev[:].indirect(T.inm[:, q0 + a:q0 + b]), B("ex")[:, 16 * a:16 * b], A_.is_ge))
-                    CG, FM = T.gl[:, 128 * ci:128 * ci + 64], T.gl[:, 128 * ci + 64:128 * ci + 128]
-                    op("p", 1024 * PEC, ["gg" + c, "w0"], ["cG" + c],
-                       mms([(CG, T.w0[:, 16 - k:144 - k], B("gg")[:, k::16]) for k in range(16)]), "gl")
-                    v(small(64), ["cG" + c, "th%d0" % t], ["mi" + c], ts(B("mi")[:], CG, TH(0), A_.is_lt), "gl")
-                    op("p", 0.1, ["mi" + c, "p2" + c, "blk"], ["fm" + c],
-                       mms([(FM, T.blk[:], B("mi")[:]), (FM, T.blk[:], B("p2")[:])]), "gl")
-                    v(small(64), ["fm" + c], ["fu" + c], ts(B("fu")[:], FM, 0.0, A_.is_equal), "gl")
-                    v(small(64), ["fm" + c], ["pu" + c], ts(B("pu")[:], FM, 36.0, A_.is_gt), "gl")
-                    v(small(64), ["fm" + c], ["nf" + c], ts(B("nf")[:], FM, 0.0, A_.is_gt, -64.0, A_.mult), "gl")
-        cur[0] = "f"
-        for ci, c in enumerate("AB"):
-            B = lambda n, c=c: T[n + c]
-            bk, bg = "tr" + c, "gl"
-            KL, MM, AL = T.gl[:, 256 + 128 * ci:320 + 128 * ci], T.gl[:, 320 + 128 * ci:384 + 128 * ci], B("tr")[:, 0:64]
-            va, vb, vm = [T.vsl[:, 256 * ci + 64 * j:256 * ci + 64 * j + 64] for j in (2, 3, 0)]
-            Sf, Gf = B("sgf")[:, 0:64], B("sgf")[:, 64:128]
-            so = T.som[:, slot(t, ci):slot(t, ci) + 192]
-            kM = "so%d%s" % (t, c)
-            op("p", 0.15, ["zk" + c, "nf" + c, "cb0", "cb1", "idb"], ["kL" + c],
-               mms([(KL, B("zk")[:, 1:17, :], T.cb0[:]), (KL, B("zk")[:, 0:16, :], T.cb1[:]), (KL, T.idb[:], B("nf")[:])]), bg)
-            op("s", 0.08, ["kL" + c, "fc14"], ["ww" + c], act(B("ww")[:], KL, F_.Exp, FC(14), 16 * ALPHA), bg)
-            op("p", 0.1, ["ww" + c, "blk"], ["MM" + c], mms([(MM, T.blk[:], B("ww")[:])]), bg)
-            v(small(64), ["MM" + c, "th%d2" % t], ["ve" + c], ts(vm, MM, 0.5, A_.mult, TH(2), A_.max), bg)
-            if t < NV - 1:
-                v(small(64), ["MM" + c, "th%d3" % t], ["nc" + c], ts(B("nc")[:], MM, TH(3), A_.is_lt), bg)
-            v(small(64), ["aL" + c, "Sf" + c], ["va" + c], tt(va, AL, Sf, A_.subtract), bk)
-            v(small(64), ["va" + c, "pos" + c], ["va" + c], tt(va, B("pos")[:], va, A_.mult))
-            v(small(64), ["va" + c, "Sf" + c], ["stS" + c], tt(B("st")[:, 0:64], Sf, va, A_.add))
-            v(small(64), ["stS" + c], [kM + "S"], cp(so[:, 0:64], B("st")[:, 0:64]))
-            v(small(64), ["aL" + c, "Gf" + c], ["vb" + c], tt(vb, AL, Gf, A_.subtract), bk)
-            vp = T.vsl[:, 256 * ci + 64:256 * ci + 128]
-            v(small(64), ["vb" + c, "pu" + c], ["vd" + c], tt(vp, B("pu")[:], vb, A_.mult))
-            v(small(64), ["vd" + c, "Gf" + c], ["upd" + c], tt(B("upd")[:], Gf, vp, A_.add))
-            v(small(64), ["ve" + c, "ww" + c], ["hit" + c], tt(B("hit")[:], B("ww")[:], vm, A_.is_gt))
-            if t < NV - 1:
-                v(small(128), ["nc" + c, "fu" + c], ["stR" + c], tt(B("st")[:, 128:192], B("nc")[:], B("fu")[:], A_.mult))
-            v(small(64), ["hit" + c, "vb" + c], ["vb" + c], tt(vb, B("hit")[:], vb, A_.mult))
-            v(small(64), ["vb" + c, "upd" + c], ["stG" + c], tt(B("st")[:, 64:128], B("upd")[:], vb, A_.add))
-            nw = 192 if t < NV - 1 else 128
-            v(small(nw - 64), ["stG" + c] + (["stR" + c] if t < NV - 1 else []), [kM], cp(so[:, 64:nw], B("st")[:, 64:nw]))
-            op("net", 1.2, [kM, kM + "S"], ["%s%d%s" % (n, t + 1, c) for n in ("iS", "iG", "iR")],
-               ("m", t + 1, ci, so[:, 0:nw]), None, 6.0)
-    for ci, c in enumerate("AB"):
-        q0 = slot(NV, ci)
+            v(small(1), ["cni"], ["cnj"], ts(T.cni[:, 8 + t:9 + t], T.cni[:, t:t + 1], 1, A_.bitwise_and))
+            v(small(1), ["cnj", "fc25", "fc26"], ["th"], ts(bias, T.cni[:, 8 + t:9 + t], FC(25), A_.mult, FC(26), A_.add))
+        for c in "AB":
+            s(small(64), ["y" + c, "dSz" + c], ["dS" + c], act(T["dS" + c][:, 1::2], T["fz" + c][:, 0], F_.Sign, -0.5), "fz" + c)
+            for h in range(2):
+                s(small(64), ["y" + c, kb, "fc27"], ["pq" + c], act(T["pq" + c][:, :, h], T["fz" + c][:, 0], F_.Relu, bias, FC(27)), "fz" + c)
+
+    def bounds(t, ci, part):
+        c = "AB"[ci]
+        B = lambda n: T[n + c]
+        cur[0] = "g"
+        q0 = slot(t, ci) + MG
+        if part == 0:
+            for a, b in cuts(CUT["g"]):
+                gather("v", b - a, EV + ["iM%d%s" % (t, c), "exs" + c, "exv" + c], ["gg" + c],
+                       tt(B("gg")[:, 16 * a:16 * b], T.tev[:].indirect(T.inm[:, q0 + a:q0 + b]), B("ex")[:, 16 * a:16 * b], A_.is_ge))
+            return
+        CG, FM = B("fz")[:, 1], B("fz")[:, 2]
+        for j in range(4):
+            mm(256, ["gg" + c, "w0"], ["cG%d%s" % (j, c)],
+               [(CG, T.w0[:, 16 - k:144 - k], B("gg")[:, k::16]) for k in range(4 * j, 4 * j + 4)], "fz" + c, j == 0, False)
+        mm(64, ["wr1", "pq" + c], ["cG" + c], [(CG, T.wr1[:], B("pq")[:, :, 0])], "fz" + c, False, True)
+        s(small(64), ["cG" + c], ["mi" + c], act(B("mi")[:], CG, F_.Sign, -56.5, -1.0), "fz" + c)
+        mm(128, ["mi" + c, "pq" + c, "blk", "wr0"], ["fm" + c], [(FM, T.wr0[:], B("pq")[:, :, 0]), (FM, T.blk[:], B("mi")[:])], "fz" + c)
+        s(small(64), ["fm" + c], ["nf" + c], act(B("nf")[:], FM, F_.Relu, 15.0 / 256, 1.0 / 256), "fz" + c)
+        s(small(64), ["fm" + c], ["pu" + c], act(B("pu")[:], FM, F_.Relu, -57.0), "fz" + c)
+
+    def back(i, c, out, u="ch"):
+        ZZ = T["zz%d%s" % (i % 3, c)]
+        return [(out, ZZ[:, 1:17], T[u + "0"][:]), (out, ZZ[:, 0:16], T[u + "1"][:])]
+
+    def gathers(t, i, ci):
+        c = "AB"[ci]
+        B = lambda n: T[n + c]
+        cur[0] = str(i)
+        q0 = slot(t, ci) + MS
+        off, kF = (T.inm[:, q0:q0 + 64], "iM%d%s" % (t, c)) if i == 0 else (B("off"), "off" + c)
+        for a, b in cuts(CUT["s0" if i == 0 else "s"]):
+            gather("s", b - a, PT + [kF], ["gp" + c], act(B("gp")[:, 16 * a:16 * b], T.ptab[:].indirect(off[:, a:b]), F_.Copy))
+        for a, b in cuts(CUT["v0" if i == 0 else "v"]):
+            gather("v", b - a, EV + [kF, "exs" + c, "exv" + c], ["ge" + c],
+                   tt(B("ge")[:, 16 * a:16 * b], T.tev[:].indirect(off[:, a:b]), B("ex")[:, 16 * a:16 * b], A_.is_ge))
+
+    def step(t, i, ci):
+        c = "AB"[ci]
+        B = lambda n: T[n + c]
+        cur[0] = str(i)
+        kz = lambda j: "zz%d%s" % (j % 3, c)
+        ZZ, X, E = T[kz(i)][:, 1::2], B("cv")[:, 0:2], B("cv")[:, 2]
+        pre = [(X, B("pq")[:], T.cna[:])]
+        cov = [(X[:, :, :, k], B("ge")[:, k::8], T.bo[:]) for k in range(8)]
+        nf, wp = (3, "wp1") if i else (4, "wp0")
+        if PF:
+            PX = lambda f: B("pa")[:, f:192:3] if f < 3 else B("pa")[:, 192:256]
+            par = [(PX(f)[:, k::8], B("gp")[:, k::8], T[wp][:, :, f]) for k in range(8) for f in range(nf)]
+        else:
+            PX = lambda f: B("pa")[:, 0, :, :, f]
+            par = [(B("pa")[:, 0, :, k, 0:nf], B("gp")[:, k::8], T[wp][:]) for k in range(8)]
+        if i == 0:
+            mm(64 * len(par), ["gp" + c, wp], ["pa" + c], par, "pa" + c)
+            mm(512, ["ge" + c, "bo"], ["cw" + c], cov, "cv" + c, True, False)
+            mm(128, ["pq" + c, "cna", "cna1"], ["cv" + c], pre, "cv" + c, False, True)
+        else:
+            ka, AP = ("a0" + c, B("a0")[:]) if i == 1 else (kz(i - 2), T[kz(i - 2)][:, 1::2])
+            NE = B("ne")[:, 2::3]
+            mm(192 if PF else 320, [ka, "ne" + c, "idh", "ndh"], ["pw" + c],
+               [(PX(3), T.idh[:], AP), (PX(3), T.ndh[:], NE),
+                (PX(2), T.idh[:], NE) if PF else (B("pa")[:, 0, :, :, 0:3], T.idh[:], B("ne")[:])], "pa" + c, True, False)
+            mm(64 * len(par), ["gp" + c, wp], ["pa" + c], par, "pa" + c, False, True)
+            mm(128, ["pq" + c, "cna", "cna1"], ["cw" + c], pre, "cv" + c, True, False)
+            mm(512, ["ge" + c, "bo"], ["cv" + c], cov, "cv" + c, False, True)
+        if not PF:
+            s(small(192), ["pa" + c], ["va" + c], act(B("va")[:], B("pa")[:, 0, :, :, 0:3], F_.Copy), "pa" + c)
         for j in range(2):
-            v(small(64), ["iS4" + c], ["yo%d%s" % (j, c)], cp(T.yo[:, 128 * j + 64 * ci:128 * j + 64 * ci + 64], T.inm[:, q0 + 64 * j:q0 + 64 * j + 64]))
-            dma("ys"[j], ["yo%d%s" % (j, c)], [], (T.ys, T.yg)[j][:, 64 * ci:64 * ci + 64], T.yo[:, 128 * j + 64 * ci:128 * j + 64 * ci + 64], 2.0)
+            s(small(64), ["cv" + c, "d1z" + c], ["d1" + c], act(B("d1")[:, 1 + j::3], X[:, j], F_.Sign, -7.5), "cv" + c)
+        if i >= STEPS - 2:
+            s(small(64), ["cv" + c], ["zc%d%s" % (i, c)], act(B("zc%d" % i)[:, 1::2], X[:, 0], F_.Copy, 68.0), "cv" + c)
+        if PF:
+            v(small(192), ["d1" + c, "pa" + c], ["nx" + c], scan(B("nx")[:], B("d1")[:], B("pa")[:, 0:192]), "pa" + c)
+        else:
+            v(small(192), ["d1" + c, "va" + c], ["nx" + c], scan(B("nx")[:], B("d1")[:], B("va")[:]))
+        if i == 0:
+            v(small(64), ["nx" + c], [kz(i)], cp(ZZ, B("nx")[:, 2::3]))
+            v(small(64), ["pa" + c], ["a0" + c], cp(B("a0")[:], PX(3)), "pa" + c)
+        else:
+            v(small(64), ["nx" + c, "pa" + c], [kz(i)], tt(ZZ, B("nx")[:, 2::3], PX(3), A_.max), "pa" + c)
+        if i < STEPS - 1:
+            mm(128, [kz(i), "ch0", "ch1"], ["aL" + c], back(i, c, B("tr")[:, 0:64]), "tr" + c)
+            v(small(64), ["aL" + c], ["off" + c], ts(B("off")[:], B("tr")[:, 0:64], MID, A_.add), "tr" + c)
+            mm(192, [kz(i), "idh", "pg" + c, "cg", "pq" + c, "cne"], ["e" + c],
+               [(E, B("pg")[:], T.cg[:]), (E, B("pq")[:], T.cne[:]), (E, T.idh[:], ZZ)], "cv" + c)
+            v(small(64), ["e" + c, "nez" + c], ["ne" + c], ts(B("ne")[:, 2::3], E, 0.0, A_.not_equal, BIG, A_.mult), "cv" + c)
+        F = lambda j: B("tr")[:, 64 + j:256:3] if j < 3 else B("tr")[:, 253 + j:384:2] if j < 5 else B("tr")[:, 379 + j:512:2]
+        MH = lambda a: B("mh")[:, a:a + 64]
+        if i == STEPS - 2:
+            lst = back(i, c, F(0), "nh") + back(i, c, F(2)) \
+                + [(F(1), T.ndh[:], MH(MG)), (F(2), T.idh[:], MH(MG)), (F(5), T.ndh[:], MH(MS)), (F(6), T.idh[:], MH(MS))]
+            if t < NV - 1:
+                ZN = T.zn[:, ci, 64 * t:64 * t + 64]
+                lst += [(F(3), T.ndh[:], MH(MX)), (F(4), T.idh[:], MH(MX)), (F(3), T.idh[:], ZN), (F(4), T.idh[:], ZN)]
+            for j in range(0, len(lst), 4):
+                mm(256, [kz(i), "nh0", "nh1", "mh" + c, "zn" + c], ["fw" + c], lst[j:j + 4], "tr" + c, j == 0, False)
+        if i == STEPS - 1:
+            mm(256, [kz(i)], ["fv" + c], back(i, c, F(5)) + back(i, c, F(6)), "tr" + c, False, False)
+            mm(256, [kz(i)], ["fv" + c], back(i, c, F(0)) + back(i, c, F(1)), "tr" + c, False, True)
+
+    def weight(i, ci):
+        c = "AB"[ci]
+        B = lambda n: T[n + c]
+        cur[0] = "w"
+        Z, ww, ZC = B("fz")[:, i - 1], "w%d" % i, B("zc%d" % i)
+        mm(256, ["zc%d%s" % (i, c), "cb0", "cb1", "nf" + c, "idb", "ndh", "mh" + c], ["zw" + c],
+           [(Z, T.ndh[:], B("mh")[:, MG:MG + 64]), (Z, T.idb[:], B("nf")[:]), (Z, ZC[:, 1:17], T.cb0[:]), (Z, ZC[:, 0:16], T.cb1[:])],
+           "fz" + c, True, False)
+        mm(128, ["zz%d%s" % (i % 3, c), "ch0", "ch1"], ["Z" + c], back(i, c, Z), "fz" + c, False, True)
+        s(small(64), ["Z" + c], ["ab" + c], act(B("ab")[:], Z, F_.Abs), "fz" + c)
+        s(small(64), ["ab" + c, "fc14"], [ww + c], act(B(ww)[:], B("ab")[:], F_.Exp, FC(14), -ALPHA * GAP * 4096))
+
+    def finish(t, ci):
+        c = "AB"[ci]
+        B = lambda n: T[n + c]
+        cur[0] = "f"
+        D4, D45, RD = B("cv")[:, 3], B("cv")[:, 4], B("cv")[:, 5]
+        more = t < NV - 1
+        lst = [(D4, T.idb[:], B("pu")[:]), (D45, T.idb[:], B("pu")[:]), (D4, T.tbk[:], B("w4")[:]), (D45, T.tbk[:], B("w4")[:])]
+        if more:
+            lst += [(RD, T.idb[:], B("nf")[:]), (RD, T.blk[:], B("w4")[:])]
+        mm(64 * len(lst), ["pu" + c, "nf" + c, "w4" + c, "tbk"], ["dw" + c], lst, "cv" + c, True, False)
+        lst = [(D4, T.nbk[:], B("w5")[:]), (D45, T.tbk[:], B("w5")[:])] + ([(RD, T.blk[:], B("w5")[:])] if more else [])
+        mm(64 * len(lst), ["w5" + c], ["D" + c], lst, "cv" + c, False, True)
+        so = lambda a: T.som[:, slot(t, ci) + a:slot(t, ci) + a + 64]
+        kM = "so%d%s" % (t, c)
+        v(small(128), ["dS" + c, "fv" + c], ["oS" + c], scan(B("oS")[:], B("dS")[:], B("tr")[:, 384:512]), "tr" + c)
+        v(small(64), ["oS" + c], [kM + "S"], ts(so(MS), B("oS")[:, 1::2], 0.5, A_.mult, MID, A_.add))
+        for j, D in enumerate((D4, D45)):
+            s(small(64), ["D" + c, "dGz" + c], ["dG" + c], act(B("dG")[:, 1 + j::3], D, F_.Sign, -TAU), "cv" + c)
+        v(small(192), ["dG" + c, "fv" + c], ["oG" + c], scan(B("oG")[:], B("dG")[:], B("tr")[:, 64:256]), "tr" + c)
+        v(small(64), ["oG" + c], [kM + "G"], ts(so(MG), B("oG")[:, 2::3], 0.5, A_.mult, MID, A_.add))
+        R = [kM + "S", kM + "G"]
+        if more:
+            s(small(64), ["D" + c, "dXz" + c], ["dX" + c], act(B("dX")[:, 1::2], RD, F_.Sign, -TAU), "cv" + c)
+            v(small(128), ["dX" + c, "fv" + c], ["oX" + c], scan(B("oX")[:], B("dX")[:], B("tr")[:, 256:384]), "tr" + c)
+            v(small(64), ["dX" + c], [kM + "R"], ts(so(MR), B("dX")[:, 1::2], 0.0, A_.is_lt))
+            v(small(64), ["oX" + c], [kM + "X"], ts(so(MX), B("oX")[:, 1::2], 0.5, A_.mult, MID, A_.add))
+            R += [kM + "X", kM + "R"]
+        a, w = span(t + 1, ci)
+        op("net", 0.4, R, ["iX%d%s" % (t + 1, c), "iM%d%s" % (t + 1, c), "iR" + c],
+           ("m", t + 1, ci, T.som[:, a - 2 * MW:a - 2 * MW + w], T.inm[:, a:a + w]), None, PAR["net"])
+
+    late = OPT["late"]
+    for t in range(NV):
+        arrive(t, 0)
+        gathers(t, 0, 0)
+        bounds(t, 0, 0)
+        arrive(t, 1)
+        threshold(t)
+        for i in range(STEPS):
+            for ci in range(NC):
+                if (i, ci) == (late, 1):
+                    bounds(t, 1, 0)
+                if (i, ci) != (0, 0):
+                    gathers(t, i, ci)
+                step(t, i, ci)
+                if i == (late if ci else 0):
+                    bounds(t, ci, 1)
+                for j in (STEPS - 2, STEPS - 1):
+                    if i == max(j, late if ci else 0):
+                        weight(j, ci)
+                if i == STEPS - 1:
+                    finish(t, ci)
+    for ci, c in enumerate("AB"):
+        q0 = slot(NV, ci) + MS
+        v(small(128), ["iM4" + c], ["yo" + c], cp(T.yo[:, 128 * ci:128 * ci + 128], T.inm[:, q0:q0 + 128]))
+        for j in range(2):
+            dma("ys"[j], ["yo" + c], [], (T.ys, T.yg)[j][:, 64 * ci:64 * ci + 64], T.yo[:, 128 * ci + 64 * j:128 * ci + 64 * j + 64], 2.0)
     return ops
 
 
 def link(ops):
-    wr, rd, base, bank = {}, {}, {}, {}
+    wr, rd, base, bank, line = {}, {}, {}, {}, {}
     for n, o in enumerate(ops):
         d = set()
         for k in o["R"]:
@@ -397,10 +479,15 @@ def link(ops):
                 wr[k] = [n]
                 rd[k] = []
             d.update(base[k])
+        o["O"] = [line[o["line"]]] if o["line"] in line else []
+        if o["line"]:
+            line[o["line"]] = n
         if o["b"]:
             sg = bank.get(o["b"])
             if not sg or sg["e"] != o["e"]:
                 sg = bank[o["b"]] = {"e": o["e"], "n": [], "pre": set(sg["n"]) if sg else set()}
+            elif o["e"] == "p":
+                d.add(sg["n"][-1])
             d.update(sg["pre"])
             sg["n"].append(n)
         d.discard(n)
@@ -412,82 +499,92 @@ def link(ops):
 
 
 def order(ops):
-    n = len(ops)
+    n, LAT = len(ops), PAR["lat"]
     suc = [[] for _ in ops]
     pri = [0.0] * n
-    need = [len(o["D"]) for o in ops]
+    need = [len(o["D"]) + len(o["O"]) for o in ops]
     for i, o in enumerate(ops):
         for d in o["D"]:
-            suc[d].append(i)
+            suc[d].append((i, ops[d]["lat"] + (0.0 if ops[d]["e"] == o["e"] == "p" else LAT)))
+        for d in o["O"]:
+            suc[d].append((i, 0.0))
     for i in range(n - 1, -1, -1):
-        o = ops[i]
-        pri[i] = o["c"] + o["lat"] + LAT + max([pri[j] for j in suc[i]] or [0.0])
+        pri[i] = ops[i]["c"] + max([pri[j] + gap for j, gap in suc[i]] or [ops[i]["lat"]])
     for i in range(n):
-        pri[i] += SHIFT.get(ops[i]["key"], 0.0)
-    free, ready, est, done, seq = {}, [], [0.0] * n, [0.0] * n, []
+        pri[i] += SHIFT.get(ops[i]["key"], 0.0) - (100.0 if ops[i]["line"] in ("v", "s") else 0.0)
+    free, est, seq = {}, [0.0] * n, []
     ready = [i for i in range(n) if not need[i]]
     q = lambda e: "g" if e == "net" else e
     while ready:
-        tm = min(max(est[i], free.get(q(ops[i]["e"]), 0.0)) for i in ready)
         first = min((max(est[i], free.get(q(ops[i]["e"]), 0.0)), -pri[i], i) for i in ready)
-        eng = q(ops[first[2]]["e"])
-        cand = [i for i in ready if q(ops[i]["e"]) == eng and max(est[i], free.get(eng, 0.0)) <= tm + 0.02]
+        tm, eng = first[0], q(ops[first[2]]["e"])
+        cand = [i for i in ready if q(ops[i]["e"]) == eng and max(est[i], free.get(eng, 0.0)) <= tm + PAR.get("eps", 0.02)]
         b = max(cand, key=lambda i: (pri[i], -i))
-        s = max(est[b], free.get(eng, 0.0))
-        free[eng] = s + ops[b]["c"]
-        done[b] = s + ops[b]["c"] + ops[b]["lat"]
+        free[eng] = max(est[b], free.get(eng, 0.0)) + ops[b]["c"]
         ready.remove(b)
         seq.append(b)
-        for j in suc[b]:
+        for j, gap in suc[b]:
             need[j] -= 1
-            est[j] = max(est[j], done[b] + LAT)
+            est[j] = max(est[j], free[eng] + gap)
             if not need[j]:
                 ready.append(j)
     return seq
 
 
-def emit(g, core, T, topo, ops, seq, nxt, home):
+def peer(T, rank, kind, t, sign):
+    step = -1 if kind == "z" else (1 if t < NV else 1 - NV)
+    return T.cores[(rank + sign * step) % len(T.cores)]
+
+
+def name(kind, t, ci):
+    return "zar" + "AB"[ci] if kind == "z" else "arr%d%s" % (t, "AB"[ci])
+
+
+def emit(g, core, T, topo, ops, seq):
     qs = {"v": g.vector, "s": g.scalar, "p": g.tensor, "g": g, "net": g, "y": g.sync}
     cs = {"v": "v", "s": "s", "p": "p", "g": "q"}
     known = {e: {} for e in "vspgy"}
     count = {}
     loc = 0
+    rank = T.rank_of(core)
     for n in seq:
         o = ops[n]
         e = "g" if o["e"] == "net" else o["e"]
         q, kn = qs[e], known[e]
+        need = {}
         for d in o["D"]:
-            for sem, val, clk in ops[d]["sig"]:
-                if kn.get(sem, 0) < val:
-                    q.wait_ge(T.sem[sem], val)
-                    kn[sem] = val
-                    for k2, v2 in clk.items():
-                        if kn.get(k2, 0) < v2:
-                            kn[k2] = v2
+            if e == "p" and ops[d]["e"] == "p":
+                continue
+            sem, val, clk = ops[d]["sig"]
+            if val > need.get(sem, (0, None))[0]:
+                need[sem] = (val, clk)
+        for sem, (val, clk) in sorted(need.items(), key=lambda x: -len(x[1][1])):
+            if kn.get(sem, 0) < val:
+                q.wait_ge(T.sem[sem], val)
+                kn[sem] = val
+                for k2, v2 in clk.items():
+                    if kn.get(k2, 0) < v2:
+                        kn[k2] = v2
         if o["e"] == "net":
-            kind, t, ci, src = o["f"]
-            dst = home if t == NV else nxt
+            kind, t, ci, src, land = o["f"]
+            dst, frm = peer(T, rank, kind, t, 1), peer(T, rank, kind, t, -1)
             via = routes(core, dst, topo)[ci]
             to = dst if via == core else via
-            sem = ("arr%d%s" if kind == "m" else "xar%d%s") % (t, "AB"[ci])
-            wide = 192 if kind == "m" else 64
-            w = 128 if kind == "m" and t == NV else wide
-            at = wide * (2 * t + ci)
-            land = (T.inm if kind == "m" else T.rxm)[:, at:at + w]
+            sem = name(kind, t, ci)
             rid, pid = topo.addr(to, core)
             g.remote_dma(land, src, T.sem[sem], T.sem.loc, pid, rid, topo.mask(core, to))
             loc += len(topo.engines(core, to))
-            o["sig"] = [(sem, last_hop(T, core, t, kind, ci, topo), {})]
+            o["sig"] = (sem, len(topo.engines(routes(frm, core, topo)[ci], core)), {})
         elif "dsem" in o:
             o["f"](q).then_inc(T.sem[o["dsem"]], 16)
-            o["sig"] = [(o["dsem"], 16, dict(kn))]
+            o["sig"] = (o["dsem"], 16, dict(kn))
         else:
             sem = cs[e]
             count[sem] = count.get(sem, 0) + 1
             o["f"](q).then_inc(T.sem[sem], 1)
             clk = dict(kn)
             clk[sem] = count[sem]
-            o["sig"] = [(sem, count[sem], clk)]
+            o["sig"] = (sem, count[sem], clk)
     for o in ops:
         if "dsem" in o:
             g.wait_ge(T.sem[o["dsem"]], 16)
@@ -496,51 +593,30 @@ def emit(g, core, T, topo, ops, seq, nxt, home):
     g.wait_ge(T.sem.loc, loc)
 
 
-def ends(rank, T, kind, t):
-    n = len(T.cores)
-    return (rank - (NV - 1)) % n if t == NV else (rank + 1) % n
-
-
-def last_hop(T, core, t, kind, ci, topo):
-    rank, n = T.rank_of(core), len(T.cores)
-    src = T.cores[(rank + (NV - 1)) % n] if t == NV else T.cores[(rank - 1) % n]
-    via = routes(src, core, topo)[ci]
-    return len(topo.engines(via, core))
-
-
 def relay(g, core, T, topo):
-    jobs = []
+    loc = 0
     for rank, src in enumerate(T.cores):
         if core not in topo.cores_of(src):
             continue
-        for t in range(1, NV + 1):
-            dst = T.cores[ends(rank, T, "m", t)]
+        for kind, t in [("z", 0)] + [("m", t) for t in range(1, NV + 1)]:
+            dst = peer(T, rank, kind, t, 1)
             for ci in range(NC):
-                if routes(src, dst, topo)[ci] == core:
-                    if t < NV:
-                        jobs.append((src, dst, t, 0, ci))
-                    jobs.append((src, dst, t, 1, ci))
-    jobs.sort(key=lambda j: (j[2], j[3], j[4]))
-    loc = 0
-    for src, dst, t, m, ci in jobs:
-        wide = 192 if m else 64
-        w = 128 if m and t == NV else wide
-        at = wide * (2 * t + ci)
-        sem = T.sem[("arr%d%s" if m else "xar%d%s") % (t, "AB"[ci])]
-        buf = (T.inm if m else T.rxm)[:, at:at + w]
-        g.wait_ge(sem, len(topo.engines(src, core)))
-        rid, pid = topo.addr(dst, core)
-        g.remote_dma(buf, buf, sem, T.sem.loc, pid, rid, topo.mask(core, dst))
-        loc += len(topo.engines(core, dst))
+                if routes(src, dst, topo)[ci] != core:
+                    continue
+                a, w = span(t, ci)
+                buf = T.zn[:, ci] if kind == "z" else T.inm[:, a:a + w]
+                sem = T.sem[name(kind, t, ci)]
+                g.wait_ge(sem, len(topo.engines(src, core)))
+                rid, pid = topo.addr(dst, core)
+                g.remote_dma(buf, buf, sem, T.sem.loc, pid, rid, topo.mask(core, dst))
+                loc += len(topo.engines(core, dst))
     if loc:
         g.wait_ge(T.sem.loc, loc)
 
 
 def rank_program(g, core, T, topo):
-    rank = T.rank_of(core)
-    if rank is None:
+    if T.rank_of(core) is None:
         relay(g, core, T, topo)
         return
     ops = link(build(T))
-    seq = order(ops)
-    emit(g, core, T, topo, ops, seq, T.cores[ends(rank, T, "m", 1)], T.cores[ends(rank, T, "m", NV)])
+    emit(g, core, T, topo, ops, order(ops))

@@ -4,9 +4,11 @@ from concourse.mybir import dt, AluOpType, AxisListType, ActivationFunctionType
 A_ = AluOpType
 F_ = ActivationFunctionType
 NV, NC, L2, STEPS = 4, 2, 64, 6
-CUT = {"v": (34, 16, 14), "v0": (32, 32), "g": (32, 32), "s": (24, 20, 20), "s0": (32, 32), "x": (32, 32)}
-XV = (0,)
-OPT = {"late": 5, "nev": True}
+CUT = {"v": (32, 8, 24), "v0": (32, 32), "v5": (34, 8, 22), "g": (8,) * 8,
+       "s": (18, 46), "s0": (32, 32), "s5": (20, 44), "xA": (30, 34), "xB": (30, 16, 18), "v1": (16, 8, 40), "s1": (8, 56)}
+LP = [64]
+XV = [0, 1]
+OPT = {"late": 5, "t0": True}
 PF = False
 ALPHA, GAP, TOP = 0.8, 18, 86.0
 TAU = 5.0 * math.exp(TOP - ALPHA * GAP * 12)
@@ -22,8 +24,8 @@ SCRATCH = {
     "zo": ("sbuf", [128, 2, 192], "float16"), "zn": ("sbuf", [128, 2, 192], "float16"),
     "sgi": ("sbuf", [128, 512], "int32"), "sgb": ("sbuf", [128, 512], "float16"),
     "inm": ("sbuf", [128, 10 * MW], "uint16"), "som": ("sbuf", [128, 8 * MW], "uint16"),
-    "cnt": ("sbuf", [128, 8], "float32"), "cni": ("sbuf", [128, 16], "int32"), "junk": ("sbuf", [128, 64], "float32"),
-    "yo": ("sbuf", [128, 256], "float32"),
+    "cnt": ("sbuf", [128, 8], "float32"), "hw0": ("sbuf", [128, 128], "float32"),
+    "yo": ("sbuf", [128, 256], "float32"), "thc": ("sbuf", [128, 16], "float32"), "tho": ("sbuf", [128, 16], "float32"),
     "pcol": ("sbuf", [128, 16], "int32"), "fcol": ("sbuf", [128, 32], "float32"),
     "itf": ("sbuf", [128, 144], "bfloat16"), "itg": ("sbuf", [128, 128], "bfloat16"), "it8": ("sbuf", [128, 8], "bfloat16"),
     "itk": ("sbuf", [128, 8, 8], "bfloat16"),
@@ -35,9 +37,9 @@ for _n in ("ch0", "ch1", "nh0", "nh1"):
     SCRATCH[_n] = ("sbuf", [128, 64], "float16")
 for _n in ("cb0", "cb1"):
     SCRATCH[_n] = ("sbuf", [128, 64], "bfloat16")
-for _n in ("idh", "ndh", "hw0", "r8"):
+for _n in ("idh", "ndh", "idB", "ndB", "r8"):
     SCRATCH[_n] = ("sbuf", [128, 128], "float16")
-for _n in ("idb", "blk", "nbk", "tbk", "wr0", "wr1"):
+for _n in ("idb", "blk", "nbk", "tbk"):
     SCRATCH[_n] = ("sbuf", [128, 128], "bfloat16")
 for _c in "AB":
     SCRATCH["mh" + _c] = ("sbuf", [128, MW], "float16")
@@ -46,10 +48,10 @@ for _c in "AB":
         SCRATCH[_n + _c] = ("sbuf", [128, 1024], "bfloat16")
     for _n, _w in (("d1", 192), ("dG", 192), ("dX", 128), ("dS", 128), ("mi", 64), ("nf", 64), ("pu", 64), ("w4", 64), ("w5", 64)):
         SCRATCH[_n + _c] = ("sbuf", [128, _w], "bfloat16")
-    for _n, _w in (("va", 192), ("nx", 192), ("oG", 192), ("oX", 128), ("oS", 128), ("ab", 64)):
+    for _n, _w in (("va", 192), ("nx", 192), ("oG", 192), ("oX", 128), ("oS", 128)):
         SCRATCH[_n + _c] = ("sbuf", [128, _w], "float32")
     SCRATCH.update({
-        "ne" + _c: ("sbuf", [128, 192], "float16"), "a0" + _c: ("sbuf", [128, 64], "float16"),
+        "ne" + _c: ("sbuf", [128, 17, 8], "float16"), "a0" + _c: ("sbuf", [128, 64], "float16"),
         "zc4" + _c: ("sbuf", [128, 17, 8], "bfloat16"), "zc5" + _c: ("sbuf", [128, 17, 8], "bfloat16"),
         "pq" + _c: ("sbuf", [128, 64, 2], "bfloat16"), "pg" + _c: ("sbuf", [128, 64, 2], "float16"),
         "cv" + _c: ("psum", [128, 8, 8, 8], "float32"), "pa" + _c: ("psum", [128, 512] if PF else [128, 2, 8, 8, 4], "float32"),
@@ -58,11 +60,11 @@ for _c in "AB":
     for _j in range(3):
         SCRATCH["zz%d%s" % (_j, _c)] = ("sbuf", [128, 17, 8], "float16")
 NDMA = 24
-SEMAPHORES = ["v", "s", "p", "q", "loc", "zarA", "zarB"] + ["d%d" % i for i in range(NDMA)] \
+SEMAPHORES = ["v", "s", "p", "q", "loc", "zarA", "zarB", "thr1", "thr2", "thr3"] + ["d%d" % i for i in range(NDMA)] \
     + ["arr%d%s" % (t, c) for t in range(1, 5) for c in "AB"]
 
-SHIFT = {}
-PAR = {"cyc": 0.95e-3, "pec": 0.55e-3, "lat": 0.16, "gat": 1.4, "net": 5.0, "ev": 8.5}
+SHIFT = {"uv": -150.0, "pmhA": -120.0, "ppgA": -120.0, "pmhB": -120.0, "ppgB": -120.0}
+PAR = {"cyc": 0.9e-3, "pec": 0.55e-3, "lat": 0.2, "gat": 1.3, "net": 5.5, "ev": 9.0, "eps": 0.04}
 
 
 def gath(n):
@@ -98,8 +100,8 @@ def build(T):
     nd = [0]
     cur = ["u"]
 
-    def op(eng, cost, R, W, fn, bank=None, lat=0.0, line=None):
-        ops.append({"e": eng, "c": cost, "R": R, "W": W, "f": fn, "b": bank, "lat": lat, "key": cur[0] + W[0], "line": line})
+    def op(eng, cost, R, W, fn, bank=None, lat=0.0, line=None, after=None):
+        ops.append({"e": eng, "c": cost, "R": R, "W": W, "f": fn, "b": bank, "lat": lat, "key": cur[0] + W[0], "line": line, "after": after})
 
     def v(cost, R, W, fn, bank=None):
         op("v", cost, R, W, fn, bank)
@@ -107,14 +109,14 @@ def build(T):
     def s(cost, R, W, fn, bank=None):
         op("s", cost, R, W, fn, bank)
 
-    def gather(eng, lanes, R, W, fn):
-        op(eng, gath(16 * lanes), R, W, fn, line=eng)
+    def gather(eng, lanes, R, W, fn, after=None):
+        op(eng, gath(16 * lanes), R, W, fn, line=eng, after=after)
 
     def dma(queue, R, W, o, i, dur):
         k = nd[0]
         nd[0] += 1
         ops.append({"e": queue, "c": 0.1, "R": R, "W": W, "b": None, "lat": dur, "dsem": "d%d" % k, "key": "u" + (W or ["out"])[0],
-                    "f": (lambda q, o=o, i=i: q.dma_start(o, i)), "line": "d" + queue})
+                    "f": (lambda q, o=o, i=i: q.dma_start(o, i)), "line": "d" + queue, "after": None})
 
     def ts(out, in0, s1, o0, s2=None, o1=None):
         if o1 is None:
@@ -136,21 +138,22 @@ def build(T):
     def scan(out, d0, d1):
         return lambda q: q.tensor_tensor_scan(out, d0, d1, 0.0, A_.mult, A_.add)
 
-    def mm(n, R, W, lst, bank, first=True, last=True):
+    def mm(n, R, W, lst, bank, first=True, last=True, after=None):
         def f(q):
             r = None
             for i, (o, a, b) in enumerate(lst):
                 r = q.matmul(o, a, b, first and i == 0, last and i == len(lst) - 1)
             return r
-        op("p", n * PAR["pec"], R, W, f, bank)
+        op("p", n * PAR["pec"], R, W, f, bank, after=after)
 
     dma("y", [], ["pc"], T.pc[:], T.par[:], 2.3)
-    dma("s", [], ["zi"], T.zi[:], T.z[:], 2.8)
-    dma("s", [], ["liS"], T.li[:, :, 0], T.s0[:], 3.0)
-    dma("s", [], ["liG"], T.li[:, :, 1], T.g0[:], 3.0)
-    dma("s", [], ["sgi"], T.sgi[0:8, :], T.sg[:], 3.0)
     dma("y", [], ["tev0"], T.tev[0:64, :], T.ev[0:64, :], PAR["ev"])
-    dma("s", [], ["tev1"], T.tev[64:128, :], T.ev[64:128, :], PAR["ev"])
+    dma("y", [], ["tev1"], T.tev[64:128, :], T.ev[64:128, :], PAR["ev"])
+    dma("y", [], ["zi"], T.zi[:, 1:4], T.z[:, 128:512], PAR["ev"] + 1.5)
+    dma("s", [], ["zi0"], T.zi[:, 0], T.z[:, 0:128], PAR["ev"] - 2)
+    dma("s", [], ["liS"], T.li[:, :, 0], T.s0[:], PAR["ev"] - 2)
+    dma("s", [], ["liG"], T.li[:, :, 1], T.g0[:], PAR["ev"] - 2)
+    dma("s", [], ["sgi"], T.sgi[0:8, :], T.sg[:], PAR["ev"] - 2)
 
     fl = True
     op("g", 0.2, [], ["pcol0"], lambda q: q.iota(T.pcol[:, 0:1], [[0, 1]], 0, 1))
@@ -189,13 +192,7 @@ def build(T):
     fcol(22, FC(15), FC(16), A_.add, FC(18), A_.add, dep=(15, 16, 18))
     fcol(23, FC(17), 2.0, A_.mult, FC(18), A_.add, dep=(17, 18))
     fcol(10, FC(22), FC(19), A_.add, dep=(22, 19))
-    fcol(24, FC(3), 0.0, A_.is_equal)
-    fcol(25, FC(3), 1.0, A_.is_equal)
-    fcol(26, FC(3), 1.0, A_.is_equal, 67.0, A_.mult)
-    fcol(27, FC(3), 0.0, A_.is_equal, 64.0, A_.mult)
-    fcol(28, FC(24), FC(25), A_.subtract, dep=(24, 25))
-    fcol(29, FC(3), 0.0, A_.is_equal, 128.0, A_.mult)
-    fcol(30, FC(3), 1.0, A_.is_equal, -1.0, A_.mult)
+    fcol(24, FC(3), 0.0, A_.is_equal, -0.5, A_.mult)
 
     def sel(name, out, src, col, w=None, dep=()):
         R = [src.split(":")[0], "fc"] + ["fc%d" % x for x in (col,) + tuple(dep) if x > 7]
@@ -207,30 +204,32 @@ def build(T):
         for o, col in enumerate(cols):
             sel(n, T[n][:, :, o], "it8", 1, FC(col), (col,))
     v(small(64), [], ["cna1"], ms(T.cna[:, 1], 0.0))
-    sel("cna", T.cna[:, 0], "itk", 1, FC(28), (28,))
-    sel("cne", T.cne[:], "itk", 1, FC(29), (29,))
-    sel("cg", T.cg[:], "itf:64", 8, -1.0)
+    sel("cna", T.cna[:, 0], "itk", 1, 1.0 / 16)
+    sel("cne", T.cne[:], "itk", 1, 8.0)
+    sel("cg", T.cg[:], "itf:64", 8)
+    sel("idB", T.idB[:], "itf:128", 0, BIG)
+    sel("ndB", T.ndB[:], "itf:128", 0, -BIG)
     for h, col in ((0, 9), (1, 11)):
         sel("ch%d" % h, T["ch%d" % h][:], "itf:64", col)
         sel("nh%d" % h, T["nh%d" % h][:], "itf:64", col, -1.0)
-        sel("cb%d" % h, T["cb%d" % h][:], "itf:64", col, 2.0 ** -12)
+        sel("cb%d" % h, T["cb%d" % h][:], "itf:64", col, 1.0 / 32)
     sel("idh", T.idh[:], "itf:128", 0)
     sel("ndh", T.ndh[:], "itf:128", 0, -1.0)
     sel("idb", T.idb[:], "itf:128", 0)
     sel("blk", T.blk[:], "itg", 1)
     sel("nbk", T.nbk[:], "itg", 1, -1.0)
-    sel("wr0", T.wr0[:], "itg", 1, FC(24), (24,))
-    sel("wr1", T.wr1[:], "itg", 1, FC(30), (30,))
     sel("r8", T.r8[:], "itg", 0)
     sel("w0", T.w0[:], "itf:144", 12)
     sel("tb0", T.tbk[:], "itf:128", 0, 2.0)
     v(small(256), ["tb0", "nbk"], ["tbk"], tt(T.tbk[:], T.tbk[:], T.nbk[:], A_.add))
-    v(small(64), ["itg", "fc24"], ["hw0"], ts(T.hw0[:], T.itg[:], 0.0, A_.mult, FC(24), A_.add))
-    s(1.4, ["fc"], ["warm"], act(T.junk[:, 0:1], FC(0), F_.Exp, 0.0, -1.0))
+    v(small(128), ["itg", "fc24"], ["hw0"], ts(T.hw0[:], T.itg[:], 0.0, A_.mult, FC(24), A_.add))
+    for j, x in enumerate((-74.5, 1.0, -10.5, 0.0)):
+        v(small(1), [], ["th0"], ms(T.thc[:, j:j + 1], x))
+    v(small(1), [], ["cn2"], ms(T.cnt[:, 2:3], -2.0 ** -12))
+    s(1.4, ["cn2"], ["warm"], act(T.cnt[:, 4:5], T.cnt[:, 2:3], F_.Exp))
     for c in "AB":
-        for n in ("zz0", "zz1", "zz2", "zc4", "zc5"):
+        for n in ("zz0", "zz1", "zz2", "zc4", "zc5", "ne"):
             v(small(68), [], [n + c], ms(T[n + c][:], 0.0))
-        v(small(96), [], ["nez" + c], ms(T["ne" + c][:], 0.0))
         for n, k in (("d1", 3), ("dG", 3), ("dX", 2), ("dS", 2)):
             v(small(64), [], [n + "z" + c], ms(T[n + c][:, 0::k], 0.0))
 
@@ -239,11 +238,12 @@ def build(T):
         DI, DG = T.dgi[:, 256 * d:256 * d + 256], T.dg[:, 256 * d:256 * d + 256]
         v(small(256), [nm], ["dgi%d" % d], ts(DI, src[:], 63 << (6 * (d % 4)), A_.bitwise_and))
         v(small(256), ["dgi%d" % d], ["dg%d" % d], cp(DG, DI))
-        dma("y", ["dg%d" % d], ["ptab%d" % d], T.ptab[d::16, :], DG, 2.5)
+        dma("s", ["dg%d" % d], ["ptab%d" % d], T.ptab[d::16, :], DG, 2.5)
     PT = ["ptab%d" % d for d in range(6)]
     EV = ["tev0", "tev1"]
 
-    v(small(512), ["sgi"], ["sgb"], ts(T.sgb[0:8, :], T.sgi[0:8, :], -MID, A_.add))
+    for t in range(NV):
+        v(small(128), ["sgi"], ["sgb%d" % t], ts(T.sgb[0:8, 128 * t:128 * t + 128], T.sgi[0:8, 128 * t:128 * t + 128], -MID, A_.add))
     for ci, c in enumerate("AB"):
         v(small(192), ["zi"], ["zo" + c], ts(T.zo[:, ci], T.zi[:, 1:4, ci], -MID, A_.add))
         op("net", 0.4, ["zo" + c], ["zn" + c], ("z", 0, ci, T.zo[:, ci], T.zn[:, ci]), None, 8.0)
@@ -259,10 +259,10 @@ def build(T):
         M = lambda a, w=64: T.inm[:, q0 + a:q0 + a + w]
         kX, kM = "iX%d%s" % (t, c), "iM%d%s" % (t, c)
         if t == 0:
-            v(small(64), ["zi"], [kX], cp(M(MX), T.zi[:, 0, ci]))
+            v(small(64), ["zi0"], [kX], cp(M(MX), T.zi[:, 0, ci]))
             v(small(128), ["liS", "liG"], [kM], cp(M(MS, 128), T.li[:, ci]))
             v(small(64), [], ["iR" + c], ms(M(MR), 0))
-        for j, (a, b) in enumerate(cuts(CUT["x"])):
+        for j, (a, b) in enumerate(cuts(CUT["x" + c])):
             EX, IN = B("ex")[:, 16 * a:16 * b], T.tev[:].indirect(T.inm[:, q0 + a:q0 + b])
             if ci in XV and j == 0:
                 gather("v", b - a, EV + [kX], ["exv" + c], cp(EX, IN))
@@ -272,25 +272,22 @@ def build(T):
         for h in range(2):
             v(small(64), [kM, "fc", "fc13"], ["pg" + c], ts(B("pg")[:, :, h], M(MG), -MID, A_.add, FC(13) if h == 0 else FC(5), A_.mult))
         lo = 128 * t + L2 * ci
-        mm(128, ["sgb", "r8", "ndh", "mh" + c], ["y" + c],
+        mm(128, ["sgb%d" % t, "r8", "ndh", "mh" + c], ["y" + c],
            [(B("fz")[:, 0], T.r8[0:8, :], T.sgb[0:8, lo:lo + L2]), (B("fz")[:, 0], T.ndh[:], B("mh")[:, MR:MR + 64])], "fz" + c)
+        for h in range(2):
+            s(small(64), ["y" + c], ["pq" + c], act(B("pq")[:, :, h], B("fz")[:, 0], F_.Relu, 0.0, 64.0), "fz" + c)
+        s(small(64), ["y" + c, "dSz" + c], ["dS" + c], act(B("dS")[:, 1::2], B("fz")[:, 0], F_.Sign, -0.5), "fz" + c)
+
+    TH = lambda t, j: T.thc[:, 4 * t + j:4 * t + j + 1]
 
     def threshold(t):
-        cur[0] = "p"
-        bias, kb = FC(26), "fc26"
-        if t > 0:
-            bias, kb = T.cnt[:, 4 + t:5 + t], "th"
-            mm(128, ["hw0", "mhA", "mhB"], ["par"],
-               [(T.fzB[:, 2], T.hw0[:], T.mhA[:, MR:MR + 64]), (T.fzB[:, 2], T.hw0[:], T.mhB[:, MR:MR + 64])], "fzB")
-            s(small(64) + 0.02, ["par"], ["cnt"],
-              lambda q: q.activation(T.junk[:], T.fzB[:, 2], F_.Copy, bias=16 * MID, accum_out=T.cnt[:, t:t + 1]), "fzB")
-            v(small(1), ["cnt"], ["cni"], cp(T.cni[:, t:t + 1], T.cnt[:, t:t + 1]))
-            v(small(1), ["cni"], ["cnj"], ts(T.cni[:, 8 + t:9 + t], T.cni[:, t:t + 1], 1, A_.bitwise_and))
-            v(small(1), ["cnj", "fc25", "fc26"], ["th"], ts(bias, T.cni[:, 8 + t:9 + t], FC(25), A_.mult, FC(26), A_.add))
-        for c in "AB":
-            s(small(64), ["y" + c, "dSz" + c], ["dS" + c], act(T["dS" + c][:, 1::2], T["fz" + c][:, 0], F_.Sign, -0.5), "fz" + c)
-            for h in range(2):
-                s(small(64), ["y" + c, kb, "fc27"], ["pq" + c], act(T["pq" + c][:, :, h], T["fz" + c][:, 0], F_.Relu, bias, FC(27)), "fz" + c)
+        cur[0] = "f"
+        Y, R2 = T.cvB[:, 6, 0, 0:1], T.cnt[:, 3:4]
+        mm(512, ["hw0", "cnA", "cn2"], ["yw"], [(Y, T.hw0[:], T.cnt[:, 2:3]), (Y, T.hw0[:], T.cnt[:, 0:1])], "cvB", True, False)
+        mm(256, ["cnB"], ["yn"], [(Y, T.hw0[:], T.cnt[:, 1:2])], "cvB", False, True)
+        v(small(1), ["yn"], ["r2"], ts(R2, Y, 1.5 * 2 ** 24, A_.add, -1.5 * 2 ** 24, A_.add), "cvB")
+        v(small(4), ["yn", "r2", "th0"], ["tho%d" % t], ts(T.tho[:, 4 * t:4 * t + 4], T.thc[:, 0:4], Y, A_.add, R2, A_.subtract), "cvB")
+        op("net", 0.4, ["tho%d" % t], ["th%d" % (t + 1)], ("h", t + 1, 0, T.tho[:, 4 * t:4 * t + 4], T.thc[:, 4 * t + 4:4 * t + 8]), None, PAR["net"])
 
     def bounds(t, ci, part):
         c = "AB"[ci]
@@ -299,17 +296,16 @@ def build(T):
         q0 = slot(t, ci) + MG
         if part == 0:
             for a, b in cuts(CUT["g"]):
-                gather("v", b - a, EV + ["iM%d%s" % (t, c), "exs" + c, "exv" + c], ["gg" + c],
-                       tt(B("gg")[:, 16 * a:16 * b], T.tev[:].indirect(T.inm[:, q0 + a:q0 + b]), B("ex")[:, 16 * a:16 * b], A_.is_ge))
+                op("v", gath(16 * (b - a)), EV + ["iM%d%s" % (t, c), "exs" + c, "exv" + c], ["gg" + c],
+                   tt(B("gg")[:, 16 * a:16 * b], T.tev[:].indirect(T.inm[:, q0 + a:q0 + b]), B("ex")[:, 16 * a:16 * b], A_.is_ge), line="w")
             return
         CG, FM = B("fz")[:, 1], B("fz")[:, 2]
         for j in range(4):
             mm(256, ["gg" + c, "w0"], ["cG%d%s" % (j, c)],
-               [(CG, T.w0[:, 16 - k:144 - k], B("gg")[:, k::16]) for k in range(4 * j, 4 * j + 4)], "fz" + c, j == 0, False)
-        mm(64, ["wr1", "pq" + c], ["cG" + c], [(CG, T.wr1[:], B("pq")[:, :, 0])], "fz" + c, False, True)
-        s(small(64), ["cG" + c], ["mi" + c], act(B("mi")[:], CG, F_.Sign, -56.5, -1.0), "fz" + c)
-        mm(128, ["mi" + c, "pq" + c, "blk", "wr0"], ["fm" + c], [(FM, T.wr0[:], B("pq")[:, :, 0]), (FM, T.blk[:], B("mi")[:])], "fz" + c)
-        s(small(64), ["fm" + c], ["nf" + c], act(B("nf")[:], FM, F_.Relu, 15.0 / 256, 1.0 / 256), "fz" + c)
+               [(CG, T.w0[:, 16 - k:144 - k], B("gg")[:, k::16]) for k in range(4 * j, 4 * j + 4)], "fz" + c, j == 0, j == 3)
+        s(small(64), ["cG3" + c, "th%d" % t], ["mi" + c], act(B("mi")[:], CG, F_.Sign, TH(t, 2)), "fz" + c)
+        mm(128, ["mi" + c, "pq" + c, "nbk", "idb"], ["fm" + c], [(FM, T.idb[:], B("pq")[:, :, 0]), (FM, T.nbk[:], B("mi")[:])], "fz" + c)
+        s(small(64), ["fm" + c], ["nf" + c], act(B("nf")[:], FM, F_.Relu, 7.5, 0.5), "fz" + c)
         s(small(64), ["fm" + c], ["pu" + c], act(B("pu")[:], FM, F_.Relu, -57.0), "fz" + c)
 
     def back(i, c, out, u="ch"):
@@ -322,20 +318,25 @@ def build(T):
         cur[0] = str(i)
         q0 = slot(t, ci) + MS
         off, kF = (T.inm[:, q0:q0 + 64], "iM%d%s" % (t, c)) if i == 0 else (B("off"), "off" + c)
-        for a, b in cuts(CUT["s0" if i == 0 else "s"]):
-            gather("s", b - a, PT + [kF], ["gp" + c], act(B("gp")[:, 16 * a:16 * b], T.ptab[:].indirect(off[:, a:b]), F_.Copy))
-        for a, b in cuts(CUT["v0" if i == 0 else "v"]):
-            gather("v", b - a, EV + [kF, "exs" + c, "exv" + c], ["ge" + c],
-                   tt(B("ge")[:, 16 * a:16 * b], T.tev[:].indirect(off[:, a:b]), B("ex")[:, 16 * a:16 * b], A_.is_ge))
+        o, io = "AB"[1 - ci], i - 1 + ci
+        turn = (i, ci) > (0, 0) and (i > 0 or OPT["t0"])
+        name = "v5" if (i, ci) == (STEPS - 1, 1) else "v1" if (i, ci) == (0, 1) else "v" if turn else "v0"
+        for j, (a, b) in enumerate(cuts(CUT["s" + name[1:]])):
+            gather("s", b - a, PT + [kF], ["gp" + c], act(B("gp")[:, 16 * a:16 * b], T.ptab[:].indirect(off[:, a:b]), F_.Copy),
+                   "d1" + o if turn and j == 1 else None)
+        for j, (a, b) in enumerate(cuts(CUT[name])):
+            after = (None, "nx" + o, "zz%d%s" % (io % 3, o), None, None)[j] if turn else None
+            gather("v", b - a, EV + [kF, "exs" + c, "exv" + c], ["ge%d%s" % (k, c) for k, (x, y) in enumerate(cuts(LP)) if x < b and a < y],
+                   tt(B("ge")[:, 16 * a:16 * b], T.tev[:].indirect(off[:, a:b]), B("ex")[:, 16 * a:16 * b], A_.is_ge), after)
 
     def step(t, i, ci):
         c = "AB"[ci]
         B = lambda n: T[n + c]
         cur[0] = str(i)
         kz = lambda j: "zz%d%s" % (j % 3, c)
-        ZZ, X, E = T[kz(i)][:, 1::2], B("cv")[:, 0:2], B("cv")[:, 2]
-        pre = [(X, B("pq")[:], T.cna[:])]
-        cov = [(X[:, :, :, k], B("ge")[:, k::8], T.bo[:]) for k in range(8)]
+        ZZ, X, E = T[kz(i)][:, 1::2], B("cv")[:, 0:2], B("pa")[:, 256:320] if PF else B("pa")[:, 1, :, :, 0]
+        pre, NE = [(X, B("pq")[:], T.cna[:])], B("ne")[:, 1::2]
+        cov = lambda a, b: [(B("cv")[2 * a:2 * b, 0:2, :, k], B("ge")[:, 16 * a + k:16 * b:8], T.bo[:]) for k in range(8)]
         nf, wp = (3, "wp1") if i else (4, "wp0")
         if PF:
             PX = lambda f: B("pa")[:, f:192:3] if f < 3 else B("pa")[:, 192:256]
@@ -344,28 +345,28 @@ def build(T):
             PX = lambda f: B("pa")[:, 0, :, :, f]
             par = [(B("pa")[:, 0, :, k, 0:nf], B("gp")[:, k::8], T[wp][:]) for k in range(8)]
         if i == 0:
+            mm(128, ["pg" + c, "cg", "pq" + c, "cne"], ["gE" + c], [(E, B("pg")[:], T.cg[:]), (E, B("pq")[:], T.cne[:])], "pa" + c)
             mm(64 * len(par), ["gp" + c, wp], ["pa" + c], par, "pa" + c)
-            mm(512, ["ge" + c, "bo"], ["cw" + c], cov, "cv" + c, True, False)
-            mm(128, ["pq" + c, "cna", "cna1"], ["cv" + c], pre, "cv" + c, False, True)
         else:
             ka, AP = ("a0" + c, B("a0")[:]) if i == 1 else (kz(i - 2), T[kz(i - 2)][:, 1::2])
-            NE = B("ne")[:, 2::3]
-            mm(192 if PF else 320, [ka, "ne" + c, "idh", "ndh"], ["pw" + c],
-               [(PX(3), T.idh[:], AP), (PX(3), T.ndh[:], NE),
-                (PX(2), T.idh[:], NE) if PF else (B("pa")[:, 0, :, :, 0:3], T.idh[:], B("ne")[:])], "pa" + c, True, False)
-            mm(64 * len(par), ["gp" + c, wp], ["pa" + c], par, "pa" + c, False, True)
-            mm(128, ["pq" + c, "cna", "cna1"], ["cw" + c], pre, "cv" + c, True, False)
-            mm(512, ["ge" + c, "bo"], ["cv" + c], cov, "cv" + c, False, True)
+            mm(128, [ka, "ne" + c, "idh", "ndB"], ["pw" + c], [(PX(3), T.idh[:], AP), (PX(3), T.ndB[:], NE)], "pa" + c, True, False)
+            mm(64 * len(par) + 64, ["gp" + c, wp, "idB"], ["pa" + c], par + [(PX(2), T.idB[:], NE)], "pa" + c, False, True)
+        mm(128, ["pq" + c, "cna", "cna1"], ["cw" + c], pre, "cv" + c, True, False)
+        for j, (a, b) in enumerate(cuts(LP)):
+            mm(8 * min(64, 2 * (b - a)), ["ge%d%s" % (j, c), "bo"], ["cv" + c if b == L2 else "cw" + c], cov(a, b), "cv" + c, False, b == L2,
+               "aL" + "AB"[1 - ci] if 0 < 2 * i + ci < 2 * STEPS - 1 and j == max(len(LP) - 2, 0) else None)
         if not PF:
             s(small(192), ["pa" + c], ["va" + c], act(B("va")[:], B("pa")[:, 0, :, :, 0:3], F_.Copy), "pa" + c)
-        for j in range(2):
-            s(small(64), ["cv" + c, "d1z" + c], ["d1" + c], act(B("d1")[:, 1 + j::3], X[:, j], F_.Sign, -7.5), "cv" + c)
+        s(small(64), ["cv" + c, "d1z" + c], ["d1" + c], act(B("d1")[:, 2::3], X[:, 1], F_.Sign, -7.5), "cv" + c)
+        s(small(64), ["cv" + c, "d1z" + c, "th%d" % t], ["d1" + c], act(B("d1")[:, 1::3], X[:, 0], F_.Sign, TH(t, 0)), "cv" + c)
         if i >= STEPS - 2:
-            s(small(64), ["cv" + c], ["zc%d%s" % (i, c)], act(B("zc%d" % i)[:, 1::2], X[:, 0], F_.Copy, 68.0), "cv" + c)
+            s(small(64), ["cv" + c, "th%d" % t], ["zc%d%s" % (i, c)], act(B("zc%d" % i)[:, 1::2], X[:, 0], F_.Identity, TH(t, 1)), "cv" + c)
         if PF:
             v(small(192), ["d1" + c, "pa" + c], ["nx" + c], scan(B("nx")[:], B("d1")[:], B("pa")[:, 0:192]), "pa" + c)
         else:
             v(small(192), ["d1" + c, "va" + c], ["nx" + c], scan(B("nx")[:], B("d1")[:], B("va")[:]))
+        if i == STEPS - 1:
+            v(small(64), ["nx" + c, "gE" + c], ["ne" + c], tt(NE, B("nx")[:, 2::3], E, A_.not_equal), "pa" + c)
         if i == 0:
             v(small(64), ["nx" + c], [kz(i)], cp(ZZ, B("nx")[:, 2::3]))
             v(small(64), ["pa" + c], ["a0" + c], cp(B("a0")[:], PX(3)), "pa" + c)
@@ -374,9 +375,7 @@ def build(T):
         if i < STEPS - 1:
             mm(128, [kz(i), "ch0", "ch1"], ["aL" + c], back(i, c, B("tr")[:, 0:64]), "tr" + c)
             v(small(64), ["aL" + c], ["off" + c], ts(B("off")[:], B("tr")[:, 0:64], MID, A_.add), "tr" + c)
-            mm(192, [kz(i), "idh", "pg" + c, "cg", "pq" + c, "cne"], ["e" + c],
-               [(E, B("pg")[:], T.cg[:]), (E, B("pq")[:], T.cne[:]), (E, T.idh[:], ZZ)], "cv" + c)
-            v(small(64), ["e" + c, "nez" + c], ["ne" + c], ts(B("ne")[:, 2::3], E, 0.0, A_.not_equal, BIG, A_.mult), "cv" + c)
+            v(small(64), [kz(i), "gE" + c], ["ne" + c], tt(NE, ZZ, E, A_.not_equal), "pa" + c)
         F = lambda j: B("tr")[:, 64 + j:256:3] if j < 3 else B("tr")[:, 253 + j:384:2] if j < 5 else B("tr")[:, 379 + j:512:2]
         MH = lambda a: B("mh")[:, a:a + 64]
         if i == STEPS - 2:
@@ -396,12 +395,10 @@ def build(T):
         B = lambda n: T[n + c]
         cur[0] = "w"
         Z, ww, ZC = B("fz")[:, i - 1], "w%d" % i, B("zc%d" % i)
-        mm(256, ["zc%d%s" % (i, c), "cb0", "cb1", "nf" + c, "idb", "ndh", "mh" + c], ["zw" + c],
-           [(Z, T.ndh[:], B("mh")[:, MG:MG + 64]), (Z, T.idb[:], B("nf")[:]), (Z, ZC[:, 1:17], T.cb0[:]), (Z, ZC[:, 0:16], T.cb1[:])],
-           "fz" + c, True, False)
-        mm(128, ["zz%d%s" % (i % 3, c), "ch0", "ch1"], ["Z" + c], back(i, c, Z), "fz" + c, False, True)
-        s(small(64), ["Z" + c], ["ab" + c], act(B("ab")[:], Z, F_.Abs), "fz" + c)
-        s(small(64), ["ab" + c, "fc14"], [ww + c], act(B(ww)[:], B("ab")[:], F_.Exp, FC(14), -ALPHA * GAP * 4096))
+        mm(192, ["zc%d%s" % (i, c), "cb0", "cb1", "nf" + c, "idb"], ["zw" + c],
+           [(Z, T.idb[:], B("nf")[:]), (Z, ZC[:, 1:17], T.cb0[:]), (Z, ZC[:, 0:16], T.cb1[:])], "fz" + c, True, False)
+        mm(128, ["ne" + c, "ch0", "ch1"], ["Z" + c], [(Z, B("ne")[:, 1:17], T.ch0[:]), (Z, B("ne")[:, 0:16], T.ch1[:])], "fz" + c, False, True)
+        s(small(64), ["Z" + c, "fc14"], [ww + c], act(B(ww)[:], Z, F_.Exp, FC(14), -ALPHA * GAP * 32), "fz" + c)
 
     def finish(t, ci):
         c = "AB"[ci]
@@ -412,7 +409,7 @@ def build(T):
         lst = [(D4, T.idb[:], B("pu")[:]), (D45, T.idb[:], B("pu")[:]), (D4, T.tbk[:], B("w4")[:]), (D45, T.tbk[:], B("w4")[:])]
         if more:
             lst += [(RD, T.idb[:], B("nf")[:]), (RD, T.blk[:], B("w4")[:])]
-        mm(64 * len(lst), ["pu" + c, "nf" + c, "w4" + c, "tbk"], ["dw" + c], lst, "cv" + c, True, False)
+        mm(64 * len(lst), ["pu" + c, "nf" + c, "w4" + c, "tbk", "blk", "idb"], ["dw" + c], lst, "cv" + c, True, False)
         lst = [(D4, T.nbk[:], B("w5")[:]), (D45, T.tbk[:], B("w5")[:])] + ([(RD, T.blk[:], B("w5")[:])] if more else [])
         mm(64 * len(lst), ["w5" + c], ["D" + c], lst, "cv" + c, False, True)
         so = lambda a: T.som[:, slot(t, ci) + a:slot(t, ci) + a + 64]
@@ -425,7 +422,8 @@ def build(T):
         v(small(64), ["oG" + c], [kM + "G"], ts(so(MG), B("oG")[:, 2::3], 0.5, A_.mult, MID, A_.add))
         R = [kM + "S", kM + "G"]
         if more:
-            s(small(64), ["D" + c, "dXz" + c], ["dX" + c], act(B("dX")[:, 1::2], RD, F_.Sign, -TAU), "cv" + c)
+            s(small(64) + 0.02, ["D" + c, "dXz" + c], ["dX" + c, "cn" + c],
+              lambda q: q.activation(B("dX")[:, 1::2], RD, F_.Sign, bias=-TAU, accum_out=T.cnt[:, ci:ci + 1]), "cv" + c)
             v(small(128), ["dX" + c, "fv" + c], ["oX" + c], scan(B("oX")[:], B("dX")[:], B("tr")[:, 256:384]), "tr" + c)
             v(small(64), ["dX" + c], [kM + "R"], ts(so(MR), B("dX")[:, 1::2], 0.0, A_.is_lt))
             v(small(64), ["oX" + c], [kM + "X"], ts(so(MX), B("oX")[:, 1::2], 0.5, A_.mult, MID, A_.add))
@@ -434,27 +432,26 @@ def build(T):
         op("net", 0.4, R, ["iX%d%s" % (t + 1, c), "iM%d%s" % (t + 1, c), "iR" + c],
            ("m", t + 1, ci, T.som[:, a - 2 * MW:a - 2 * MW + w], T.inm[:, a:a + w]), None, PAR["net"])
 
-    late = OPT["late"]
     for t in range(NV):
         arrive(t, 0)
         gathers(t, 0, 0)
         bounds(t, 0, 0)
         arrive(t, 1)
-        threshold(t)
         for i in range(STEPS):
             for ci in range(NC):
-                if (i, ci) == (late, 1):
-                    bounds(t, 1, 0)
                 if (i, ci) != (0, 0):
                     gathers(t, i, ci)
+                if (i, ci) == (0, 1):
+                    bounds(t, 1, 0)
                 step(t, i, ci)
-                if i == (late if ci else 0):
+                if i == 0:
                     bounds(t, ci, 1)
-                for j in (STEPS - 2, STEPS - 1):
-                    if i == max(j, late if ci else 0):
-                        weight(j, ci)
+                if i >= STEPS - 2:
+                    weight(i, ci)
                 if i == STEPS - 1:
                     finish(t, ci)
+        if t < NV - 1:
+            threshold(t)
     for ci, c in enumerate("AB"):
         q0 = slot(NV, ci) + MS
         v(small(128), ["iM4" + c], ["yo" + c], cp(T.yo[:, 128 * ci:128 * ci + 128], T.inm[:, q0:q0 + 128]))
@@ -471,7 +468,7 @@ def link(ops):
             d.update(wr.get(k, ()))
         for k in o["W"]:
             old = wr.get(k, [])
-            piece = old and k not in o["R"] and not rd.get(k) and all(ops[m]["e"] == o["e"] and ops[m]["W"] == o["W"] for m in old)
+            piece = old and k not in o["R"] and not rd.get(k) and all(ops[m]["e"] == o["e"] and (o["line"] or ops[m]["W"] == o["W"]) for m in old)
             if piece:
                 wr[k] = old + [n]
             else:
@@ -480,6 +477,8 @@ def link(ops):
                 rd[k] = []
             d.update(base[k])
         o["O"] = [line[o["line"]]] if o["line"] in line else []
+        if o["after"]:
+            o["O"].append(wr[o["after"]][-1])
         if o["line"]:
             line[o["line"]] = n
         if o["b"]:
@@ -511,7 +510,7 @@ def order(ops):
     for i in range(n - 1, -1, -1):
         pri[i] = ops[i]["c"] + max([pri[j] + gap for j, gap in suc[i]] or [ops[i]["lat"]])
     for i in range(n):
-        pri[i] += SHIFT.get(ops[i]["key"], 0.0) - (100.0 if ops[i]["line"] in ("v", "s") else 0.0)
+        pri[i] += SHIFT.get(ops[i]["key"], SHIFT.get(ops[i]["key"][0] + ops[i]["e"], 0.0)) - {"v": 100.0, "s": 100.0, "w": 200.0}.get(ops[i]["line"], 0.0)
     free, est, seq = {}, [0.0] * n, []
     ready = [i for i in range(n) if not need[i]]
     q = lambda e: "g" if e == "net" else e
@@ -537,7 +536,7 @@ def peer(T, rank, kind, t, sign):
 
 
 def name(kind, t, ci):
-    return "zar" + "AB"[ci] if kind == "z" else "arr%d%s" % (t, "AB"[ci])
+    return "zar" + "AB"[ci] if kind == "z" else "thr%d" % t if kind == "h" else "arr%d%s" % (t, "AB"[ci])
 
 
 def emit(g, core, T, topo, ops, seq):
@@ -598,13 +597,13 @@ def relay(g, core, T, topo):
     for rank, src in enumerate(T.cores):
         if core not in topo.cores_of(src):
             continue
-        for kind, t in [("z", 0)] + [("m", t) for t in range(1, NV + 1)]:
+        for kind, t in [("z", 0)] + [(k, t) for t in range(1, NV + 1) for k in "mh"][:-1]:
             dst = peer(T, rank, kind, t, 1)
-            for ci in range(NC):
+            for ci in range(1 if kind == "h" else NC):
                 if routes(src, dst, topo)[ci] != core:
                     continue
                 a, w = span(t, ci)
-                buf = T.zn[:, ci] if kind == "z" else T.inm[:, a:a + w]
+                buf = T.zn[:, ci] if kind == "z" else T.thc[:, 4 * t:4 * t + 4] if kind == "h" else T.inm[:, a:a + w]
                 sem = T.sem[name(kind, t, ci)]
                 g.wait_ge(sem, len(topo.engines(src, core)))
                 rid, pid = topo.addr(dst, core)

@@ -4,71 +4,69 @@ from concourse.mybir import dt, AluOpType, AxisListType, ActivationFunctionType
 A_ = AluOpType
 F_ = ActivationFunctionType
 NV, NC, L2, STEPS = 4, 2, 64, 6
-CUT = {"v": (32, 8, 24), "v0": (32, 32), "v5": (34, 8, 22), "g": (8,) * 8,
-       "s": (18, 46), "s0": (32, 32), "s5": (20, 44), "xA": (30, 34), "xB": (30, 16, 18), "v1": (16, 8, 40), "s1": (8, 56)}
-LP = [64]
-XV = [0, 1]
-OPT = {"late": 5, "t0": True}
-PF = False
+CUT = {"v": (34, 8, 22), "v0": (32, 32), "v1": (16, 8, 24, 16), "v5": (32, 8, 24), "s": (20, 44), "s0": (32, 32), "s1": (14, 50), "s5": (18, 30, 16),
+       "xA": (38, 26), "xB": (30, 16, 10, 8), "gA": (8, 12, 12, 14, 18), "gB": (12, 12, 12, 8, 20)}
+OPT = {"lead": 0, "r1": "gh"}
 ALPHA, GAP, TOP = 0.8, 18, 86.0
 TAU = 5.0 * math.exp(TOP - ALPHA * GAP * 12)
 MID = 2048.0
 BIG = 16384.0
-MX, MS, MG, MR, MW = 0, 64, 128, 192, 256
+MX, MS, MR, MG, MW = 0, 64, 128, 192, 256
 
 SCRATCH = {
     "tev": ("sbuf", [128, 4096], "bfloat16"), "ptab": ("sbuf", [128, 4096], "bfloat16"),
-    "pc": ("sbuf", [128, 256], "int32"), "ti": ("sbuf", [128, 256], "int32"),
-    "dgi": ("sbuf", [128, 6 * 256], "int32"), "dg": ("sbuf", [128, 6 * 256], "bfloat16"),
-    "zi": ("sbuf", [128, 4, 2, 64], "int32"), "li": ("sbuf", [128, 2, 2, 64], "int32"),
+    "pc": ("sbuf", [128, 256], "int32"), "dgi": ("sbuf", [128, 4 * 256], "int32"), "dg": ("sbuf", [128, 6 * 256], "bfloat16"),
+    "zi": ("sbuf", [128, 4, 2, 64], "int32"), "li": ("sbuf", [128, 2, 128], "int32"),
     "zo": ("sbuf", [128, 2, 192], "float16"), "zn": ("sbuf", [128, 2, 192], "float16"),
     "sgi": ("sbuf", [128, 512], "int32"), "sgb": ("sbuf", [128, 512], "float16"),
-    "inm": ("sbuf", [128, 10 * MW], "uint16"), "som": ("sbuf", [128, 8 * MW], "uint16"),
+    "inm": ("sbuf", [128, 8 * MW], "uint16"), "som": ("sbuf", [128, 6 * MW], "uint16"),
+    "fo": ("sbuf", [128, 4, 64], "float32"), "yo": ("sbuf", [128, 4, 64], "float32"),
     "cnt": ("sbuf", [128, 8], "float32"), "hw0": ("sbuf", [128, 128], "float32"),
-    "yo": ("sbuf", [128, 256], "float32"), "thc": ("sbuf", [128, 16], "float32"), "tho": ("sbuf", [128, 16], "float32"),
-    "pcol": ("sbuf", [128, 16], "int32"), "fcol": ("sbuf", [128, 32], "float32"),
-    "itf": ("sbuf", [128, 144], "bfloat16"), "itg": ("sbuf", [128, 128], "bfloat16"), "it8": ("sbuf", [128, 8], "bfloat16"),
-    "itk": ("sbuf", [128, 8, 8], "bfloat16"),
-    "bo": ("sbuf", [128, 2, 8], "bfloat16"), "wp0": ("sbuf", [128, 8, 4], "bfloat16"), "wp1": ("sbuf", [128, 8, 3], "bfloat16"),
-    "cna": ("sbuf", [128, 2, 8, 8], "bfloat16"), "cne": ("sbuf", [128, 8, 8], "bfloat16"), "cg": ("sbuf", [128, 64], "float16"),
+    "thc": ("sbuf", [128, 16], "float32"), "tho": ("sbuf", [128, 16], "float32"),
+    "pcol": ("sbuf", [128, 8], "int32"), "fcol": ("sbuf", [128, 32], "float32"),
+    "itg": ("sbuf", [128, 128], "bfloat16"), "it8": ("sbuf", [128, 8], "bfloat16"), "itk": ("sbuf", [128, 8, 8], "bfloat16"),
+    "bo": ("sbuf", [128, 2, 8], "bfloat16"), "wp0": ("sbuf", [128, 8, 3], "bfloat16"), "wp1": ("sbuf", [128, 8, 3], "bfloat16"),
+    "wp2": ("sbuf", [128, 8, 2], "bfloat16"), "one": ("sbuf", [128, 64], "bfloat16"),
+    "cna": ("sbuf", [128, 2, 8, 8], "bfloat16"), "cne": ("sbuf", [128, 8, 8], "bfloat16"),
     "w0": ("sbuf", [128, 144], "bfloat16"),
+    "zz": ("sbuf", [128, 8, 17, 8], "float16"), "zc": ("sbuf", [128, 4, 17, 8], "bfloat16"), "dd": ("sbuf", [128, 1536], "bfloat16"),
 }
-for _n in ("ch0", "ch1", "nh0", "nh1"):
-    SCRATCH[_n] = ("sbuf", [128, 64], "float16")
-for _n in ("cb0", "cb1"):
+for _n in ("ch0", "ch1", "nh0", "nh1", "cb0", "cb1", "cg"):
     SCRATCH[_n] = ("sbuf", [128, 64], "bfloat16")
-for _n in ("idh", "ndh", "idB", "ndB", "r8"):
-    SCRATCH[_n] = ("sbuf", [128, 128], "float16")
-for _n in ("idb", "blk", "nbk", "tbk"):
+for _n in ("idb", "ndb", "idB", "ndB", "ihB", "nhB", "n64", "r8", "blk", "nbk", "tbk"):
     SCRATCH[_n] = ("sbuf", [128, 128], "bfloat16")
 for _c in "AB":
     SCRATCH["mh" + _c] = ("sbuf", [128, MW], "float16")
     SCRATCH["off" + _c] = ("sbuf", [128, 64], "uint16")
     for _n in ("ex", "ge", "gg", "gp"):
         SCRATCH[_n + _c] = ("sbuf", [128, 1024], "bfloat16")
-    for _n, _w in (("d1", 192), ("dG", 192), ("dX", 128), ("dS", 128), ("mi", 64), ("nf", 64), ("pu", 64), ("w4", 64), ("w5", 64)):
-        SCRATCH[_n + _c] = ("sbuf", [128, _w], "bfloat16")
+    for _n in ("mi", "nf", "pu", "w4", "w5"):
+        SCRATCH[_n + _c] = ("sbuf", [128, 64], "bfloat16")
     for _n, _w in (("va", 192), ("nx", 192), ("oG", 192), ("oX", 128), ("oS", 128)):
         SCRATCH[_n + _c] = ("sbuf", [128, _w], "float32")
     SCRATCH.update({
-        "ne" + _c: ("sbuf", [128, 17, 8], "float16"), "a0" + _c: ("sbuf", [128, 64], "float16"),
-        "zc4" + _c: ("sbuf", [128, 17, 8], "bfloat16"), "zc5" + _c: ("sbuf", [128, 17, 8], "bfloat16"),
+        "a0" + _c: ("sbuf", [128, 64], "float16"), "n2" + _c: ("sbuf", [128, 64, 2], "bfloat16"), "s2" + _c: ("sbuf", [128, 64, 2], "bfloat16"),
         "pq" + _c: ("sbuf", [128, 64, 2], "bfloat16"), "pg" + _c: ("sbuf", [128, 64, 2], "float16"),
-        "cv" + _c: ("psum", [128, 8, 8, 8], "float32"), "pa" + _c: ("psum", [128, 512] if PF else [128, 2, 8, 8, 4], "float32"),
+        "cv" + _c: ("psum", [128, 8, 8, 8], "float32"), "pa" + _c: ("psum", [128, 2, 8, 8, 4], "float32"),
         "tr" + _c: ("psum", [128, 512], "float32"), "fz" + _c: ("psum", [128, 8, 64], "float32"),
     })
-    for _j in range(3):
-        SCRATCH["zz%d%s" % (_j, _c)] = ("sbuf", [128, 17, 8], "float16")
+DD = {"d1": (0, 192), "dG": (192, 384), "dX": (384, 512), "dS": (512, 640), "d2": (640, 768)}
+PART = {"s": "", "x": "XS", "g": "RG"}
+SEQ = [("s", 0), ("x", 0), ("g", 0), ("s", 1), ("x", 1), ("g", 1), ("h", 0)]
+
+
+def messages():
+    return [("z", 0, 0), ("z", 0, 1)] + [(k, t, ci) for t in range(1, NV + 1) for k, ci in SEQ
+                                         if (k in "sg" if t == NV else PART.get(k, 1))]
+
+
+MSG = [(k, t, ci) for k in "zsxgh" for t in range(5) for ci in range(2)]
 NDMA = 24
-SEMAPHORES = ["v", "s", "p", "q", "loc", "zarA", "zarB", "thr1", "thr2", "thr3"] + ["d%d" % i for i in range(NDMA)] \
-    + ["arr%d%s" % (t, c) for t in range(1, 5) for c in "AB"]
+SEMAPHORES = ["v", "s", "p", "q", "loc"] + ["d%d" % i for i in range(NDMA)] + ["%s%d%d" % m for m in MSG]
 
-SHIFT = {"uv": -150.0, "pmhA": -120.0, "ppgA": -120.0, "pmhB": -120.0, "ppgB": -120.0}
-PAR = {"cyc": 0.9e-3, "pec": 0.55e-3, "lat": 0.2, "gat": 1.3, "net": 5.5, "ev": 9.0, "eps": 0.04}
-
-
-def gath(n):
-    return 0.06 + PAR["gat"] * PAR["cyc"] * n
+SHIFT = {"uv": -150.0, "us": -150.0, "upcol": 0.0, "ucn2": 0.0, "uwarm": 0.0, "pmh": -120.0, "ppg": -120.0, "pmg": -120.0,
+         "0st": -120.0, "1st": -120.0, "2st": -120.0, "3st": -120.0, "4st": -120.0, "5ne": 1.0, "wZ": 1.0, "ww5": 1.0, "fD": 1.0, "fdX": 1.0, "foX": 1.0, "fsoX": 1.0, "fyn": 10.0, "fr2": 10.0, "ftho": 10.0}
+PAR = {"cyc": 0.9e-3, "pec": 0.55e-3, "lat": 0.2, "gat": 1.3, "net": 5.0, "ev": 9.0, "eps": 0.06, "iss": 0.6}
 
 
 def cuts(ws):
@@ -83,18 +81,6 @@ def small(n):
     return max(64, n) * PAR["cyc"]
 
 
-def routes(core, dst, topo):
-    if topo.may_write(core, dst):
-        return [core, core]
-    own = [c for c in topo.cores_of(core) if c != core and topo.may_write(c, dst)]
-    own.sort(key=lambda c: topo.die(c) != topo.die(core))
-    return [own[0], own[1]]
-
-
-def span(t, ci):
-    return (MW * (2 * t + ci), MW) if t < NV else (MW * (2 * t + ci) + MS, 128)
-
-
 def build(T):
     ops = []
     nd = [0]
@@ -103,20 +89,22 @@ def build(T):
     def op(eng, cost, R, W, fn, bank=None, lat=0.0, line=None, after=None):
         ops.append({"e": eng, "c": cost, "R": R, "W": W, "f": fn, "b": bank, "lat": lat, "key": cur[0] + W[0], "line": line, "after": after})
 
-    def v(cost, R, W, fn, bank=None):
-        op("v", cost, R, W, fn, bank)
+    def v(n, R, W, fn, bank=None):
+        op("v", small(n), R, W, fn, bank)
 
-    def s(cost, R, W, fn, bank=None):
-        op("s", cost, R, W, fn, bank)
+    def s(n, R, W, fn, bank=None):
+        op("s", small(n), R, W, fn, bank)
 
-    def gather(eng, lanes, R, W, fn, after=None):
-        op(eng, gath(16 * lanes), R, W, fn, line=eng, after=after)
+    def gather(eng, lanes, R, W, fn, after=None, line=None):
+        op(eng, 0.06 + PAR["gat"] * PAR["cyc"] * 16 * lanes, R, W, fn, line=line or eng, after=after)
 
     def dma(queue, R, W, o, i, dur):
-        k = nd[0]
+        op(queue, 0.1, R, W, lambda q: q.dma_start(o, i), lat=dur, line="d" + queue)
+        ops[-1]["dsem"] = "d%d" % nd[0]
         nd[0] += 1
-        ops.append({"e": queue, "c": 0.1, "R": R, "W": W, "b": None, "lat": dur, "dsem": "d%d" % k, "key": "u" + (W or ["out"])[0],
-                    "f": (lambda q, o=o, i=i: q.dma_start(o, i)), "line": "d" + queue, "after": None})
+
+    def send(msg, R, W, src):
+        op("net", PAR["iss"], R, W, (msg, src), lat=PAR["net"], line="net")
 
     def ts(out, in0, s1, o0, s2=None, o1=None):
         if o1 is None:
@@ -151,105 +139,125 @@ def build(T):
     dma("y", [], ["tev1"], T.tev[64:128, :], T.ev[64:128, :], PAR["ev"])
     dma("y", [], ["zi"], T.zi[:, 1:4], T.z[:, 128:512], PAR["ev"] + 1.5)
     dma("s", [], ["zi0"], T.zi[:, 0], T.z[:, 0:128], PAR["ev"] - 2)
-    dma("s", [], ["liS"], T.li[:, :, 0], T.s0[:], PAR["ev"] - 2)
-    dma("s", [], ["liG"], T.li[:, :, 1], T.g0[:], PAR["ev"] - 2)
+    dma("s", [], ["liS"], T.li[:, 0], T.s0[:], PAR["ev"] - 2)
+    dma("s", [], ["liG"], T.li[:, 1], T.g0[:], PAR["ev"] - 2)
     dma("s", [], ["sgi"], T.sgi[0:8, :], T.sg[:], PAR["ev"] - 2)
 
-    fl = True
-    op("g", 0.2, [], ["pcol0"], lambda q: q.iota(T.pcol[:, 0:1], [[0, 1]], 0, 1))
-    op("g", 0.6, [], ["ti"], lambda q: q.iota(T.ti[:], [[1, 256]], 0, 256))
-    op("g", 0.4, [], ["itf"], lambda q: q.iota(T.itf[:], [[1, 144]], 0, 0, allow_small_or_imprecise_dtypes=fl))
-    op("g", 0.4, [], ["itg"], lambda q: q.iota(T.itg[:], [[1, 8], [0, 16]], 0, 0, allow_small_or_imprecise_dtypes=fl))
-    op("g", 0.2, [], ["it8"], lambda q: q.iota(T.it8[:], [[1, 8]], 0, 0, allow_small_or_imprecise_dtypes=fl))
-    op("g", 0.3, [], ["itk"], lambda q: q.iota(T.itk[:], [[1, 8], [0, 8]], 0, 0, allow_small_or_imprecise_dtypes=fl))
-    v(small(2048), [], ["ptab%d" % d for d in range(6)], ms(T.ptab[:], 1.0))
+    def iota(name, out, pattern, cost):
+        op("g", cost, [], [name], lambda q: q.iota(out, pattern, 0, 0, allow_small_or_imprecise_dtypes=True))
+    DG = lambda d: T.dg[:, 256 * d:256 * d + 256]
+    op("g", 0.15, [], ["pcol0"], lambda q: q.iota(T.pcol[:, 0:1], [[0, 1]], 0, 1))
+    iota("itf", DG(4), [[1, 256]], 0.6)
+    iota("itg", T.itg[:], [[1, 8], [0, 16]], 0.4)
+    iota("it8", T.it8[:], [[1, 8]], 0.15)
+    iota("itk", T.itk[:], [[1, 8], [0, 8]], 0.25)
 
     def icol(j, *a):
-        v(small(1), ["pcol0"], ["pcol%d" % j], ts(T.pcol[:, j:j + 1], T.pcol[:, 0:1], *a))
+        v(1, ["pcol0"], ["pcol%d" % j], ts(T.pcol[:, j:j + 1], T.pcol[:, 0:1], *a))
     icol(1, 4, A_.arith_shift_right)
     icol(2, 1, A_.arith_shift_right, 7, A_.bitwise_and)
     icol(3, 15, A_.bitwise_and)
     icol(4, 7, A_.bitwise_and)
     icol(5, 3, A_.arith_shift_right, 1, A_.bitwise_and)
-    v(small(8), ["pcol%d" % j for j in range(6)], ["fc"], cp(T.fcol[:, 0:6], T.pcol[:, 0:6]))
+    v(8, ["pcol%d" % j for j in range(6)], ["fc"], cp(T.fcol[:, 0:6], T.pcol[:, 0:6]))
     FC = lambda j: T.fcol[:, j:j + 1]
+    for a in (0, 2048):
+        op("v", small(1024), [], ["ptab%d" % d for d in range(6)], ms(T.ptab[:, a:a + 2048], 1.0), after="fc" if a else "pcol5")
 
     def fcol(j, in0, s1, o0, s2=None, o1=None, dep=()):
-        v(small(1), ["fc"] + ["fc%d" % x for x in dep], ["fc%d" % j], ts(FC(j), in0, s1, o0, s2, o1))
+        v(1, ["fc"] + ["fc%d" % x for x in dep], ["fc%d" % j], ts(FC(j), in0, s1, o0, s2, o1))
+
+    def lcol(j, src, scale, bias):
+        s(1, ["fc"], ["fc%d" % j], act(FC(j), FC(src), F_.Copy, bias, scale))
     fcol(8, FC(1), 8.0, A_.mult, FC(4), A_.add)
-    fcol(9, FC(0), 0.5, A_.mult)
-    fcol(11, FC(0), -1.0, A_.add, 0.5, A_.mult)
-    fcol(12, FC(1), 16.0, A_.mult, 16.0, A_.add)
-    fcol(13, FC(5), -1.0, A_.mult, 1.0, A_.add)
-    fcol(14, FC(3), -ALPHA, A_.mult, TOP, A_.add)
+    lcol(9, 0, 0.5, 0.0)
+    lcol(11, 0, 0.5, -0.5)
+    lcol(12, 1, 16.0, 16.0)
+    lcol(13, 5, -1.0, 1.0)
+    lcol(14, 3, -ALPHA, TOP)
     fcol(15, FC(2), 0.0, A_.is_equal, 0.5, A_.mult)
     fcol(16, FC(2), 1.0, A_.is_equal, 2.0 ** -13, A_.mult)
     fcol(17, FC(2), 2.0, A_.is_equal, 0.5, A_.mult)
     fcol(18, FC(3), 6.0, A_.is_equal, -MID, A_.mult)
-    fcol(19, FC(3), 6.0, A_.is_equal, -BIG, A_.mult)
     fcol(20, FC(17), FC(15), A_.subtract, dep=(17, 15))
     fcol(21, FC(17), FC(16), A_.subtract, dep=(17, 16))
     fcol(22, FC(15), FC(16), A_.add, FC(18), A_.add, dep=(15, 16, 18))
     fcol(23, FC(17), 2.0, A_.mult, FC(18), A_.add, dep=(17, 18))
-    fcol(10, FC(22), FC(19), A_.add, dep=(22, 19))
+    fcol(19, FC(15), FC(16), A_.subtract, dep=(15, 16))
+    fcol(10, FC(18), 1.5 * BIG / MID, A_.mult, FC(22), A_.add, dep=(22, 18))
     fcol(24, FC(3), 0.0, A_.is_equal, -0.5, A_.mult)
 
     def sel(name, out, src, col, w=None, dep=()):
         R = [src.split(":")[0], "fc"] + ["fc%d" % x for x in (col,) + tuple(dep) if x > 7]
-        it = T.itf[:, 0:int(src.split(":")[1])] if ":" in src else T[src][:]
-        v(small(1), R, [name], ts(out, it, FC(col), A_.is_equal) if w is None else ts(out, it, FC(col), A_.is_equal, w, A_.mult))
+        it = T.dg[:, 1024:1024 + int(src.split(":")[1])] if ":" in src else T[src][:]
+        v(1, R, [name], ts(out, it, FC(col), A_.is_equal) if w is None else ts(out, it, FC(col), A_.is_equal, w, A_.mult))
+
+    def times(name, src, w):
+        s(T[name].shape[1], [src], [name], act(T[name][:], T[src][:], F_.Copy, 0.0, w))
     for o in range(2):
         sel("bo", T.bo[:, o], "it8", 1)
-    for n, cols in (("wp0", (20, 21, 22, 23)), ("wp1", (20, 21, 10))):
+    for n, cols in (("wp0", (19, 22, 23)), ("wp1", (20, 21, 10))):
         for o, col in enumerate(cols):
             sel(n, T[n][:, :, o], "it8", 1, FC(col), (col,))
-    v(small(64), [], ["cna1"], ms(T.cna[:, 1], 0.0))
-    sel("cna", T.cna[:, 0], "itk", 1, 1.0 / 16)
+    s(8, ["wp0"], ["wp2"], act(T.wp2[:, :, 0], T.wp0[:, :, 0], F_.Copy))
+    s(8, ["wp1"], ["wp2a"], act(T.wp2[:, :, 1], T.wp1[:, :, 2], F_.Copy))
+    s(64, ["itk"], ["one"], act(T.one[:], T.itk[:], F_.Copy, 1.0, 0.0))
+    for n in ("n2A", "n2B", "s2A", "s2B"):
+        v(64, [], [n[0:2] + "z" + n[2]], ms(T[n][:, :, 0], 0.0))
     sel("cne", T.cne[:], "itk", 1, 8.0)
+    for o in range(2):
+        s(64, ["cne"], ["cna"], act(T.cna[:, o], T.cne[:], F_.Copy, 0.0, (1.0 - o) / 128))
     sel("cg", T.cg[:], "itf:64", 8)
-    sel("idB", T.idB[:], "itf:128", 0, BIG)
-    sel("ndB", T.ndB[:], "itf:128", 0, -BIG)
     for h, col in ((0, 9), (1, 11)):
         sel("ch%d" % h, T["ch%d" % h][:], "itf:64", col)
-        sel("nh%d" % h, T["nh%d" % h][:], "itf:64", col, -1.0)
-        sel("cb%d" % h, T["cb%d" % h][:], "itf:64", col, 1.0 / 32)
-    sel("idh", T.idh[:], "itf:128", 0)
-    sel("ndh", T.ndh[:], "itf:128", 0, -1.0)
+        times("nh%d" % h, "ch%d" % h, -1.0)
+        times("cb%d" % h, "ch%d" % h, 1.0 / 32)
     sel("idb", T.idb[:], "itf:128", 0)
+    for n, w in (("ndb", -1.0), ("idB", BIG), ("ndB", -BIG), ("ihB", BIG / 2), ("nhB", -BIG / 2), ("n64", -64.0)):
+        times(n, "idb", w)
     sel("blk", T.blk[:], "itg", 1)
-    sel("nbk", T.nbk[:], "itg", 1, -1.0)
+    times("nbk", "blk", -1.0)
     sel("r8", T.r8[:], "itg", 0)
     sel("w0", T.w0[:], "itf:144", 12)
     sel("tb0", T.tbk[:], "itf:128", 0, 2.0)
-    v(small(256), ["tb0", "nbk"], ["tbk"], tt(T.tbk[:], T.tbk[:], T.nbk[:], A_.add))
-    v(small(128), ["itg", "fc24"], ["hw0"], ts(T.hw0[:], T.itg[:], 0.0, A_.mult, FC(24), A_.add))
+    v(256, ["tb0", "nbk"], ["tbk"], tt(T.tbk[:], T.tbk[:], T.nbk[:], A_.add))
+    s(128, ["itg", "fc24"], ["hw0"], act(T.hw0[:], T.itg[:], F_.Identity, FC(24), 0.0))
     for j, x in enumerate((-74.5, 1.0, -10.5, 0.0)):
-        v(small(1), [], ["th0"], ms(T.thc[:, j:j + 1], x))
-    v(small(1), [], ["cn2"], ms(T.cnt[:, 2:3], -2.0 ** -12))
-    s(1.4, ["cn2"], ["warm"], act(T.cnt[:, 4:5], T.cnt[:, 2:3], F_.Exp))
-    for c in "AB":
-        for n in ("zz0", "zz1", "zz2", "zc4", "zc5", "ne"):
-            v(small(68), [], [n + c], ms(T[n + c][:], 0.0))
-        for n, k in (("d1", 3), ("dG", 3), ("dX", 2), ("dS", 2)):
-            v(small(64), [], [n + "z" + c], ms(T[n + c][:, 0::k], 0.0))
+        s(1, ["fc"], ["th0"], act(T.thc[:, j:j + 1], FC(0), F_.Copy, x, 0.0))
+    s(1, ["fc"], ["cn2"], act(T.cnt[:, 2:3], FC(0), F_.Copy, -2.0 ** -12, 0.0))
+    op("s", 1.4, ["cn2"], ["warm"], act(T.cnt[:, 4:5], T.cnt[:, 2:3], F_.Exp))
+    v(288, [], ["zz0"], ms(T.zz[:, :, 0::2], 0.0))
+    v(144, [], ["zc0"], ms(T.zc[:, :, 0::2], 0.0))
+    v(768, [], ["dd0"], ms(T.dd[:], 0.0))
 
-    for d in (4, 5, 0, 1, 2, 3):
-        src, nm = (T.ti, "ti") if d > 3 else (T.pc, "pc")
-        DI, DG = T.dgi[:, 256 * d:256 * d + 256], T.dg[:, 256 * d:256 * d + 256]
-        v(small(256), [nm], ["dgi%d" % d], ts(DI, src[:], 63 << (6 * (d % 4)), A_.bitwise_and))
-        v(small(256), ["dgi%d" % d], ["dg%d" % d], cp(DG, DI))
-        dma("s", ["dg%d" % d], ["ptab%d" % d], T.ptab[d::16, :], DG, 2.5)
+    v(128, ["itf", "fc"], ["dg5"], ts(DG(5), DG(4), 0.0, A_.mult, FC(3), A_.add))
+    v(128, ["dg5"], ["dg5"], ts(DG(5), DG(5), 256.0, A_.mult))
+    for d in (4, 0, 1, 2, 3, 5):
+        if d < 4:
+            DI = T.dgi[:, 256 * d:256 * d + 256]
+            v(256, ["pc"], ["dgi%d" % d], ts(DI, T.pc[:], 63 << (6 * d), A_.bitwise_and))
+            v(256, ["dgi%d" % d], ["dg%d" % d], cp(DG(d), DI))
+        dma("s", ["itf" if d == 4 else "dg%d" % d], ["ptab%d" % d], T.ptab[d::16, :], DG(d), 2.5)
     PT = ["ptab%d" % d for d in range(6)]
     EV = ["tev0", "tev1"]
 
     for t in range(NV):
-        v(small(128), ["sgi"], ["sgb%d" % t], ts(T.sgb[0:8, 128 * t:128 * t + 128], T.sgi[0:8, 128 * t:128 * t + 128], -MID, A_.add))
+        v(128, ["sgi"], ["sgb%d" % t], ts(T.sgb[0:8, 128 * t:128 * t + 128], T.sgi[0:8, 128 * t:128 * t + 128], -MID, A_.add))
     for ci, c in enumerate("AB"):
-        v(small(192), ["zi"], ["zo" + c], ts(T.zo[:, ci], T.zi[:, 1:4, ci], -MID, A_.add))
-        op("net", 0.4, ["zo" + c], ["zn" + c], ("z", 0, ci, T.zo[:, ci], T.zn[:, ci]), None, 8.0)
+        v(192, ["zi"], ["zo" + c], ts(T.zo[:, ci], T.zi[:, 1:4, ci], -MID, A_.add))
+        send(("z", 0, ci), ["zo" + c], ["zn" + c], T.zo[:, ci])
 
     def slot(t, ci):
         return MW * (2 * t + ci)
+
+    def D(n, ci, first=0, step=1):
+        return T.dd[:, 768 * ci + DD[n][0] + first:768 * ci + DD[n][1]:step]
+
+    def ZZ(j, ci):
+        return T.zz[:, 4 * ci + j]
+
+    def back(z, out, u="ch"):
+        return [(out, z[:, 1:17], T[u + "0"][:]), (out, z[:, 0:16], T[u + "1"][:])]
 
     def arrive(t, ci):
         c = "AB"[ci]
@@ -257,26 +265,28 @@ def build(T):
         cur[0] = "p"
         q0 = slot(t, ci)
         M = lambda a, w=64: T.inm[:, q0 + a:q0 + a + w]
-        kX, kM = "iX%d%s" % (t, c), "iM%d%s" % (t, c)
+        kX, kS, kG = "iX%d%s" % (t, c), "iS%d%s" % (t, c), "iG%d%s" % (t, c)
         if t == 0:
-            v(small(64), ["zi0"], [kX], cp(M(MX), T.zi[:, 0, ci]))
-            v(small(128), ["liS", "liG"], [kM], cp(M(MS, 128), T.li[:, ci]))
-            v(small(64), [], ["iR" + c], ms(M(MR), 0))
+            v(64, ["zi0"], [kX], cp(M(MX), T.zi[:, 0, ci]))
+            v(64, ["liS"], [kS], cp(M(MS), T.li[:, 0, 64 * ci:64 * ci + 64]))
+            v(64, [], ["iR0" + c], ms(M(MR), 0))
+            v(64, ["liG"], [kG], cp(M(MG), T.li[:, 1, 64 * ci:64 * ci + 64]))
         for j, (a, b) in enumerate(cuts(CUT["x" + c])):
-            EX, IN = B("ex")[:, 16 * a:16 * b], T.tev[:].indirect(T.inm[:, q0 + a:q0 + b])
-            if ci in XV and j == 0:
+            EX, IN = B("ex")[:, 16 * a:16 * b], T.tev[:].indirect(M(MX + a, b - a))
+            if j == 0:
                 gather("v", b - a, EV + [kX], ["exv" + c], cp(EX, IN))
             else:
-                gather("s", b - a, EV + [kX], ["ex" + "vs"[j > 0] + c], act(EX, IN, F_.Copy))
-        v(small(128), [kX, kM, "iR" + c], ["mh" + c], ts(B("mh")[:], M(0, MW), -MID, A_.add))
+                gather("s", b - a, EV + [kX], ["exs" + c], act(EX, IN, F_.Copy))
+        v(64, [kX, kS], ["mh" + c], ts(B("mh")[:, 0:MR], M(0, MR), -MID, A_.add))
+        v(64, [kG, "iR%d%s" % (t, c)], ["mg" + c], ts(B("mh")[:, MR:MW], M(MR, 128), -MID, A_.add))
         for h in range(2):
-            v(small(64), [kM, "fc", "fc13"], ["pg" + c], ts(B("pg")[:, :, h], M(MG), -MID, A_.add, FC(13) if h == 0 else FC(5), A_.mult))
+            v(64, [kG, "fc", "fc13"], ["pg" + c], ts(B("pg")[:, :, h], M(MG), -MID, A_.add, FC(13) if h == 0 else FC(5), A_.mult))
         lo = 128 * t + L2 * ci
-        mm(128, ["sgb%d" % t, "r8", "ndh", "mh" + c], ["y" + c],
-           [(B("fz")[:, 0], T.r8[0:8, :], T.sgb[0:8, lo:lo + L2]), (B("fz")[:, 0], T.ndh[:], B("mh")[:, MR:MR + 64])], "fz" + c)
+        mm(128, ["sgb%d" % t, "r8", "ndb", "mg" + c], ["y" + c],
+           [(B("fz")[:, 0], T.r8[0:8, :], T.sgb[0:8, lo:lo + L2]), (B("fz")[:, 0], T.ndb[:], B("mh")[:, MR:MR + 64])], "fz" + c)
         for h in range(2):
-            s(small(64), ["y" + c], ["pq" + c], act(B("pq")[:, :, h], B("fz")[:, 0], F_.Relu, 0.0, 64.0), "fz" + c)
-        s(small(64), ["y" + c, "dSz" + c], ["dS" + c], act(B("dS")[:, 1::2], B("fz")[:, 0], F_.Sign, -0.5), "fz" + c)
+            s(64, ["y" + c], ["pq" + c], act(B("pq")[:, :, h], B("fz")[:, 0], F_.Relu, 0.0, 64.0), "fz" + c)
+        s(64, ["y" + c, "dd0"], ["dS" + c], act(D("dS", ci, 1, 2), B("fz")[:, 0], F_.Sign, -0.5), "fz" + c)
 
     TH = lambda t, j: T.thc[:, 4 * t + j:4 * t + j + 1]
 
@@ -285,120 +295,116 @@ def build(T):
         Y, R2 = T.cvB[:, 6, 0, 0:1], T.cnt[:, 3:4]
         mm(512, ["hw0", "cnA", "cn2"], ["yw"], [(Y, T.hw0[:], T.cnt[:, 2:3]), (Y, T.hw0[:], T.cnt[:, 0:1])], "cvB", True, False)
         mm(256, ["cnB"], ["yn"], [(Y, T.hw0[:], T.cnt[:, 1:2])], "cvB", False, True)
-        v(small(1), ["yn"], ["r2"], ts(R2, Y, 1.5 * 2 ** 24, A_.add, -1.5 * 2 ** 24, A_.add), "cvB")
-        v(small(4), ["yn", "r2", "th0"], ["tho%d" % t], ts(T.tho[:, 4 * t:4 * t + 4], T.thc[:, 0:4], Y, A_.add, R2, A_.subtract), "cvB")
-        op("net", 0.4, ["tho%d" % t], ["th%d" % (t + 1)], ("h", t + 1, 0, T.tho[:, 4 * t:4 * t + 4], T.thc[:, 4 * t + 4:4 * t + 8]), None, PAR["net"])
+        v(1, ["yn"], ["r2"], ts(R2, Y, 1.5 * 2 ** 24, A_.add, -1.5 * 2 ** 24, A_.add), "cvB")
+        v(4, ["yn", "r2", "th0"], ["tho%d" % t], ts(T.tho[:, 4 * t:4 * t + 4], T.thc[:, 0:4], Y, A_.add, R2, A_.subtract), "cvB")
+        send(("h", t + 1, 0), ["tho%d" % t], ["th%d" % (t + 1)], T.tho[:, 4 * t:4 * t + 4])
 
-    def bounds(t, ci, part):
+    def bounds(t, ci):
         c = "AB"[ci]
         B = lambda n: T[n + c]
         cur[0] = "g"
         q0 = slot(t, ci) + MG
-        if part == 0:
-            for a, b in cuts(CUT["g"]):
-                op("v", gath(16 * (b - a)), EV + ["iM%d%s" % (t, c), "exs" + c, "exv" + c], ["gg" + c],
-                   tt(B("gg")[:, 16 * a:16 * b], T.tev[:].indirect(T.inm[:, q0 + a:q0 + b]), B("ex")[:, 16 * a:16 * b], A_.is_ge), line="w")
-            return
+        for a, b in cuts(CUT["g" + c]):
+            gather("v", b - a, EV + ["iG%d%s" % (t, c), "exs" + c, "exv" + c], ["gg" + c],
+                   tt(B("gg")[:, 16 * a:16 * b], T.tev[:].indirect(T.inm[:, q0 + a:q0 + b]), B("ex")[:, 16 * a:16 * b], A_.is_ge),
+                   "w4A" if ci and OPT["lead"] else None, "w")
         CG, FM = B("fz")[:, 1], B("fz")[:, 2]
         for j in range(4):
             mm(256, ["gg" + c, "w0"], ["cG%d%s" % (j, c)],
                [(CG, T.w0[:, 16 - k:144 - k], B("gg")[:, k::16]) for k in range(4 * j, 4 * j + 4)], "fz" + c, j == 0, j == 3)
-        s(small(64), ["cG3" + c, "th%d" % t], ["mi" + c], act(B("mi")[:], CG, F_.Sign, TH(t, 2)), "fz" + c)
+        s(64, ["cG3" + c, "th%d" % t], ["mi" + c], act(B("mi")[:], CG, F_.Sign, TH(t, 2)), "fz" + c)
         mm(128, ["mi" + c, "pq" + c, "nbk", "idb"], ["fm" + c], [(FM, T.idb[:], B("pq")[:, :, 0]), (FM, T.nbk[:], B("mi")[:])], "fz" + c)
-        s(small(64), ["fm" + c], ["nf" + c], act(B("nf")[:], FM, F_.Relu, 7.5, 0.5), "fz" + c)
-        s(small(64), ["fm" + c], ["pu" + c], act(B("pu")[:], FM, F_.Relu, -57.0), "fz" + c)
+        s(64, ["fm" + c], ["nf" + c], act(B("nf")[:], FM, F_.Relu, 7.5, 0.5), "fz" + c)
+        s(64, ["fm" + c], ["pu" + c], act(B("pu")[:], FM, F_.Relu, -57.0), "fz" + c)
 
-    def back(i, c, out, u="ch"):
-        ZZ = T["zz%d%s" % (i % 3, c)]
-        return [(out, ZZ[:, 1:17], T[u + "0"][:]), (out, ZZ[:, 0:16], T[u + "1"][:])]
-
-    def gathers(t, i, ci):
-        c = "AB"[ci]
+    def step(t, i, ci, other):
+        c, o = "AB"[ci], "AB"[1 - ci]
         B = lambda n: T[n + c]
         cur[0] = str(i)
         q0 = slot(t, ci) + MS
-        off, kF = (T.inm[:, q0:q0 + 64], "iM%d%s" % (t, c)) if i == 0 else (B("off"), "off" + c)
-        o, io = "AB"[1 - ci], i - 1 + ci
-        turn = (i, ci) > (0, 0) and (i > 0 or OPT["t0"])
-        name = "v5" if (i, ci) == (STEPS - 1, 1) else "v1" if (i, ci) == (0, 1) else "v" if turn else "v0"
-        for j, (a, b) in enumerate(cuts(CUT["s" + name[1:]])):
+        off, kF = (T.inm[:, q0:q0 + 64], "iS%d%s" % (t, c)) if i == 0 else (B("off"), "off" + c)
+        turn = other is not None
+        name = "5" if (i, ci) == (STEPS - 1, 1) else "1" if (i, ci) == (0, 1) else "" if turn else "0"
+        for j, (a, b) in enumerate(cuts(CUT["s" + name])):
             gather("s", b - a, PT + [kF], ["gp" + c], act(B("gp")[:, 16 * a:16 * b], T.ptab[:].indirect(off[:, a:b]), F_.Copy),
                    "d1" + o if turn and j == 1 else None)
-        for j, (a, b) in enumerate(cuts(CUT[name])):
-            after = (None, "nx" + o, "zz%d%s" % (io % 3, o), None, None)[j] if turn else None
-            gather("v", b - a, EV + [kF, "exs" + c, "exv" + c], ["ge%d%s" % (k, c) for k, (x, y) in enumerate(cuts(LP)) if x < b and a < y],
-                   tt(B("ge")[:, 16 * a:16 * b], T.tev[:].indirect(off[:, a:b]), B("ex")[:, 16 * a:16 * b], A_.is_ge), after)
-
-    def step(t, i, ci):
-        c = "AB"[ci]
-        B = lambda n: T[n + c]
-        cur[0] = str(i)
+        for j, (a, b) in enumerate(cuts(CUT["v" + name])):
+            gather("v", b - a, EV + [kF, "exs" + c, "exv" + c], ["ge" + c],
+                   tt(B("ge")[:, 16 * a:16 * b], T.tev[:].indirect(off[:, a:b]), B("ex")[:, 16 * a:16 * b], A_.is_ge),
+                   (None, "nx" + o, "zz%d%s" % (other % 3, o), None, None)[j] if turn else None)
         kz = lambda j: "zz%d%s" % (j % 3, c)
-        ZZ, X, E = T[kz(i)][:, 1::2], B("cv")[:, 0:2], B("pa")[:, 256:320] if PF else B("pa")[:, 1, :, :, 0]
-        pre, NE = [(X, B("pq")[:], T.cna[:])], B("ne")[:, 1::2]
-        cov = lambda a, b: [(B("cv")[2 * a:2 * b, 0:2, :, k], B("ge")[:, 16 * a + k:16 * b:8], T.bo[:]) for k in range(8)]
-        nf, wp = (3, "wp1") if i else (4, "wp0")
-        if PF:
-            PX = lambda f: B("pa")[:, f:192:3] if f < 3 else B("pa")[:, 192:256]
-            par = [(PX(f)[:, k::8], B("gp")[:, k::8], T[wp][:, :, f]) for k in range(8) for f in range(nf)]
-        else:
-            PX = lambda f: B("pa")[:, 0, :, :, f]
-            par = [(B("pa")[:, 0, :, k, 0:nf], B("gp")[:, k::8], T[wp][:]) for k in range(8)]
+        last = i == STEPS - 1
+        Z, X, E = ZZ(i % 3, ci), B("cv")[:, 0:2], B("pa")[:, 1, :, :, 0]
+        NE = lambda j: ZZ(3, ci)[:, 1::2] if j >= STEPS - 2 else B("n2")[:, :, 1]
+        ST = B("s2")[:, :, 1]
+        PX = lambda f: B("pa")[:, 0, :, :, f]
+        n = 3 if last else 2
+        wp = "wp1" if last else "wp2" if i else "wp0"
+        par = [(B("pa")[:, 0, :, k, 0:T[wp].shape[2]], B("gp")[:, k::8], T[wp][:]) for k in range(8)]
+        pre = [(X, B("pq")[:], T.cna[:])]
         if i == 0:
+            mm(512, ["gp" + c, wp], ["pa" + c], par, "pa" + c)
             mm(128, ["pg" + c, "cg", "pq" + c, "cne"], ["gE" + c], [(E, B("pg")[:], T.cg[:]), (E, B("pq")[:], T.cne[:])], "pa" + c)
-            mm(64 * len(par), ["gp" + c, wp], ["pa" + c], par, "pa" + c)
         else:
-            ka, AP = ("a0" + c, B("a0")[:]) if i == 1 else (kz(i - 2), T[kz(i - 2)][:, 1::2])
-            mm(128, [ka, "ne" + c, "idh", "ndB"], ["pw" + c], [(PX(3), T.idh[:], AP), (PX(3), T.ndB[:], NE)], "pa" + c, True, False)
-            mm(64 * len(par) + 64, ["gp" + c, wp, "idB"], ["pa" + c], par + [(PX(2), T.idB[:], NE)], "pa" + c, False, True)
-        mm(128, ["pq" + c, "cna", "cna1"], ["cw" + c], pre, "cv" + c, True, False)
-        for j, (a, b) in enumerate(cuts(LP)):
-            mm(8 * min(64, 2 * (b - a)), ["ge%d%s" % (j, c), "bo"], ["cv" + c if b == L2 else "cw" + c], cov(a, b), "cv" + c, False, b == L2,
-               "aL" + "AB"[1 - ci] if 0 < 2 * i + ci < 2 * STEPS - 1 and j == max(len(LP) - 2, 0) else None)
-        if not PF:
-            s(small(192), ["pa" + c], ["va" + c], act(B("va")[:], B("pa")[:, 0, :, :, 0:3], F_.Copy), "pa" + c)
-        s(small(64), ["cv" + c, "d1z" + c], ["d1" + c], act(B("d1")[:, 2::3], X[:, 1], F_.Sign, -7.5), "cv" + c)
-        s(small(64), ["cv" + c, "d1z" + c, "th%d" % t], ["d1" + c], act(B("d1")[:, 1::3], X[:, 0], F_.Sign, TH(t, 0)), "cv" + c)
+            ka, AP = ("a0" + c, B("a0")[:]) if i == 1 else (kz(i - 2), ZZ((i - 2) % 3, ci)[:, 1::2])
+            lst = [(PX(3), T.idb[:], AP), (PX(3), T.ihB[:], T.one[:]), (PX(3), T.ndB[:], NE(i - 1)), (PX(3), T.ihB[:], ST)]
+            down = [(PX(2), T.idB[:], NE(i - 1)), (PX(2), T.nhB[:], ST)] if last else \
+                [(B("pa")[:, 0, :, :, 0:2], T.idB[:], B("n2")[:]), (B("pa")[:, 0, :, :, 0:2], T.nhB[:], B("s2")[:])]
+            mm(256, [ka, "ne" + c, "st" + c, "idb", "ndB", "ihB", "one"], ["pw" + c], lst, "pa" + c, True, False)
+            if last:
+                mm(640, ["gp" + c, wp, wp + "a", "idB", "nhB"], ["pa" + c], par + down, "pa" + c, False, True)
+            else:
+                mm(256, ["ne" + c, "st" + c, "idB", "nhB"], ["pw" + c], down, "pa" + c, False, False)
+                mm(512, ["gp" + c, wp, wp + "a"], ["pa" + c], par, "pa" + c, False, True)
+            pre += [(X[:, 0], T.n64[:], T.one[:]), (X[:, 0], T.n64[:], ST)]
+        mm(256 if i else 128, ["pq" + c, "cna", "n64", "one"] + ["st" + c] * (i > 0), ["cw" + c], pre, "cv" + c, True, False)
+        mm(512, ["ge" + c, "bo"], ["cv" + c], [(X[:, :, :, k], B("ge")[:, k::8], T.bo[:]) for k in range(8)], "cv" + c, False, True,
+           "aL" + o if turn and other < STEPS - 1 else None)
+        dn = "d1" if last else "d2"
+        s(64 * n, ["pa" + c], ["va" + c], act(B("va")[:, 0:64 * n], B("pa")[:, 0, :, :, 0:n], F_.Copy), "pa" + c)
+        s(64, ["cv" + c, "dd0"], ["d1" + c], act(D(dn, ci, n - 1, n), X[:, 1], F_.Sign, -7.5), "cv" + c)
+        if last:
+            s(64, ["cv" + c, "dd0", "th%d" % t], ["d1" + c], act(D(dn, ci, 1, 3), X[:, 0], F_.Sign, TH(t, 0)), "cv" + c)
         if i >= STEPS - 2:
-            s(small(64), ["cv" + c, "th%d" % t], ["zc%d%s" % (i, c)], act(B("zc%d" % i)[:, 1::2], X[:, 0], F_.Identity, TH(t, 1)), "cv" + c)
-        if PF:
-            v(small(192), ["d1" + c, "pa" + c], ["nx" + c], scan(B("nx")[:], B("d1")[:], B("pa")[:, 0:192]), "pa" + c)
-        else:
-            v(small(192), ["d1" + c, "va" + c], ["nx" + c], scan(B("nx")[:], B("d1")[:], B("va")[:]))
-        if i == STEPS - 1:
-            v(small(64), ["nx" + c, "gE" + c], ["ne" + c], tt(NE, B("nx")[:, 2::3], E, A_.not_equal), "pa" + c)
+            s(64, ["cv" + c, "th%d" % t, "zc0"], ["zc%d%s" % (i, c)], act(T.zc[:, 2 * ci + i % 2, 1::2], X[:, 0], F_.Identity, TH(t, 1)), "cv" + c)
+        if not last:
+            s(64, ["cv" + c, "s2z" + c, "th%d" % t], ["st" + c], act(ST, X[:, 0], F_.Sign, TH(t, 0)), "cv" + c)
+        NX = B("nx")[:, n - 1:64 * n:n]
+        v(64 * n, ["d1" + c, "va" + c], ["nx" + c], scan(B("nx")[:, 0:64 * n], D(dn, ci), B("va")[:, 0:64 * n]))
+        if last:
+            v(64, ["nx" + c, "gE" + c], ["ne" + c], tt(NE(i), NX, E, A_.not_equal), "pa" + c)
         if i == 0:
-            v(small(64), ["nx" + c], [kz(i)], cp(ZZ, B("nx")[:, 2::3]))
-            v(small(64), ["pa" + c], ["a0" + c], cp(B("a0")[:], PX(3)), "pa" + c)
+            v(64, ["nx" + c, "zz0"], [kz(i)], cp(Z[:, 1::2], NX))
+            v(64, ["pa" + c], ["a0" + c], cp(B("a0")[:], PX(2)), "pa" + c)
         else:
-            v(small(64), ["nx" + c, "pa" + c], [kz(i)], tt(ZZ, B("nx")[:, 2::3], PX(3), A_.max), "pa" + c)
-        if i < STEPS - 1:
-            mm(128, [kz(i), "ch0", "ch1"], ["aL" + c], back(i, c, B("tr")[:, 0:64]), "tr" + c)
-            v(small(64), ["aL" + c], ["off" + c], ts(B("off")[:], B("tr")[:, 0:64], MID, A_.add), "tr" + c)
-            v(small(64), [kz(i), "gE" + c], ["ne" + c], tt(NE, ZZ, E, A_.not_equal), "pa" + c)
+            v(64, ["nx" + c, "pa" + c], [kz(i)], tt(Z[:, 1::2], NX, PX(3), A_.max), "pa" + c)
+        if not last:
+            mm(128, [kz(i), "ch0", "ch1"], ["aL" + c], back(Z, B("tr")[:, 0:64]), "tr" + c)
+            v(64, ["aL" + c], ["off" + c], ts(B("off")[:], B("tr")[:, 0:64], MID, A_.add), "tr" + c)
+            v(64, [kz(i), "gE" + c, "n2z" + c], ["ne" + c], tt(NE(i), Z[:, 1::2], E, A_.not_equal), "pa" + c)
         F = lambda j: B("tr")[:, 64 + j:256:3] if j < 3 else B("tr")[:, 253 + j:384:2] if j < 5 else B("tr")[:, 379 + j:512:2]
         MH = lambda a: B("mh")[:, a:a + 64]
         if i == STEPS - 2:
-            lst = back(i, c, F(0), "nh") + back(i, c, F(2)) \
-                + [(F(1), T.ndh[:], MH(MG)), (F(2), T.idh[:], MH(MG)), (F(5), T.ndh[:], MH(MS)), (F(6), T.idh[:], MH(MS))]
+            lst = back(Z, F(0), "nh") + back(Z, F(2)) \
+                + [(F(1), T.ndb[:], MH(MG)), (F(2), T.idb[:], MH(MG)), (F(5), T.ndb[:], MH(MS)), (F(6), T.idb[:], MH(MS))]
             if t < NV - 1:
                 ZN = T.zn[:, ci, 64 * t:64 * t + 64]
-                lst += [(F(3), T.ndh[:], MH(MX)), (F(4), T.idh[:], MH(MX)), (F(3), T.idh[:], ZN), (F(4), T.idh[:], ZN)]
+                lst += [(F(3), T.ndb[:], MH(MX)), (F(4), T.idb[:], MH(MX)), (F(3), T.idb[:], ZN), (F(4), T.idb[:], ZN)]
             for j in range(0, len(lst), 4):
-                mm(256, [kz(i), "nh0", "nh1", "mh" + c, "zn" + c], ["fw" + c], lst[j:j + 4], "tr" + c, j == 0, False)
+                mm(256, [kz(i), "nh0", "nh1", "mh" + c, "mg" + c, "zn" + c], ["fw" + c], lst[j:j + 4], "tr" + c, j == 0, False)
         if i == STEPS - 1:
-            mm(256, [kz(i)], ["fv" + c], back(i, c, F(5)) + back(i, c, F(6)), "tr" + c, False, False)
-            mm(256, [kz(i)], ["fv" + c], back(i, c, F(0)) + back(i, c, F(1)), "tr" + c, False, True)
+            mm(256, [kz(i)], ["fv" + c], back(Z, F(5)) + back(Z, F(6)), "tr" + c, False, False)
+            mm(256, [kz(i)], ["fv" + c], back(Z, F(0)) + back(Z, F(1)), "tr" + c, False, True)
 
     def weight(i, ci):
         c = "AB"[ci]
         B = lambda n: T[n + c]
         cur[0] = "w"
-        Z, ww, ZC = B("fz")[:, i - 1], "w%d" % i, B("zc%d" % i)
+        Z, ww = B("fz")[:, i - 1], "w%d" % i
         mm(192, ["zc%d%s" % (i, c), "cb0", "cb1", "nf" + c, "idb"], ["zw" + c],
-           [(Z, T.idb[:], B("nf")[:]), (Z, ZC[:, 1:17], T.cb0[:]), (Z, ZC[:, 0:16], T.cb1[:])], "fz" + c, True, False)
-        mm(128, ["ne" + c, "ch0", "ch1"], ["Z" + c], [(Z, B("ne")[:, 1:17], T.ch0[:]), (Z, B("ne")[:, 0:16], T.ch1[:])], "fz" + c, False, True)
-        s(small(64), ["Z" + c, "fc14"], [ww + c], act(B(ww)[:], Z, F_.Exp, FC(14), -ALPHA * GAP * 32), "fz" + c)
+           [(Z, T.idb[:], B("nf")[:])] + back(T.zc[:, 2 * ci + i % 2], Z, "cb"), "fz" + c, True, False)
+        mm(128, ["ne" + c, "ch0", "ch1"], ["Z" + c], back(ZZ(3, ci), Z), "fz" + c, False, True)
+        s(64, ["Z" + c, "fc14"], [ww + c], act(B(ww)[:], Z, F_.Exp, FC(14), -ALPHA * GAP * 32), "fz" + c)
 
     def finish(t, ci):
         c = "AB"[ci]
@@ -412,51 +418,53 @@ def build(T):
         mm(64 * len(lst), ["pu" + c, "nf" + c, "w4" + c, "tbk", "blk", "idb"], ["dw" + c], lst, "cv" + c, True, False)
         lst = [(D4, T.nbk[:], B("w5")[:]), (D45, T.tbk[:], B("w5")[:])] + ([(RD, T.blk[:], B("w5")[:])] if more else [])
         mm(64 * len(lst), ["w5" + c], ["D" + c], lst, "cv" + c, False, True)
-        so = lambda a: T.som[:, slot(t, ci) + a:slot(t, ci) + a + 64]
-        kM = "so%d%s" % (t, c)
-        v(small(128), ["dS" + c, "fv" + c], ["oS" + c], scan(B("oS")[:], B("dS")[:], B("tr")[:, 384:512]), "tr" + c)
-        v(small(64), ["oS" + c], [kM + "S"], ts(so(MS), B("oS")[:, 1::2], 0.5, A_.mult, MID, A_.add))
-        for j, D in enumerate((D4, D45)):
-            s(small(64), ["D" + c, "dGz" + c], ["dG" + c], act(B("dG")[:, 1 + j::3], D, F_.Sign, -TAU), "cv" + c)
-        v(small(192), ["dG" + c, "fv" + c], ["oG" + c], scan(B("oG")[:], B("dG")[:], B("tr")[:, 64:256]), "tr" + c)
-        v(small(64), ["oG" + c], [kM + "G"], ts(so(MG), B("oG")[:, 2::3], 0.5, A_.mult, MID, A_.add))
-        R = [kM + "S", kM + "G"]
+        q0, q1, k = slot(t, ci), slot(t + 1, ci), "%d%s" % (t, c)
+        so = lambda a: T.som[:, q0 + a:q0 + a + 64] if more else T.fo[:, 2 * ci + (a == MG)]
+        out = lambda a, x: ts(so(a), x, 0.5, A_.mult, MID, A_.add)
+        v(128, ["dS" + c, "fv" + c], ["oS" + c], scan(B("oS")[:], D("dS", ci), B("tr")[:, 384:512]), "tr" + c)
+        v(64, ["oS" + c], ["soS" + k], out(MS, B("oS")[:, 1::2]))
+        if not more:
+            send(("s", NV, ci), ["soS" + k], ["yS" + c], so(MS))
         if more:
-            s(small(64) + 0.02, ["D" + c, "dXz" + c], ["dX" + c, "cn" + c],
-              lambda q: q.activation(B("dX")[:, 1::2], RD, F_.Sign, bias=-TAU, accum_out=T.cnt[:, ci:ci + 1]), "cv" + c)
-            v(small(128), ["dX" + c, "fv" + c], ["oX" + c], scan(B("oX")[:], B("dX")[:], B("tr")[:, 256:384]), "tr" + c)
-            v(small(64), ["dX" + c], [kM + "R"], ts(so(MR), B("dX")[:, 1::2], 0.0, A_.is_lt))
-            v(small(64), ["oX" + c], [kM + "X"], ts(so(MX), B("oX")[:, 1::2], 0.5, A_.mult, MID, A_.add))
-            R += [kM + "X", kM + "R"]
-        a, w = span(t + 1, ci)
-        op("net", 0.4, R, ["iX%d%s" % (t + 1, c), "iM%d%s" % (t + 1, c), "iR" + c],
-           ("m", t + 1, ci, T.som[:, a - 2 * MW:a - 2 * MW + w], T.inm[:, a:a + w]), None, PAR["net"])
+            s(84, ["D" + c, "dd0"], ["dX" + c, "cn" + c],
+              lambda q: q.activation(D("dX", ci, 1, 2), RD, F_.Sign, bias=-TAU, accum_out=T.cnt[:, ci:ci + 1]), "cv" + c)
+            v(128, ["dX" + c, "fv" + c], ["oX" + c], scan(B("oX")[:], D("dX", ci), B("tr")[:, 256:384]), "tr" + c)
+            v(64, ["oX" + c], ["soX" + k], out(MX, B("oX")[:, 1::2]))
+            v(64, ["dX" + c], ["soR" + k], ts(so(MR), D("dX", ci, 1, 2), 0.0, A_.is_lt))
+        for j, x in enumerate((D4, D45)):
+            s(64, ["D" + c, "dd0"], ["dG" + c], act(D("dG", ci, 1 + j, 3), x, F_.Sign, -TAU), "cv" + c)
+        v(192, ["dG" + c, "fv" + c], ["oG" + c], scan(B("oG")[:], D("dG", ci), B("tr")[:, 64:256]), "tr" + c)
+        v(64, ["oG" + c], ["soG" + k], out(MG, B("oG")[:, 2::3]))
+        if not more:
+            send(("g", NV, ci), ["soG" + k], ["yG" + c], so(MG))
 
+    def hand_on(t):
+        for kind, t1, ci in messages():
+            if t1 == t + 1 and kind == "h":
+                threshold(t)
+            elif t1 == t + 1:
+                a = slot(t, ci) + 64 * "XSRG".index(PART[kind][0])
+                send((kind, t1, ci), ["so%s%d%s" % (n, t, "AB"[ci]) for n in PART[kind]], ["i%s%d%s" % (n, t1, "AB"[ci]) for n in PART[kind]],
+                     T.som[:, a:a + 64 * len(PART[kind])])
+
+    lead = OPT["lead"]
+    turns = [(i - ci * lead, ci) for i in range(STEPS + lead) for ci in range(NC) if 0 <= i - ci * lead < STEPS]
     for t in range(NV):
-        arrive(t, 0)
-        gathers(t, 0, 0)
-        bounds(t, 0, 0)
-        arrive(t, 1)
-        for i in range(STEPS):
-            for ci in range(NC):
-                if (i, ci) != (0, 0):
-                    gathers(t, i, ci)
-                if (i, ci) == (0, 1):
-                    bounds(t, 1, 0)
-                step(t, i, ci)
-                if i == 0:
-                    bounds(t, ci, 1)
-                if i >= STEPS - 2:
-                    weight(i, ci)
-                if i == STEPS - 1:
-                    finish(t, ci)
+        for n, (i, ci) in enumerate(turns):
+            if i == 0:
+                arrive(t, ci)
+            step(t, i, ci, turns[n - 1][0] if n and turns[n - 1][1] != ci else None)
+            if i == (STEPS - 2 if ci and lead else 0):
+                bounds(t, ci)
+            if i >= STEPS - 2:
+                weight(i, ci)
+            if i == STEPS - 1:
+                finish(t, ci)
         if t < NV - 1:
-            threshold(t)
+            hand_on(t)
     for ci, c in enumerate("AB"):
-        q0 = slot(NV, ci) + MS
-        v(small(128), ["iM4" + c], ["yo" + c], cp(T.yo[:, 128 * ci:128 * ci + 128], T.inm[:, q0:q0 + 128]))
         for j in range(2):
-            dma("ys"[j], ["yo" + c], [], (T.ys, T.yg)[j][:, 64 * ci:64 * ci + 64], T.yo[:, 128 * ci + 64 * j:128 * ci + 64 * j + 64], 2.0)
+            dma("ys"[j], ["y" + "SG"[j] + c], ["out"], (T.ys, T.yg)[j][:, 64 * ci:64 * ci + 64], T.yo[:, 2 * ci + j], 2.0)
     return ops
 
 
@@ -472,7 +480,7 @@ def link(ops):
             if piece:
                 wr[k] = old + [n]
             else:
-                base[k] = set(old) | set(rd.get(k, ()))
+                base[k] = set(old) | set(rd.get(k, ())) if k != "out" else set()
                 wr[k] = [n]
                 rd[k] = []
             d.update(base[k])
@@ -510,14 +518,15 @@ def order(ops):
     for i in range(n - 1, -1, -1):
         pri[i] = ops[i]["c"] + max([pri[j] + gap for j, gap in suc[i]] or [ops[i]["lat"]])
     for i in range(n):
-        pri[i] += SHIFT.get(ops[i]["key"], SHIFT.get(ops[i]["key"][0] + ops[i]["e"], 0.0)) - {"v": 100.0, "s": 100.0, "w": 200.0}.get(ops[i]["line"], 0.0)
+        k = ops[i]["key"]
+        pri[i] += ([SHIFT[x] for x in (k, k[:-1], k[:-2], k[0] + ops[i]["e"]) if x in SHIFT] + [0.0])[0] - {"v": 100.0, "s": 100.0, "w": 200.0}.get(ops[i]["line"], 0.0)
     free, est, seq = {}, [0.0] * n, []
     ready = [i for i in range(n) if not need[i]]
     q = lambda e: "g" if e == "net" else e
     while ready:
         first = min((max(est[i], free.get(q(ops[i]["e"]), 0.0)), -pri[i], i) for i in ready)
         tm, eng = first[0], q(ops[first[2]]["e"])
-        cand = [i for i in ready if q(ops[i]["e"]) == eng and max(est[i], free.get(eng, 0.0)) <= tm + PAR.get("eps", 0.02)]
+        cand = [i for i in ready if q(ops[i]["e"]) == eng and max(est[i], free.get(eng, 0.0)) <= tm + PAR["eps"]]
         b = max(cand, key=lambda i: (pri[i], -i))
         free[eng] = max(est[b], free.get(eng, 0.0)) + ops[b]["c"]
         ready.remove(b)
@@ -530,13 +539,30 @@ def order(ops):
     return seq
 
 
-def peer(T, rank, kind, t, sign):
-    step = -1 if kind == "z" else (1 if t < NV else 1 - NV)
+def peer(T, rank, msg, sign):
+    step = -1 if msg[0] == "z" else (1 if msg[1] < NV else 1 - NV)
     return T.cores[(rank + sign * step) % len(T.cores)]
 
 
-def name(kind, t, ci):
-    return "zar" + "AB"[ci] if kind == "z" else "thr%d" % t if kind == "h" else "arr%d%s" % (t, "AB"[ci])
+def route(src, dst, msg, topo):
+    if topo.may_write(src, dst):
+        return src
+    own = [c for c in topo.cores_of(src) if c != src and topo.may_write(c, dst)]
+    own.sort(key=lambda c: topo.die(c) != topo.die(src))
+    return own[msg[2] if msg[0] == "z" else int(msg[0] in OPT["r1"])]
+
+
+def landing(T, msg):
+    kind, t, ci = msg
+    if kind == "z":
+        return T.zn[:, ci]
+    if kind == "h":
+        return T.thc[:, 4 * t:4 * t + 4]
+    if t == NV:
+        return T.yo[:, 2 * ci + (kind == "g")]
+    q0 = MW * (2 * t + ci)
+    a = q0 + 64 * "XSRG".index(PART[kind][0])
+    return T.inm[:, a:a + 64 * len(PART[kind])]
 
 
 def emit(g, core, T, topo, ops, seq):
@@ -565,15 +591,14 @@ def emit(g, core, T, topo, ops, seq):
                     if kn.get(k2, 0) < v2:
                         kn[k2] = v2
         if o["e"] == "net":
-            kind, t, ci, src, land = o["f"]
-            dst, frm = peer(T, rank, kind, t, 1), peer(T, rank, kind, t, -1)
-            via = routes(core, dst, topo)[ci]
+            msg, src = o["f"]
+            dst, frm = peer(T, rank, msg, 1), peer(T, rank, msg, -1)
+            via = route(core, dst, msg, topo)
             to = dst if via == core else via
-            sem = name(kind, t, ci)
             rid, pid = topo.addr(to, core)
-            g.remote_dma(land, src, T.sem[sem], T.sem.loc, pid, rid, topo.mask(core, to))
+            g.remote_dma(landing(T, msg), src, T.sem["%s%d%d" % msg], T.sem.loc, pid, rid, topo.mask(core, to))
             loc += len(topo.engines(core, to))
-            o["sig"] = (sem, len(topo.engines(routes(frm, core, topo)[ci], core)), {})
+            o["sig"] = ("%s%d%d" % msg, len(topo.engines(route(frm, core, msg, topo), core)), {})
         elif "dsem" in o:
             o["f"](q).then_inc(T.sem[o["dsem"]], 16)
             o["sig"] = (o["dsem"], 16, dict(kn))
@@ -595,19 +620,13 @@ def emit(g, core, T, topo, ops, seq):
 def relay(g, core, T, topo):
     loc = 0
     for rank, src in enumerate(T.cores):
-        if core not in topo.cores_of(src):
-            continue
-        for kind, t in [("z", 0)] + [(k, t) for t in range(1, NV + 1) for k in "mh"][:-1]:
-            dst = peer(T, rank, kind, t, 1)
-            for ci in range(1 if kind == "h" else NC):
-                if routes(src, dst, topo)[ci] != core:
-                    continue
-                a, w = span(t, ci)
-                buf = T.zn[:, ci] if kind == "z" else T.thc[:, 4 * t:4 * t + 4] if kind == "h" else T.inm[:, a:a + w]
-                sem = T.sem[name(kind, t, ci)]
+        for msg in messages() if core in topo.cores_of(src) else []:
+            dst = peer(T, rank, msg, 1)
+            if route(src, dst, msg, topo) == core:
+                sem = T.sem["%s%d%d" % msg]
                 g.wait_ge(sem, len(topo.engines(src, core)))
                 rid, pid = topo.addr(dst, core)
-                g.remote_dma(buf, buf, sem, T.sem.loc, pid, rid, topo.mask(core, dst))
+                g.remote_dma(landing(T, msg), landing(T, msg), sem, T.sem.loc, pid, rid, topo.mask(core, dst))
                 loc += len(topo.engines(core, dst))
     if loc:
         g.wait_ge(T.sem.loc, loc)

import math
from concourse.mybir import dt, AluOpType, AxisListType, ActivationFunctionType

A_ = AluOpType
F_ = ActivationFunctionType
NV, NC, L2, STEPS = 4, 2, 64, 6
CUT = {"v": (34, 8, 22), "v0": (32, 32), "v1": (16, 8, 24, 16), "v5": (32, 8, 24), "s": (20, 44), "s0": (32, 32), "s1": (14, 50), "s5": (18, 30, 16),
       "xA": (38, 26), "xB": (30, 16, 10, 8), "gA": (8, 12, 12, 14, 18), "gB": (12, 12, 12, 8, 20)}
OPT = {"lead": 0, "r1": "gh"}
ALPHA, GAP, TOP = 0.8, 18, 86.0
TAU = 5.0 * math.exp(TOP - ALPHA * GAP * 12)
MID = 2048.0
BIG = 16384.0
MX, MS, MR, MG, MW = 0, 64, 128, 192, 256

SCRATCH = {
    "tev": ("sbuf", [128, 4096], "bfloat16"), "ptab": ("sbuf", [128, 4096], "bfloat16"),
    "pc": ("sbuf", [128, 256], "int32"), "dgi": ("sbuf", [128, 4 * 256], "int32"), "dg": ("sbuf", [128, 6 * 256], "bfloat16"),
    "zi": ("sbuf", [128, 4, 2, 64], "int32"), "li": ("sbuf", [128, 2, 128], "int32"),
    "zo": ("sbuf", [128, 2, 192], "float16"), "zn": ("sbuf", [128, 2, 192], "float16"),
    "sgi": ("sbuf", [128, 512], "int32"), "sgb": ("sbuf", [128, 512], "float16"),
    "inm": ("sbuf", [128, 8 * MW], "uint16"), "som": ("sbuf", [128, 6 * MW], "uint16"),
    "fo": ("sbuf", [128, 4, 64], "float32"), "yo": ("sbuf", [128, 4, 64], "float32"),
    "cnt": ("sbuf", [128, 8], "float32"), "hw0": ("sbuf", [128, 128], "float32"),
    "thc": ("sbuf", [128, 16], "float32"), "tho": ("sbuf", [128, 16], "float32"),
    "pcol": ("sbuf", [128, 8], "int32"), "fcol": ("sbuf", [128, 32], "float32"),
    "itg": ("sbuf", [128, 128], "bfloat16"), "it8": ("sbuf", [128, 8], "bfloat16"), "itk": ("sbuf", [128, 8, 8], "bfloat16"),
    "bo": ("sbuf", [128, 2, 8], "bfloat16"), "wp0": ("sbuf", [128, 8, 3], "bfloat16"), "wp1": ("sbuf", [128, 8, 3], "bfloat16"),
    "wp2": ("sbuf", [128, 8, 2], "bfloat16"), "one": ("sbuf", [128, 64], "bfloat16"),
    "cna": ("sbuf", [128, 2, 8, 8], "bfloat16"), "cne": ("sbuf", [128, 8, 8], "bfloat16"),
    "w0": ("sbuf", [128, 144], "bfloat16"),
    "zz": ("sbuf", [128, 8, 17, 8], "float16"), "zc": ("sbuf", [128, 4, 17, 8], "bfloat16"), "dd": ("sbuf", [128, 1536], "bfloat16"),
}
for _n in ("ch0", "ch1", "nh0", "nh1", "cb0", "cb1", "cg"):
    SCRATCH[_n] = ("sbuf", [128, 64], "bfloat16")
for _n in ("idb", "ndb", "idB", "ndB", "ihB", "nhB", "n64", "r8", "blk", "nbk", "tbk"):
    SCRATCH[_n] = ("sbuf", [128, 128], "bfloat16")
for _c in "AB":
    SCRATCH["mh" + _c] = ("sbuf", [128, MW], "float16")
    SCRATCH["off" + _c] = ("sbuf", [128, 64], "uint16")
    for _n in ("ex", "ge", "gg", "gp"):
        SCRATCH[_n + _c] = ("sbuf", [128, 1024], "bfloat16")
    for _n in ("mi", "nf", "pu", "w4", "w5"):
        SCRATCH[_n + _c] = ("sbuf", [128, 64], "bfloat16")
    for _n, _w in (("va", 192), ("nx", 192), ("oG", 192), ("oX", 128), ("oS", 128)):
        SCRATCH[_n + _c] = ("sbuf", [128, _w], "float32")
    SCRATCH.update({
        "a0" + _c: ("sbuf", [128, 64], "float16"), "n2" + _c: ("sbuf", [128, 64, 2], "bfloat16"), "s2" + _c: ("sbuf", [128, 64, 2], "bfloat16"),
        "pq" + _c: ("sbuf", [128, 64, 2], "bfloat16"), "pg" + _c: ("sbuf", [128, 64, 2], "float16"),
        "cv" + _c: ("psum", [128, 8, 8, 8], "float32"), "pa" + _c: ("psum", [128, 2, 8, 8, 4], "float32"),
        "tr" + _c: ("psum", [128, 512], "float32"), "fz" + _c: ("psum", [128, 8, 64], "float32"),
    })
DD = {"d1": (0, 192), "dG": (192, 384), "dX": (384, 512), "dS": (512, 640), "d2": (640, 768)}
PART = {"s": "", "x": "XS", "g": "RG"}
SEQ = [("s", 0), ("x", 0), ("g", 0), ("s", 1), ("x", 1), ("g", 1), ("h", 0)]


def messages():
    return [("z", 0, 0), ("z", 0, 1)] + [(k, t, ci) for t in range(1, NV + 1) for k, ci in SEQ
                                         if (k in "sg" if t == NV else PART.get(k, 1))]


MSG = [(k, t, ci) for k in "zsxgh" for t in range(5) for ci in range(2)]
NDMA = 24
SEMAPHORES = ["v", "s", "p", "q", "loc"] + ["d%d" % i for i in range(NDMA)] + ["%s%d%d" % m for m in MSG]

SHIFT = {"uv": -150.0, "us": -150.0, "upcol": 0.0, "ucn2": 0.0, "uwarm": 0.0, "pmh": -120.0, "ppg": -120.0, "pmg": -120.0,
         "0st": -120.0, "1st": -120.0, "2st": -120.0, "3st": -120.0, "4st": -120.0, "5ne": 1.0, "wZ": 1.0, "ww5": 1.0, "fD": 1.0, "fdX": 1.0, "foX": 1.0, "fsoX": 1.0, "fyn": 10.0, "fr2": 10.0, "ftho": 10.0}
PAR = {"cyc": 0.9e-3, "pec": 0.55e-3, "lat": 0.2, "gat": 1.3, "net": 5.0, "ev": 9.0, "eps": 0.06, "iss": 0.6}


def cuts(ws):
    out = []
    for w in ws:
        a = out[-1][1] if out else 0
        out.append((a, a + w))
    return out


def small(n):
    return max(64, n) * PAR["cyc"]


def build(T):
    ops = []
    nd = [0]
    cur = ["u"]

    def op(eng, cost, R, W, fn, bank=None, lat=0.0, line=None, after=None):
        ops.append({"e": eng, "c": cost, "R": R, "W": W, "f": fn, "b": bank, "lat": lat, "key": cur[0] + W[0], "line": line, "after": after})

    def v(n, R, W, fn, bank=None):
        op("v", small(n), R, W, fn, bank)

    def s(n, R, W, fn, bank=None):
        op("s", small(n), R, W, fn, bank)

    def gather(eng, lanes, R, W, fn, after=None, line=None):
        op(eng, 0.06 + PAR["gat"] * PAR["cyc"] * 16 * lanes, R, W, fn, line=line or eng, after=after)

    def dma(queue, R, W, o, i, dur):
        op(queue, 0.1, R, W, lambda q: q.dma_start(o, i), lat=dur, line="d" + queue)
        ops[-1]["dsem"] = "d%d" % nd[0]
        nd[0] += 1

    def send(msg, R, W, src):
        op("net", PAR["iss"], R, W, (msg, src), lat=PAR["net"], line="net")

    def ts(out, in0, s1, o0, s2=None, o1=None):
        if o1 is None:
            return lambda q: q.tensor_scalar(out, in0, s1, None, o0)
        return lambda q: q.tensor_scalar(out, in0, s1, s2, o0, o1)

    def tt(out, a, b, o):
        return lambda q: q.tensor_tensor(out, a, b, o)

    def cp(out, a):
        return lambda q: q.tensor_copy(out, a)

    def ms(out, x):
        return lambda q: q.memset(out, x)

    def act(out, a, f, bias=0.0, scale=1.0):
        return lambda q: q.activation(out, a, f, bias=bias, scale=scale)

    def scan(out, d0, d1):
        return lambda q: q.tensor_tensor_scan(out, d0, d1, 0.0, A_.mult, A_.add)

    def mm(n, R, W, lst, bank, first=True, last=True, after=None):
        def f(q):
            r = None
            for i, (o, a, b) in enumerate(lst):
                r = q.matmul(o, a, b, first and i == 0, last and i == len(lst) - 1)
            return r
        op("p", n * PAR["pec"], R, W, f, bank, after=after)

    dma("y", [], ["pc"], T.pc[:], T.par[:], 2.3)
    dma("y", [], ["tev0"], T.tev[0:64, :], T.ev[0:64, :], PAR["ev"])
    dma("y", [], ["tev1"], T.tev[64:128, :], T.ev[64:128, :], PAR["ev"])
    dma("y", [], ["zi"], T.zi[:, 1:4], T.z[:, 128:512], PAR["ev"] + 1.5)
    dma("s", [], ["zi0"], T.zi[:, 0], T.z[:, 0:128], PAR["ev"] - 2)
    dma("s", [], ["liS"], T.li[:, 0], T.s0[:], PAR["ev"] - 2)
    dma("s", [], ["liG"], T.li[:, 1], T.g0[:], PAR["ev"] - 2)
    dma("s", [], ["sgi"], T.sgi[0:8, :], T.sg[:], PAR["ev"] - 2)

    def iota(name, out, pattern, cost):
        op("g", cost, [], [name], lambda q: q.iota(out, pattern, 0, 0, allow_small_or_imprecise_dtypes=True))
    DG = lambda d: T.dg[:, 256 * d:256 * d + 256]
    op("g", 0.15, [], ["pcol0"], lambda q: q.iota(T.pcol[:, 0:1], [[0, 1]], 0, 1))
    iota("itf", DG(4), [[1, 256]], 0.6)
    iota("itg", T.itg[:], [[1, 8], [0, 16]], 0.4)
    iota("it8", T.it8[:], [[1, 8]], 0.15)
    iota("itk", T.itk[:], [[1, 8], [0, 8]], 0.25)

    def icol(j, *a):
        v(1, ["pcol0"], ["pcol%d" % j], ts(T.pcol[:, j:j + 1], T.pcol[:, 0:1], *a))
    icol(1, 4, A_.arith_shift_right)
    icol(2, 1, A_.arith_shift_right, 7, A_.bitwise_and)
    icol(3, 15, A_.bitwise_and)
    icol(4, 7, A_.bitwise_and)
    icol(5, 3, A_.arith_shift_right, 1, A_.bitwise_and)
    v(8, ["pcol%d" % j for j in range(6)], ["fc"], cp(T.fcol[:, 0:6], T.pcol[:, 0:6]))
    FC = lambda j: T.fcol[:, j:j + 1]
    for a in (0, 2048):
        op("v", small(1024), [], ["ptab%d" % d for d in range(6)], ms(T.ptab[:, a:a + 2048], 1.0), after="fc" if a else "pcol5")

    def fcol(j, in0, s1, o0, s2=None, o1=None, dep=()):
        v(1, ["fc"] + ["fc%d" % x for x in dep], ["fc%d" % j], ts(FC(j), in0, s1, o0, s2, o1))

    def lcol(j, src, scale, bias):
        s(1, ["fc"], ["fc%d" % j], act(FC(j), FC(src), F_.Copy, bias, scale))
    fcol(8, FC(1), 8.0, A_.mult, FC(4), A_.add)
    lcol(9, 0, 0.5, 0.0)
    lcol(11, 0, 0.5, -0.5)
    lcol(12, 1, 16.0, 16.0)
    lcol(13, 5, -1.0, 1.0)
    lcol(14, 3, -ALPHA, TOP)
    fcol(15, FC(2), 0.0, A_.is_equal, 0.5, A_.mult)
    fcol(16, FC(2), 1.0, A_.is_equal, 2.0 ** -13, A_.mult)
    fcol(17, FC(2), 2.0, A_.is_equal, 0.5, A_.mult)
    fcol(18, FC(3), 6.0, A_.is_equal, -MID, A_.mult)
    fcol(20, FC(17), FC(15), A_.subtract, dep=(17, 15))
    fcol(21, FC(17), FC(16), A_.subtract, dep=(17, 16))
    fcol(22, FC(15), FC(16), A_.add, FC(18), A_.add, dep=(15, 16, 18))
    fcol(23, FC(17), 2.0, A_.mult, FC(18), A_.add, dep=(17, 18))
    fcol(19, FC(15), FC(16), A_.subtract, dep=(15, 16))
    fcol(10, FC(18), 1.5 * BIG / MID, A_.mult, FC(22), A_.add, dep=(22, 18))
    fcol(24, FC(3), 0.0, A_.is_equal, -0.5, A_.mult)

    def sel(name, out, src, col, w=None, dep=()):
        R = [src.split(":")[0], "fc"] + ["fc%d" % x for x in (col,) + tuple(dep) if x > 7]
        it = T.dg[:, 1024:1024 + int(src.split(":")[1])] if ":" in src else T[src][:]
        v(1, R, [name], ts(out, it, FC(col), A_.is_equal) if w is None else ts(out, it, FC(col), A_.is_equal, w, A_.mult))

    def times(name, src, w):
        s(T[name].shape[1], [src], [name], act(T[name][:], T[src][:], F_.Copy, 0.0, w))
    for o in range(2):
        sel("bo", T.bo[:, o], "it8", 1)
    for n, cols in (("wp0", (19, 22, 23)), ("wp1", (20, 21, 10))):
        for o, col in enumerate(cols):
            sel(n, T[n][:, :, o], "it8", 1, FC(col), (col,))
    s(8, ["wp0"], ["wp2"], act(T.wp2[:, :, 0], T.wp0[:, :, 0], F_.Copy))
    s(8, ["wp1"], ["wp2a"], act(T.wp2[:, :, 1], T.wp1[:, :, 2], F_.Copy))
    s(64, ["itk"], ["one"], act(T.one[:], T.itk[:], F_.Copy, 1.0, 0.0))
    for n in ("n2A", "n2B", "s2A", "s2B"):
        v(64, [], [n[0:2] + "z" + n[2]], ms(T[n][:, :, 0], 0.0))
    sel("cne", T.cne[:], "itk", 1, 8.0)
    for o in range(2):
        s(64, ["cne"], ["cna"], act(T.cna[:, o], T.cne[:], F_.Copy, 0.0, (1.0 - o) / 128))
    sel("cg", T.cg[:], "itf:64", 8)
    for h, col in ((0, 9), (1, 11)):
        sel("ch%d" % h, T["ch%d" % h][:], "itf:64", col)
        times("nh%d" % h, "ch%d" % h, -1.0)
        times("cb%d" % h, "ch%d" % h, 1.0 / 32)
    sel("idb", T.idb[:], "itf:128", 0)
    for n, w in (("ndb", -1.0), ("idB", BIG), ("ndB", -BIG), ("ihB", BIG / 2), ("nhB", -BIG / 2), ("n64", -64.0)):
        times(n, "idb", w)
    sel("blk", T.blk[:], "itg", 1)
    times("nbk", "blk", -1.0)
    sel("r8", T.r8[:], "itg", 0)
    sel("w0", T.w0[:], "itf:144", 12)
    sel("tb0", T.tbk[:], "itf:128", 0, 2.0)
    v(256, ["tb0", "nbk"], ["tbk"], tt(T.tbk[:], T.tbk[:], T.nbk[:], A_.add))
    s(128, ["itg", "fc24"], ["hw0"], act(T.hw0[:], T.itg[:], F_.Identity, FC(24), 0.0))
    for j, x in enumerate((-74.5, 1.0, -10.5, 0.0)):
        s(1, ["fc"], ["th0"], act(T.thc[:, j:j + 1], FC(0), F_.Copy, x, 0.0))
    s(1, ["fc"], ["cn2"], act(T.cnt[:, 2:3], FC(0), F_.Copy, -2.0 ** -12, 0.0))
    op("s", 1.4, ["cn2"], ["warm"], act(T.cnt[:, 4:5], T.cnt[:, 2:3], F_.Exp))
    v(288, [], ["zz0"], ms(T.zz[:, :, 0::2], 0.0))
    v(144, [], ["zc0"], ms(T.zc[:, :, 0::2], 0.0))
    v(768, [], ["dd0"], ms(T.dd[:], 0.0))

    v(128, ["itf", "fc"], ["dg5"], ts(DG(5), DG(4), 0.0, A_.mult, FC(3), A_.add))
    v(128, ["dg5"], ["dg5"], ts(DG(5), DG(5), 256.0, A_.mult))
    for d in (4, 0, 1, 2, 3, 5):
        if d < 4:
            DI = T.dgi[:, 256 * d:256 * d + 256]
            v(256, ["pc"], ["dgi%d" % d], ts(DI, T.pc[:], 63 << (6 * d), A_.bitwise_and))
            v(256, ["dgi%d" % d], ["dg%d" % d], cp(DG(d), DI))
        dma("s", ["itf" if d == 4 else "dg%d" % d], ["ptab%d" % d], T.ptab[d::16, :], DG(d), 2.5)
    PT = ["ptab%d" % d for d in range(6)]
    EV = ["tev0", "tev1"]

    for t in range(NV):
        v(128, ["sgi"], ["sgb%d" % t], ts(T.sgb[0:8, 128 * t:128 * t + 128], T.sgi[0:8, 128 * t:128 * t + 128], -MID, A_.add))
    for ci, c in enumerate("AB"):
        v(192, ["zi"], ["zo" + c], ts(T.zo[:, ci], T.zi[:, 1:4, ci], -MID, A_.add))
        send(("z", 0, ci), ["zo" + c], ["zn" + c], T.zo[:, ci])

    def slot(t, ci):
        return MW * (2 * t + ci)

    def D(n, ci, first=0, step=1):
        return T.dd[:, 768 * ci + DD[n][0] + first:768 * ci + DD[n][1]:step]

    def ZZ(j, ci):
        return T.zz[:, 4 * ci + j]

    def back(z, out, u="ch"):
        return [(out, z[:, 1:17], T[u + "0"][:]), (out, z[:, 0:16], T[u + "1"][:])]

    def arrive(t, ci):
        c = "AB"[ci]
        B = lambda n: T[n + c]
        cur[0] = "p"
        q0 = slot(t, ci)
        M = lambda a, w=64: T.inm[:, q0 + a:q0 + a + w]
        kX, kS, kG = "iX%d%s" % (t, c), "iS%d%s" % (t, c), "iG%d%s" % (t, c)
        if t == 0:
            v(64, ["zi0"], [kX], cp(M(MX), T.zi[:, 0, ci]))
            v(64, ["liS"], [kS], cp(M(MS), T.li[:, 0, 64 * ci:64 * ci + 64]))
            v(64, [], ["iR0" + c], ms(M(MR), 0))
            v(64, ["liG"], [kG], cp(M(MG), T.li[:, 1, 64 * ci:64 * ci + 64]))
        for j, (a, b) in enumerate(cuts(CUT["x" + c])):
            EX, IN = B("ex")[:, 16 * a:16 * b], T.tev[:].indirect(M(MX + a, b - a))
            if j == 0:
                gather("v", b - a, EV + [kX], ["exv" + c], cp(EX, IN))
            else:
                gather("s", b - a, EV + [kX], ["exs" + c], act(EX, IN, F_.Copy))
        v(64, [kX, kS], ["mh" + c], ts(B("mh")[:, 0:MR], M(0, MR), -MID, A_.add))
        v(64, [kG, "iR%d%s" % (t, c)], ["mg" + c], ts(B("mh")[:, MR:MW], M(MR, 128), -MID, A_.add))
        for h in range(2):
            v(64, [kG, "fc", "fc13"], ["pg" + c], ts(B("pg")[:, :, h], M(MG), -MID, A_.add, FC(13) if h == 0 else FC(5), A_.mult))
        lo = 128 * t + L2 * ci
        mm(128, ["sgb%d" % t, "r8", "ndb", "mg" + c], ["y" + c],
           [(B("fz")[:, 0], T.r8[0:8, :], T.sgb[0:8, lo:lo + L2]), (B("fz")[:, 0], T.ndb[:], B("mh")[:, MR:MR + 64])], "fz" + c)
        for h in range(2):
            s(64, ["y" + c], ["pq" + c], act(B("pq")[:, :, h], B("fz")[:, 0], F_.Relu, 0.0, 64.0), "fz" + c)
        s(64, ["y" + c, "dd0"], ["dS" + c], act(D("dS", ci, 1, 2), B("fz")[:, 0], F_.Sign, -0.5), "fz" + c)

    TH = lambda t, j: T.thc[:, 4 * t + j:4 * t + j + 1]

    def threshold(t):
        cur[0] = "f"
        Y, R2 = T.cvB[:, 6, 0, 0:1], T.cnt[:, 3:4]
        mm(512, ["hw0", "cnA", "cn2"], ["yw"], [(Y, T.hw0[:], T.cnt[:, 2:3]), (Y, T.hw0[:], T.cnt[:, 0:1])], "cvB", True, False)
        mm(256, ["cnB"], ["yn"], [(Y, T.hw0[:], T.cnt[:, 1:2])], "cvB", False, True)
        v(1, ["yn"], ["r2"], ts(R2, Y, 1.5 * 2 ** 24, A_.add, -1.5 * 2 ** 24, A_.add), "cvB")
        v(4, ["yn", "r2", "th0"], ["tho%d" % t], ts(T.tho[:, 4 * t:4 * t + 4], T.thc[:, 0:4], Y, A_.add, R2, A_.subtract), "cvB")
        send(("h", t + 1, 0), ["tho%d" % t], ["th%d" % (t + 1)], T.tho[:, 4 * t:4 * t + 4])

    def bounds(t, ci):
        c = "AB"[ci]
        B = lambda n: T[n + c]
        cur[0] = "g"
        q0 = slot(t, ci) + MG
        for a, b in cuts(CUT["g" + c]):
            gather("v", b - a, EV + ["iG%d%s" % (t, c), "exs" + c, "exv" + c], ["gg" + c],
                   tt(B("gg")[:, 16 * a:16 * b], T.tev[:].indirect(T.inm[:, q0 + a:q0 + b]), B("ex")[:, 16 * a:16 * b], A_.is_ge),
                   "w4A" if ci and OPT["lead"] else None, "w")
        CG, FM = B("fz")[:, 1], B("fz")[:, 2]
        for j in range(4):
            mm(256, ["gg" + c, "w0"], ["cG%d%s" % (j, c)],
               [(CG, T.w0[:, 16 - k:144 - k], B("gg")[:, k::16]) for k in range(4 * j, 4 * j + 4)], "fz" + c, j == 0, j == 3)
        s(64, ["cG3" + c, "th%d" % t], ["mi" + c], act(B("mi")[:], CG, F_.Sign, TH(t, 2)), "fz" + c)
        mm(128, ["mi" + c, "pq" + c, "nbk", "idb"], ["fm" + c], [(FM, T.idb[:], B("pq")[:, :, 0]), (FM, T.nbk[:], B("mi")[:])], "fz" + c)
        s(64, ["fm" + c], ["nf" + c], act(B("nf")[:], FM, F_.Relu, 7.5, 0.5), "fz" + c)
        s(64, ["fm" + c], ["pu" + c], act(B("pu")[:], FM, F_.Relu, -57.0), "fz" + c)

    def step(t, i, ci, other):
        c, o = "AB"[ci], "AB"[1 - ci]
        B = lambda n: T[n + c]
        cur[0] = str(i)
        q0 = slot(t, ci) + MS
        off, kF = (T.inm[:, q0:q0 + 64], "iS%d%s" % (t, c)) if i == 0 else (B("off"), "off" + c)
        turn = other is not None
        name = "5" if (i, ci) == (STEPS - 1, 1) else "1" if (i, ci) == (0, 1) else "" if turn else "0"
        for j, (a, b) in enumerate(cuts(CUT["s" + name])):
            gather("s", b - a, PT + [kF], ["gp" + c], act(B("gp")[:, 16 * a:16 * b], T.ptab[:].indirect(off[:, a:b]), F_.Copy),
                   "d1" + o if turn and j == 1 else None)
        for j, (a, b) in enumerate(cuts(CUT["v" + name])):
            gather("v", b - a, EV + [kF, "exs" + c, "exv" + c], ["ge" + c],
                   tt(B("ge")[:, 16 * a:16 * b], T.tev[:].indirect(off[:, a:b]), B("ex")[:, 16 * a:16 * b], A_.is_ge),
                   (None, "nx" + o, "zz%d%s" % (other % 3, o), None, None)[j] if turn else None)
        kz = lambda j: "zz%d%s" % (j % 3, c)
        last = i == STEPS - 1
        Z, X, E = ZZ(i % 3, ci), B("cv")[:, 0:2], B("pa")[:, 1, :, :, 0]
        NE = lambda j: ZZ(3, ci)[:, 1::2] if j >= STEPS - 2 else B("n2")[:, :, 1]
        ST = B("s2")[:, :, 1]
        PX = lambda f: B("pa")[:, 0, :, :, f]
        n = 3 if last else 2
        wp = "wp1" if last else "wp2" if i else "wp0"
        par = [(B("pa")[:, 0, :, k, 0:T[wp].shape[2]], B("gp")[:, k::8], T[wp][:]) for k in range(8)]
        pre = [(X, B("pq")[:], T.cna[:])]
        if i == 0:
            mm(512, ["gp" + c, wp], ["pa" + c], par, "pa" + c)
            mm(128, ["pg" + c, "cg", "pq" + c, "cne"], ["gE" + c], [(E, B("pg")[:], T.cg[:]), (E, B("pq")[:], T.cne[:])], "pa" + c)
        else:
            ka, AP = ("a0" + c, B("a0")[:]) if i == 1 else (kz(i - 2), ZZ((i - 2) % 3, ci)[:, 1::2])
            lst = [(PX(3), T.idb[:], AP), (PX(3), T.ihB[:], T.one[:]), (PX(3), T.ndB[:], NE(i - 1)), (PX(3), T.ihB[:], ST)]
            down = [(PX(2), T.idB[:], NE(i - 1)), (PX(2), T.nhB[:], ST)] if last else \
                [(B("pa")[:, 0, :, :, 0:2], T.idB[:], B("n2")[:]), (B("pa")[:, 0, :, :, 0:2], T.nhB[:], B("s2")[:])]
            mm(256, [ka, "ne" + c, "st" + c, "idb", "ndB", "ihB", "one"], ["pw" + c], lst, "pa" + c, True, False)
            if last:
                mm(640, ["gp" + c, wp, wp + "a", "idB", "nhB"], ["pa" + c], par + down, "pa" + c, False, True)
            else:
                mm(256, ["ne" + c, "st" + c, "idB", "nhB"], ["pw" + c], down, "pa" + c, False, False)
                mm(512, ["gp" + c, wp, wp + "a"], ["pa" + c], par, "pa" + c, False, True)
            pre += [(X[:, 0], T.n64[:], T.one[:]), (X[:, 0], T.n64[:], ST)]
        mm(256 if i else 128, ["pq" + c, "cna", "n64", "one"] + ["st" + c] * (i > 0), ["cw" + c], pre, "cv" + c, True, False)
        mm(512, ["ge" + c, "bo"], ["cv" + c], [(X[:, :, :, k], B("ge")[:, k::8], T.bo[:]) for k in range(8)], "cv" + c, False, True,
           "aL" + o if turn and other < STEPS - 1 else None)
        dn = "d1" if last else "d2"
        s(64 * n, ["pa" + c], ["va" + c], act(B("va")[:, 0:64 * n], B("pa")[:, 0, :, :, 0:n], F_.Copy), "pa" + c)
        s(64, ["cv" + c, "dd0"], ["d1" + c], act(D(dn, ci, n - 1, n), X[:, 1], F_.Sign, -7.5), "cv" + c)
        if last:
            s(64, ["cv" + c, "dd0", "th%d" % t], ["d1" + c], act(D(dn, ci, 1, 3), X[:, 0], F_.Sign, TH(t, 0)), "cv" + c)
        if i >= STEPS - 2:
            s(64, ["cv" + c, "th%d" % t, "zc0"], ["zc%d%s" % (i, c)], act(T.zc[:, 2 * ci + i % 2, 1::2], X[:, 0], F_.Identity, TH(t, 1)), "cv" + c)
        if not last:
            s(64, ["cv" + c, "s2z" + c, "th%d" % t], ["st" + c], act(ST, X[:, 0], F_.Sign, TH(t, 0)), "cv" + c)
        NX = B("nx")[:, n - 1:64 * n:n]
        v(64 * n, ["d1" + c, "va" + c], ["nx" + c], scan(B("nx")[:, 0:64 * n], D(dn, ci), B("va")[:, 0:64 * n]))
        if last:
            v(64, ["nx" + c, "gE" + c], ["ne" + c], tt(NE(i), NX, E, A_.not_equal), "pa" + c)
        if i == 0:
            v(64, ["nx" + c, "zz0"], [kz(i)], cp(Z[:, 1::2], NX))
            v(64, ["pa" + c], ["a0" + c], cp(B("a0")[:], PX(2)), "pa" + c)
        else:
            v(64, ["nx" + c, "pa" + c], [kz(i)], tt(Z[:, 1::2], NX, PX(3), A_.max), "pa" + c)
        if not last:
            mm(128, [kz(i), "ch0", "ch1"], ["aL" + c], back(Z, B("tr")[:, 0:64]), "tr" + c)
            v(64, ["aL" + c], ["off" + c], ts(B("off")[:], B("tr")[:, 0:64], MID, A_.add), "tr" + c)
            v(64, [kz(i), "gE" + c, "n2z" + c], ["ne" + c], tt(NE(i), Z[:, 1::2], E, A_.not_equal), "pa" + c)
        F = lambda j: B("tr")[:, 64 + j:256:3] if j < 3 else B("tr")[:, 253 + j:384:2] if j < 5 else B("tr")[:, 379 + j:512:2]
        MH = lambda a: B("mh")[:, a:a + 64]
        if i == STEPS - 2:
            lst = back(Z, F(0), "nh") + back(Z, F(2)) \
                + [(F(1), T.ndb[:], MH(MG)), (F(2), T.idb[:], MH(MG)), (F(5), T.ndb[:], MH(MS)), (F(6), T.idb[:], MH(MS))]
            if t < NV - 1:
                ZN = T.zn[:, ci, 64 * t:64 * t + 64]
                lst += [(F(3), T.ndb[:], MH(MX)), (F(4), T.idb[:], MH(MX)), (F(3), T.idb[:], ZN), (F(4), T.idb[:], ZN)]
            for j in range(0, len(lst), 4):
                mm(256, [kz(i), "nh0", "nh1", "mh" + c, "mg" + c, "zn" + c], ["fw" + c], lst[j:j + 4], "tr" + c, j == 0, False)
        if i == STEPS - 1:
            mm(256, [kz(i)], ["fv" + c], back(Z, F(5)) + back(Z, F(6)), "tr" + c, False, False)
            mm(256, [kz(i)], ["fv" + c], back(Z, F(0)) + back(Z, F(1)), "tr" + c, False, True)

    def weight(i, ci):
        c = "AB"[ci]
        B = lambda n: T[n + c]
        cur[0] = "w"
        Z, ww = B("fz")[:, i - 1], "w%d" % i
        mm(192, ["zc%d%s" % (i, c), "cb0", "cb1", "nf" + c, "idb"], ["zw" + c],
           [(Z, T.idb[:], B("nf")[:])] + back(T.zc[:, 2 * ci + i % 2], Z, "cb"), "fz" + c, True, False)
        mm(128, ["ne" + c, "ch0", "ch1"], ["Z" + c], back(ZZ(3, ci), Z), "fz" + c, False, True)
        s(64, ["Z" + c, "fc14"], [ww + c], act(B(ww)[:], Z, F_.Exp, FC(14), -ALPHA * GAP * 32), "fz" + c)

    def finish(t, ci):
        c = "AB"[ci]
        B = lambda n: T[n + c]
        cur[0] = "f"
        D4, D45, RD = B("cv")[:, 3], B("cv")[:, 4], B("cv")[:, 5]
        more = t < NV - 1
        lst = [(D4, T.idb[:], B("pu")[:]), (D45, T.idb[:], B("pu")[:]), (D4, T.tbk[:], B("w4")[:]), (D45, T.tbk[:], B("w4")[:])]
        if more:
            lst += [(RD, T.idb[:], B("nf")[:]), (RD, T.blk[:], B("w4")[:])]
        mm(64 * len(lst), ["pu" + c, "nf" + c, "w4" + c, "tbk", "blk", "idb"], ["dw" + c], lst, "cv" + c, True, False)
        lst = [(D4, T.nbk[:], B("w5")[:]), (D45, T.tbk[:], B("w5")[:])] + ([(RD, T.blk[:], B("w5")[:])] if more else [])
        mm(64 * len(lst), ["w5" + c], ["D" + c], lst, "cv" + c, False, True)
        q0, q1, k = slot(t, ci), slot(t + 1, ci), "%d%s" % (t, c)
        so = lambda a: T.som[:, q0 + a:q0 + a + 64] if more else T.fo[:, 2 * ci + (a == MG)]
        out = lambda a, x: ts(so(a), x, 0.5, A_.mult, MID, A_.add)
        v(128, ["dS" + c, "fv" + c], ["oS" + c], scan(B("oS")[:], D("dS", ci), B("tr")[:, 384:512]), "tr" + c)
        v(64, ["oS" + c], ["soS" + k], out(MS, B("oS")[:, 1::2]))
        if not more:
            send(("s", NV, ci), ["soS" + k], ["yS" + c], so(MS))
        if more:
            s(84, ["D" + c, "dd0"], ["dX" + c, "cn" + c],
              lambda q: q.activation(D("dX", ci, 1, 2), RD, F_.Sign, bias=-TAU, accum_out=T.cnt[:, ci:ci + 1]), "cv" + c)
            v(128, ["dX" + c, "fv" + c], ["oX" + c], scan(B("oX")[:], D("dX", ci), B("tr")[:, 256:384]), "tr" + c)
            v(64, ["oX" + c], ["soX" + k], out(MX, B("oX")[:, 1::2]))
            v(64, ["dX" + c], ["soR" + k], ts(so(MR), D("dX", ci, 1, 2), 0.0, A_.is_lt))
        for j, x in enumerate((D4, D45)):
            s(64, ["D" + c, "dd0"], ["dG" + c], act(D("dG", ci, 1 + j, 3), x, F_.Sign, -TAU), "cv" + c)
        v(192, ["dG" + c, "fv" + c], ["oG" + c], scan(B("oG")[:], D("dG", ci), B("tr")[:, 64:256]), "tr" + c)
        v(64, ["oG" + c], ["soG" + k], out(MG, B("oG")[:, 2::3]))
        if not more:
            send(("g", NV, ci), ["soG" + k], ["yG" + c], so(MG))

    def hand_on(t):
        for kind, t1, ci in messages():
            if t1 == t + 1 and kind == "h":
                threshold(t)
            elif t1 == t + 1:
                a = slot(t, ci) + 64 * "XSRG".index(PART[kind][0])
                send((kind, t1, ci), ["so%s%d%s" % (n, t, "AB"[ci]) for n in PART[kind]], ["i%s%d%s" % (n, t1, "AB"[ci]) for n in PART[kind]],
                     T.som[:, a:a + 64 * len(PART[kind])])

    lead = OPT["lead"]
    turns = [(i - ci * lead, ci) for i in range(STEPS + lead) for ci in range(NC) if 0 <= i - ci * lead < STEPS]
    for t in range(NV):
        for n, (i, ci) in enumerate(turns):
            if i == 0:
                arrive(t, ci)
            step(t, i, ci, turns[n - 1][0] if n and turns[n - 1][1] != ci else None)
            if i == (STEPS - 2 if ci and lead else 0):
                bounds(t, ci)
            if i >= STEPS - 2:
                weight(i, ci)
            if i == STEPS - 1:
                finish(t, ci)
        if t < NV - 1:
            hand_on(t)
    for ci, c in enumerate("AB"):
        for j in range(2):
            dma("ys"[j], ["y" + "SG"[j] + c], ["out"], (T.ys, T.yg)[j][:, 64 * ci:64 * ci + 64], T.yo[:, 2 * ci + j], 2.0)
    return ops


def link(ops):
    wr, rd, base, bank, line = {}, {}, {}, {}, {}
    for n, o in enumerate(ops):
        d = set()
        for k in o["R"]:
            d.update(wr.get(k, ()))
        for k in o["W"]:
            old = wr.get(k, [])
            piece = old and k not in o["R"] and not rd.get(k) and all(ops[m]["e"] == o["e"] and (o["line"] or ops[m]["W"] == o["W"]) for m in old)
            if piece:
                wr[k] = old + [n]
            else:
                base[k] = set(old) | set(rd.get(k, ())) if k != "out" else set()
                wr[k] = [n]
                rd[k] = []
            d.update(base[k])
        o["O"] = [line[o["line"]]] if o["line"] in line else []
        if o["after"]:
            o["O"].append(wr[o["after"]][-1])
        if o["line"]:
            line[o["line"]] = n
        if o["b"]:
            sg = bank.get(o["b"])
            if not sg or sg["e"] != o["e"]:
                sg = bank[o["b"]] = {"e": o["e"], "n": [], "pre": set(sg["n"]) if sg else set()}
            elif o["e"] == "p":
                d.add(sg["n"][-1])
            d.update(sg["pre"])
            sg["n"].append(n)
        d.discard(n)
        o["D"] = sorted(d)
        for k in o["R"]:
            if k not in o["W"]:
                rd.setdefault(k, []).append(n)
    return ops


def order(ops):
    n, LAT = len(ops), PAR["lat"]
    suc = [[] for _ in ops]
    pri = [0.0] * n
    need = [len(o["D"]) + len(o["O"]) for o in ops]
    for i, o in enumerate(ops):
        for d in o["D"]:
            suc[d].append((i, ops[d]["lat"] + (0.0 if ops[d]["e"] == o["e"] == "p" else LAT)))
        for d in o["O"]:
            suc[d].append((i, 0.0))
    for i in range(n - 1, -1, -1):
        pri[i] = ops[i]["c"] + max([pri[j] + gap for j, gap in suc[i]] or [ops[i]["lat"]])
    for i in range(n):
        k = ops[i]["key"]
        pri[i] += ([SHIFT[x] for x in (k, k[:-1], k[:-2], k[0] + ops[i]["e"]) if x in SHIFT] + [0.0])[0] - {"v": 100.0, "s": 100.0, "w": 200.0}.get(ops[i]["line"], 0.0)
    free, est, seq = {}, [0.0] * n, []
    ready = [i for i in range(n) if not need[i]]
    q = lambda e: "g" if e == "net" else e
    while ready:
        first = min((max(est[i], free.get(q(ops[i]["e"]), 0.0)), -pri[i], i) for i in ready)
        tm, eng = first[0], q(ops[first[2]]["e"])
        cand = [i for i in ready if q(ops[i]["e"]) == eng and max(est[i], free.get(eng, 0.0)) <= tm + PAR["eps"]]
        b = max(cand, key=lambda i: (pri[i], -i))
        free[eng] = max(est[b], free.get(eng, 0.0)) + ops[b]["c"]
        ready.remove(b)
        seq.append(b)
        for j, gap in suc[b]:
            need[j] -= 1
            est[j] = max(est[j], free[eng] + gap)
            if not need[j]:
                ready.append(j)
    return seq


def peer(T, rank, msg, sign):
    step = -1 if msg[0] == "z" else (1 if msg[1] < NV else 1 - NV)
    return T.cores[(rank + sign * step) % len(T.cores)]


def route(src, dst, msg, topo):
    if topo.may_write(src, dst):
        return src
    own = [c for c in topo.cores_of(src) if c != src and topo.may_write(c, dst)]
    own.sort(key=lambda c: topo.die(c) != topo.die(src))
    return own[msg[2] if msg[0] == "z" else int(msg[0] in OPT["r1"])]


def landing(T, msg):
    kind, t, ci = msg
    if kind == "z":
        return T.zn[:, ci]
    if kind == "h":
        return T.thc[:, 4 * t:4 * t + 4]
    if t == NV:
        return T.yo[:, 2 * ci + (kind == "g")]
    q0 = MW * (2 * t + ci)
    a = q0 + 64 * "XSRG".index(PART[kind][0])
    return T.inm[:, a:a + 64 * len(PART[kind])]


def emit(g, core, T, topo, ops, seq):
    qs = {"v": g.vector, "s": g.scalar, "p": g.tensor, "g": g, "net": g, "y": g.sync}
    cs = {"v": "v", "s": "s", "p": "p", "g": "q"}
    known = {e: {} for e in "vspgy"}
    count = {}
    loc = 0
    rank = T.rank_of(core)
    for n in seq:
        o = ops[n]
        e = "g" if o["e"] == "net" else o["e"]
        q, kn = qs[e], known[e]
        need = {}
        for d in o["D"]:
            if e == "p" and ops[d]["e"] == "p":
                continue
            sem, val, clk = ops[d]["sig"]
            if val > need.get(sem, (0, None))[0]:
                need[sem] = (val, clk)
        for sem, (val, clk) in sorted(need.items(), key=lambda x: -len(x[1][1])):
            if kn.get(sem, 0) < val:
                q.wait_ge(T.sem[sem], val)
                kn[sem] = val
                for k2, v2 in clk.items():
                    if kn.get(k2, 0) < v2:
                        kn[k2] = v2
        if o["e"] == "net":
            msg, src = o["f"]
            dst, frm = peer(T, rank, msg, 1), peer(T, rank, msg, -1)
            via = route(core, dst, msg, topo)
            to = dst if via == core else via
            rid, pid = topo.addr(to, core)
            g.remote_dma(landing(T, msg), src, T.sem["%s%d%d" % msg], T.sem.loc, pid, rid, topo.mask(core, to))
            loc += len(topo.engines(core, to))
            o["sig"] = ("%s%d%d" % msg, len(topo.engines(route(frm, core, msg, topo), core)), {})
        elif "dsem" in o:
            o["f"](q).then_inc(T.sem[o["dsem"]], 16)
            o["sig"] = (o["dsem"], 16, dict(kn))
        else:
            sem = cs[e]
            count[sem] = count.get(sem, 0) + 1
            o["f"](q).then_inc(T.sem[sem], 1)
            clk = dict(kn)
            clk[sem] = count[sem]
            o["sig"] = (sem, count[sem], clk)
    for o in ops:
        if "dsem" in o:
            g.wait_ge(T.sem[o["dsem"]], 16)
    for sem, val in count.items():
        g.wait_ge(T.sem[sem], val)
    g.wait_ge(T.sem.loc, loc)


def relay(g, core, T, topo):
    loc = 0
    for rank, src in enumerate(T.cores):
        for msg in messages() if core in topo.cores_of(src) else []:
            dst = peer(T, rank, msg, 1)
            if route(src, dst, msg, topo) == core:
                sem = T.sem["%s%d%d" % msg]
                g.wait_ge(sem, len(topo.engines(src, core)))
                rid, pid = topo.addr(dst, core)
                g.remote_dma(landing(T, msg), landing(T, msg), sem, T.sem.loc, pid, rid, topo.mask(core, dst))
                loc += len(topo.engines(core, dst))
    if loc:
        g.wait_ge(T.sem.loc, loc)


def rank_program(g, core, T, topo):
    if T.rank_of(core) is None:
        relay(g, core, T, topo)
        return
    ops = link(build(T))
    emit(g, core, T, topo, ops, order(ops))
